import numpy as np, ml_dtypes
CORES = [10,34,74,98]
N = 4
BF = ml_dtypes.bfloat16
def gentries(a):
    return np.ascontiguousarray(a.reshape(8, 16, -1).transpose(0, 2, 1)).reshape(8, -1)
def gtable(e):
    e = np.asarray(e); return np.ascontiguousarray(e.reshape(8, -1, 16).transpose(0, 2, 1)).reshape(128, -1).astype(np.int32)
V, B, S, RO = 1024, 256, 8, 3
E = V + (N - 1) * B
UM, QM, LAM, H, Z = 1023, 1023, 64, 9, 13
def bars(rng):
    p = np.argsort(rng.random((N, 8, 4, V)), axis=-1); inv = np.argsort(p, axis=-1)
    m = rng.random((N, 8, 4, V)) < 0.4; mi = np.take_along_axis(m, inv, -1)
    L = np.concatenate([p, inv], axis=2); M = np.concatenate([m, mi], axis=2)
    L = np.where(M, np.where(rng.random(L.shape) < 0.5, E, rng.integers(V, E, L.shape)), L)
    return np.take_along_axis(L, np.argsort(rng.random(L.shape), axis=2), 2)
def parts(rng):
    d = {}; size = rng.choice(np.array([224, 288, 352, 448]), (N, 8, 1, 1))
    for k in ("ux", "uy"): d[k] = np.rint((2 * rng.random((N, 8, 16, V)) - 1) * size).astype(np.int64)
    d["ld"] = rng.integers(-2047, 2048, (N, 8, 16, V))
    for k in ("px", "py"): d[k] = rng.integers(0, 8, (N, 8, V))
    d["wt"] = (0.5 + rng.random((N, 8, 16, V))).astype(np.float32)
    d["nb"] = bars(rng); d["bord"] = np.ascontiguousarray(np.argsort(rng.random((N, 8, V)), axis=-1)[..., :B])
    return d
def pack(d):
    out = {}
    for k in ("ux", "uy", "ld"): out[k] = np.ascontiguousarray(d[k].reshape(N, 128, V)).astype(np.int32)
    for k in ("px", "py"): out[k] = np.ascontiguousarray(d[k]).astype(np.int32)
    out["wt"] = np.ascontiguousarray(d["wt"].reshape(N, 128, V)).astype(np.float32)
    out["nb"] = np.stack([gtable(m.reshape(8, 8 * V)) for m in d["nb"]]); out["bord"] = np.stack([gtable(m) for m in d["bord"]])
    return out
def setup_inputs(rng):
    return pack(parts(rng))
def setup_inputs_spread(rng):
    d = parts(rng)
    for k in ("ux", "uy"): d[k] = np.rint((2 * rng.random((N, 8, 16, V)) - 1) * 1023 * np.exp2(-rng.integers(0, 5, (N, 8, 1, V)))).astype(np.int64)
    d["ld"] = np.rint((2 * rng.random((N, 8, 16, V)) - 1) * 2047 * np.exp2(-rng.integers(0, 6, (N, 8, 1, V)))).astype(np.int64)
    d["wt"] = (d["wt"] * np.exp2(rng.integers(-1, 2, (N, 8, 1, V)))).astype(np.float32)
    return pack(d)
def setup_inputs_ends(rng):
    d = parts(rng)
    h = rng.random(d["wt"].shape)
    d["wt"] = np.where(h < 0.4, 4.0, np.where(h < 0.8, 0.25, d["wt"])).astype(np.float32)
    for k, m in (("ux", 1023), ("uy", 1023), ("ld", 2047)):
        x = 2 * rng.integers(0, 2, (N, 8, 16, V)) - 1
        x = np.where(rng.random((N, 8, 1, V)) < 0.6, x[:, :, :1], x)
        one = (np.arange(16)[:, None] == rng.integers(0, 16, (N, 8, 1, V))) & (rng.random((N, 8, 1, V)) < 0.3)
        d[k] = m * np.where(one, -x, x)
    for k in ("px", "py"): d[k] = 7 * rng.integers(0, 2, (N, 8, V))
    h = rng.random((N, 8, 3, V)); x = rng.integers(0, V, (N, 8, 3, V))
    x = np.where(h < 0.15, V - 1, np.where(h > 0.95, E - 1, np.where(h > 0.8, rng.integers(V, E, x.shape), x)))
    L = np.concatenate([np.full((N, 8, 2, V), E), np.zeros((N, 8, 3, V), np.int64), x], axis=2)
    L = np.take_along_axis(L, np.argsort(rng.random(L.shape), axis=2), 2); d["nb"] = L
    d["bord"] = np.where(rng.random((N, 8, B)) < 0.66, (V - 1) * rng.integers(0, 2, (N, 8, B)), d["bord"])
    for r in range(N):
        for g in range(8):
            o = 1 + rng.permutation(V // S - 3)
            for s, v in ((1, V - 1), (-1, V - 1 - S)):
                i, o = o[:12], o[12:]
                c = i[:6] * S + np.arange(6) % (S - 1); n = i[6:] * S + np.arange(6) % (S - 1); far = np.concatenate([n, c])
                for k in ("px", "py"): d[k][r, g, far] = 0; d[k][r, g, v] = 7; d[k][r, g, v - 1] = 7
                for k in ("ux", "uy"):
                    w = d[k][r, g]; w[:, far] = -1023 * s; w[:, v] = 1023 * s; w[:, v - 1] = 1023 * s
                L[r, g, :2, v] = E; L[r, g, 2:, v] = n; L[r, g, :, v - 1] = far[:8]
                for j in range(6): L[r, g, 2 + j, n[j]] = c[j]
    return pack(d)
def setup_inputs_corners(rng):
    d = parts(rng); L = d["nb"]; c = rng.choice(7, (N, 8, 1, V), p=[0.4, 0.1, 0.2, 0.1, 0.1, 0.05, 0.05])
    own = rng.integers(0, V, L.shape); gh = rng.integers(V, E, L.shape); slot = np.arange(8)[:, None]
    L = np.where(c == 1, E, np.where(c == 2, own, L)); L = np.where(c == 3, np.where(slot == (own[:, :, :1] & 7), E, gh), L)
    L = np.where(c == 4, np.where(slot == 7, E, own[:, :, :1]), np.where(c == 5, np.where(slot == 7, own, E), L))
    x = rng.choice(np.array([0, V - 1, V, E - 1, -1]), L.shape)
    d["nb"] = np.where(c == 6, np.where(x < 0, np.arange(V), x), L)
    for r in range(N):
        o = rng.permutation(np.array([4, 6, 7])); lo = V + B * int(rng.integers(0, N - 1))
        d["nb"][r, int(o[0])] = rng.integers(lo, lo + B, (8, V)); d["nb"][r, int(o[1])] = rng.integers(0, V, (8, V))
    for g, m in ((0, 3), (1, 4), (2, 8), (3, 9)):
        o = rng.permutation(16); on = (1 + (o < m).astype(np.int64)) * (1 - 2 * (o & 1)); some = rng.random((N, 1, V)) < 0.8
        for k, p in (("ux", "px"), ("uy", "py")): d[k][:, g] = np.where(some, 64 * d[p][:, g][:, None, :] * on[:, None], d[k][:, g])
    d["px"][:, 5] = 3 + (d["px"][:, 5] & 1); d["py"][:, 5] = 4
    d["ux"][:, 5] = 543 * (2 * (d["px"][:, 5] - 3) - 1)[:, None, :] + rng.integers(0, 2, (N, 16, V))
    return pack(d)
def setup_inputs_crowd(rng):
    d = parts(rng)
    for r in range(N):
        for g in (0, 2, 4, 6):
            i = 1 + rng.permutation(V // S - 1)[:2]; h, c = int(i[0]) * S, int(i[1]) * S
            sc = np.full(16, 128)
            if g == 6: sc[15] = 64
            for k, p in (("ux", "px"), ("uy", "py")):
                d[p][r, g] = np.maximum(d[p][r, g], 1); d[p][r, g, c] = 0; d[k][r, g] = sc[:, None] * d[p][r, g]
            L = d["nb"][r, g]; L[L == c] = h; L[0] = h; L[5] = E
            if g == 2:
                x = L[:, :S]; x[x == E] = h
            if g == 4: L[0, :S * int(rng.integers(2, V // S - 2))] = E
            L[:, h] = c; L[:, c] = E
        i = S * np.arange(V // S); o = rng.permutation(S - 1)[:2]
        c = rng.permutation(i + int(o[0])); n = rng.permutation(i + int(o[1])); v = i + S - 1; s = rng.integers(0, 8, V // S)
        for k, p in (("ux", "px"), ("uy", "py")):
            d[p][r, 7] = np.maximum(d[p][r, 7], 1); d[p][r, 7, c] = 0; d[k][r, 7] = 128 * d[p][r, 7]
        L = d["nb"][r, 7]; L[:, v] = E; L[s, v] = n; L[s, n] = c; L[(s + 1) % 8, c] = E
        o = rng.permutation(S - 1)[:3]; a = i + int(o[0]); b = i + int(o[1]); other = i + int(o[2])
        for k, p in (("ux", "px"), ("uy", "py")):
            d[p][r, 5] = np.maximum(d[p][r, 5], 1); d[p][r, 5, b] = 0
            w = 64 * d[p][r, 5]; w[b] = -64; d[k][r, 5] = w
        n = rng.permutation(a); c = rng.permutation(b); L = d["nb"][r, 5]
        L[:, v] = rng.choice(a, (8, V // S)); L[7, v] = n
        if r % 2 == 0: L[0, v] = E
        else: L[0, v[-4:]] = E
        L[:7, a] = rng.choice(other, (7, V // S)); L[7, n] = c; L[0, b] = E
        x = rng.permutation(i); h = V // S // 2; za = x[:h]; zb = x[h:]
        n = np.concatenate([za, zb]); c = np.concatenate([rng.permutation(zb), rng.permutation(za)]); j = rng.integers(0, 8, V // S)
        act = np.concatenate([i + S - 1 - t for t in range(RO)]); sg = 1 - 2 * (rng.permutation(16) & 1)[:, None]
        for k, p, top, pa, pb, ua, ub in (("ux", "px", 3, 5, 5, 322, 321), ("uy", "py", 4, 3, 4, 189, 255)):
            at = int(rng.integers(0, top)); off = rng.integers(-300, 301, (16, 1))
            d[p][r, 3, act] = at; d[p][r, 3, za] = at + pa; d[p][r, 3, zb] = at + pb
            w = d[k][r, 3]; w[:, act] = off; w[:, za] = off + ua * sg; w[:, zb] = off + ub * sg
        w = d["ld"][r, 3]; w[:, act] = 0; w[:, za] = 0; w[:, zb] = 8 * sg
        L = d["nb"][r, 3]; L[:, i] = E; L[:, act] = E; L[j, n] = c
        for t in range(RO):
            x = rng.permutation(V // S); L[(j[x] - t) % 8, i + S - 1 - t] = n[x]
    return pack(d)
def setup_inputs_calm(rng):
    d = parts(rng)
    for g in (1, 4, 6):
        pj = rng.choice(np.array([0.0, 0.1, 0.5, 0.9]), (N, 1, V))
        for k, p in (("ux", "px"), ("uy", "py")):
            d[k][:, g] = 64 * d[p][:, g][:, None, :] + (rng.random((N, 16, V)) < pj) * rng.integers(1, 4, (N, 16, V))
        d["ld"][:, g] = rng.integers(-16, 16, (N, 16, V))
    r = int(rng.integers(0, N)); d["nb"][r, 6] = E; d["ld"][r, 6] = rng.integers(-2047, 2048, (16, V))
    d["wt"] = (d["wt"] * 0.5).astype(np.float32)
    return pack(d)
def check_ranges(d):
    bad = []
    for k, lo, hi in (("ux", -1023, 1023), ("uy", -1023, 1023), ("ld", -2047, 2047), ("px", 0, 7), ("py", 0, 7), ("nb", 0, E), ("bord", 0, V - 1)):
        if np.min(d[k]) < lo or np.max(d[k]) > hi: bad.append("range of " + k)
    w = np.asarray(d["wt"], np.float64)
    if not np.all((w >= 0.25) & (w <= 4)): bad.append("range of wt")
    return bad
def ext(s, bd):
    out = []
    for r in range(N):
        w = [s[r]]
        for d in range(1, N):
            o = (r - d) % N; w.append(np.take_along_axis(s[o], bd[o][:, None, :], 2))
        w.append(np.zeros(s[r].shape[:2] + (1,), s.dtype)); out.append(np.concatenate(w, axis=2))
    return out
def reference(ux, uy, ld, px, py, wt, nb, bord):
    take = np.take_along_axis
    x = ux.astype(np.int32).reshape(N, 8, 16, V); y = uy.astype(np.int32).reshape(N, 8, 16, V); f = ld.astype(np.int32).reshape(N, 8, 16, V)
    P = px.astype(np.int32); Q = py.astype(np.int32)
    L = np.stack([gentries(m) for m in nb]).astype(np.int64).reshape(N, 8, 8, V); bd = np.stack([gentries(m) for m in bord]).astype(np.int64)
    PX = ext(P[:, :, None], bd); PY = ext(Q[:, :, None], bd); WT = ext(wt.astype(np.float64).reshape(N, 8, 16, V), bd)
    q = np.zeros((N, 8, 8, 16, V), np.int32); w = np.zeros((N, 8, 16, V), np.float64)
    for t in range(RO):
        rho = S - 1 - t; U = np.array(L[:, :, :, rho::S])
        own = U < V; near = np.where(own, U, 0)
        c = np.stack([take(L[:, :, (k + t) % 8], near[:, :, k], 2) for k in range(8)], axis=2)
        ok = own & (c < V) & (c % S != rho)
        for j in range(8): ok = ok & (c != U[:, :, j:j + 1])
        c = np.where(ok, c, 0); sc = []
        for k in range(8):
            i = c[:, :, k]; i4 = i[:, :, None]
            dx = (take(P, i, 2) - P[:, :, rho::S])[:, :, None]; dy = (take(Q, i, 2) - Q[:, :, rho::S])[:, :, None]
            e = (take(x, i4, 3) - x[..., rho::S]) * dx + (take(y, i4, 3) - y[..., rho::S]) * dy
            sc.append(np.sum(np.abs(e) > LAM * (dx * dx + dy * dy), axis=2))
        sc = np.where(ok, np.stack(sc, axis=2), 0); best = np.argmax(sc, axis=2)
        named = take(c, best[:, :, None], 2)[:, :, 0]; does = (np.max(sc, axis=2) >= H) & np.any(U == E, axis=2)
        for r in range(N):
            for g in range(8):
                i = np.flatnonzero(does[r, g])
                if i.size == 0: continue
                M = L[r, g]; u, j = np.unique(named[r, g, i], return_index=True); v = rho + S * i[j]
                m = np.any(M[:, u] == E, axis=0); u, v = u[m], v[m]
                if u.size == 0: continue
                su = np.argmax(M[:, u] == E, axis=0); sv = np.argmax(M[:, v] == E, axis=0)
                M[su, u] = v; M[sv, v] = u
        X = ext(x, bd); Y = ext(y, bd); nx = []; ny = []
        for r in range(N):
            sx = np.zeros((8, 16, V), np.int32); sy = np.zeros((8, 16, V), np.int32)
            for k in range(8):
                ix = np.array(L[r, :, k]); i3 = ix[:, None, :]; full = i3 < E
                dx = np.where(full, take(PX[r], i3, 2) - P[r][:, None], 0); dy = np.where(full, take(PY[r], i3, 2) - Q[r][:, None], 0)
                e = (take(X[r], i3, 2) - x[r]) * dx + (take(Y[r], i3, 2) - y[r]) * dy
                T = LAM * (dx * dx + dy * dy); z = q[r, :, k] + e
                z = np.clip(z - np.clip(z, -T, T), -QM, QM)
                stay = np.sum(z == 0, axis=1) < Z
                z = np.where(stay[:, None], z, 0); L[r, :, k] = np.where(stay, ix, E); q[r, :, k] = z
                sx = sx + z * dx; sy = sy + z * dy; w[r] = w[r] + np.abs(z) * take(WT[r], i3, 2)
            nx.append(np.clip(x[r] + ((sx + 16) >> 5), -UM, UM)); ny.append(np.clip(y[r] + ((sy + f[r] + 16) >> 5), -UM, UM))
        x = np.stack(nx); y = np.stack(ny)
    return {"yx": x.reshape(N, 128, V).astype(np.float32), "yy": y.reshape(N, 128, V).astype(np.float32), "yw": w.reshape(N, 128, V).astype(np.float32)}

def check_inputs(d):
    bad = list(check_ranges(d))
    if not bad:
        for name, y in reference(**d).items():
            for q in range(N):
                v = np.abs(np.asarray(y[q], np.float64)); s = np.sqrt(np.mean(v * v))
                if v.max() > 12 * s or s < 2.0 ** 5: bad.append('%s of rank %d is uneven or too small' % (name, q))
    return bad

@@ -1,0 +1,843 @@
+from concourse.bass import DstId, RemoteDMATransfer
+from concourse.mybir import dt, AluOpType, AxisListType, ActivationFunctionType
+
+A = AluOpType
+F = ActivationFunctionType
+f32, b16, h16, i32, u16 = "float32", "bfloat16", "float16", "int32", "uint16"
+E = 1792
+BIG = float(2 ** 20)
+RND = float(3 * 2 ** 22)
+GMODE = ["V" + "S" * 15] * 3
+DMODE = "V" * 16
+BOOST = [20.0, 20.0, 20.0]
+XK = [4, 4, 4]
+S1MODE = "S"
+CSKEW = 2
+CFIRST = True
+HK = 6
+ZB = ("Z0", "Z1")
+BT = "TB"
+BSKEW = 1
+SMODE = "Z"
+MBS = True
+CMS = True
+SEED = 0
+JIT = 0.0
+BANKS = [(("TB", "CB", "D0"), ("X0", "X1", "TB"))] * 3
+XFROM = [99, 99, 99]
+AMODE = ["V" * 16] * 3
+CAPX = ["1" * 16] * 3
+ZHALF = ["0" * 16] * 3
+RNDS = "sv"
+GMODE = ['VVVSSSSSSSSSSSSS', 'VVVSVVSSSSSSSSVS', 'VVSSSSSSVSSSSSSS']
+CAPX = ['0100000000001100', '1000111111100101', '0000001011010011']
+AMODE = ['PPVVVVVVVPPVVVVV', 'PVVVVVVVVVVPPVVV', 'VVVVVVVVVVVVPPPV']
+DMODE = 'SVVVVVVVVSSVVVVS'
+BOOST = [0, 0, 0]
+XK = [5, 5, 5]
+HK = 5
+BANKS = [(('D0', 'D1', 'CB'), ('X0', 'X1', 'TB')), (('D0', 'D1', 'TB'), ('X0', 'X1', 'TB')), (('D0', 'D1', 'CB'), ('X0', 'X1', 'TB'))]
+CFIRST = False
+CMS = False
+
+
+def _sb(shape, d):
+    return ("sbuf", [128] + list(shape), d)
+
+
+SCRATCH = {
+    "DD": _sb([8192], b16), "Q": _sb([8192], h16), "AQ": _sb([8192], h16),
+    "AT0": _sb([1024], h16), "AT1": _sb([1024], h16), "ST0": _sb([1024], b16), "ST1": _sb([1024], b16),
+    "UW": _sb([2, 1800], f32), "PW": _sb([1800], b16), "PO": _sb([1024], b16), "WW": _sb([1800], f32),
+    "LS": _sb([1152], f32), "SACC": _sb([2, 1024], f32), "WACC": _sb([1024], f32), "XACC": _sb([2, 1152], f32),
+    "LDF": _sb([1024], f32), "SL": _sb([1024], b16), "LA0": _sb([9, 256], u16), "LA1": _sb([6, 256], u16),
+    "SND": _sb([3, 256], u16),
+    "IA": _sb([2, 1024], i32), "IC": _sb([1024], i32), "NBI": _sb([512], i32),
+    "BI": _sb([16], i32), "ONB": _sb([512], u16), "OB": _sb([16], u16),
+    "G0": _sb([2, 1024], f32), "G1": _sb([2, 1024], f32), "PB0": _sb([2, 1024], f32), "PB1": _sb([2, 1024], f32),
+    "WG0": _sb([1024], f32), "WG1": _sb([1024], f32),
+    "AZ0": _sb([512], f32), "AZ1": _sb([512], f32), "NZ0": _sb([512], b16), "NZ1": _sb([512], b16),
+    "TT0": _sb([512], h16), "TT1": _sb([512], h16), "SG0": _sb([512], b16), "SG1": _sb([512], b16),
+    "PI": _sb([8], i32), "CL": _sb([32], f32), "J": _sb([144], f32), "IW": _sb([136], f32), "WC": _sb([144], b16),
+    "MX": _sb([24, 128], b16), "DIAG": _sb([128], f32), "MASK": _sb([1032], b16), "RS8": _sb([512], f32),
+    "RS16": _sb([128], f32), "DUM": _sb([128], f32), "DUMM": _sb([128], f32), "VID": _sb([2, 128], f32),
+    "OAI": _sb([64], i32), "OA": _sb([3, 64], u16),
+    "UA": _sb([2, 512], f32), "DS": _sb([2, 512], f32), "GM": _sb([1024], h16), "D1": _sb([512], b16),
+    "MB": _sb([512], b16), "CM": _sb([512], b16), "KI": _sb([128], i32), "NM": _sb([128], i32),
+    "NF": _sb([128], f32), "S1": _sb([128], f32), "SCN": _sb([128], f32), "S2": _sb([128], f32), "SC2": _sb([128], f32),
+    "U16": _sb([128], h16), "EV": _sb([128], b16), "FV": _sb([128], b16), "FC": _sb([128], b16), "MM": _sb([704], b16),
+    "MD": _sb([128], f32), "DF": _sb([128], f32), "ON": _sb([64], u16), "OC": _sb([64], u16), "OX": _sb([64], u16),
+    "OM": _sb([8], u16), "OT": _sb([3, 8], u16), "OVV": _sb([2, 128], f32), "OVC": _sb([2, 128], f32),
+    "DE": _sb([384], b16), "SE": _sb([384], b16), "QE": _sb([384], h16), "AE": _sb([384], f32),
+    "EX": _sb([384], f32), "EY": _sb([384], f32), "EZ": _sb([384], f32), "EN": _sb([384], b16), "ET": _sb([384], h16),
+    "EQ": _sb([384], h16), "E1": _sb([128], f32), "E2": _sb([128], f32), "E3": _sb([128], f32), "E4": _sb([128], f32),
+}
+if SMODE == "Z":
+    SCRATCH.pop("SG0")
+    SCRATCH.pop("SG1")
+SCRATCH["DXY"] = ("psum", [128, 2, 512], f32)
+for _n in ("Z0", "Z1", "TB", "CB", "X0", "X1"):
+    SCRATCH[_n] = ("psum", [128, 512], f32)
+SIZE = {f32: 4, i32: 4, b16: 2, h16: 2, u16: 2}
+NDS = 130
+SEMAPHORES = ["cv", "cs", "cp", "cg"] + ["d%d" % i for i in range(NDS)] + \
+    ["ar%d" % i for i in range(12)] + ["lo%d" % i for i in range(4)]
+(BLK, IB_, NI, DXP, DXN, DYP, DYN, PX_, PY_, MT, ONC, MC, SCO, NBG, PBG, NON, KC, TRI, BD0, BD1, BD2, MTMP, NMT,
+ MCAP) = range(24)
+
+
+def r(name, *ix, p=None):
+    shape = SCRATCH[name][1][1:]
+    ix = list(ix) + [None] * (len(shape) - len(ix))
+    lo = hi = 0
+    n = 1
+    out = []
+    for d, (x, w) in enumerate(zip(ix, shape)):
+        st = 1
+        for y in shape[d + 1:]:
+            st *= y
+        if isinstance(x, int):
+            lo += x * st
+            hi += x * st
+            out.append(x)
+            continue
+        a, b, s = (0, w, 1) if x is None else (tuple(x) + (1,))[:3]
+        c = (b - a + s - 1) // s
+        lo += a * st
+        hi += (a + (c - 1) * s) * st
+        n *= c
+        out.append(slice(a, b, s) if s != 1 else slice(a, b))
+    ps = slice(None) if p is None else slice(*p)
+    if SCRATCH[name][0] == "psum":
+        lo, hi = lo // 512 * 512, hi // 512 * 512 + 511
+    spans = [(lo, hi + 1)]
+    if len(shape) == 2 and isinstance(out[0], slice) and SCRATCH[name][0] != "psum":
+        rows = out[0].stop - out[0].start
+        wid = hi + 1 - lo - (rows - 1) * shape[1]
+        spans = [(lo + q * shape[1], lo + q * shape[1] + wid) for q in range(rows)]
+    return {"k": "b", "name": name, "ix": (ps,) + tuple(out), "spans": spans, "n": n}
+
+
+def ind(win, off):
+    return {"k": "i", "win": win, "off": off, "n": off["n"] * 16, "name": win["name"]}
+
+
+def hbm(name, *ix):
+    return {"k": "h", "name": name, "ix": ix}
+
+
+def mx(i):
+    return r("MX", i)
+
+
+def col(i):
+    return r("CL", (i, i + 1))
+
+
+def _ap(T, x):
+    if not isinstance(x, dict):
+        return x
+    if x["k"] == "i":
+        return _ap(T, x["win"]).indirect(_ap(T, x["off"]))
+    if x["k"] == "h":
+        return T[x["name"]][x["ix"]] if x["ix"] else T[x["name"]][:]
+    return T[x["name"]][x["ix"]]
+
+
+def _parts(x):
+    if not isinstance(x, dict) or x["k"] == "h":
+        return []
+    return [x["win"], x["off"]] if x["k"] == "i" else [x]
+
+
+def _two(x):
+    return SIZE[SCRATCH[x["name"]][2]] == 2
+
+
+def _ps(x):
+    return SCRATCH[x["name"]][0] == "psum"
+
+
+def build():
+    ops = []
+    tag = [0.0]
+
+    def add(eng, kind, args, outs, ins, cost, **kw):
+        w, rd = [], []
+        for o in outs:
+            q = _parts(o)
+            w += q[:1]
+            rd += q[1:]
+        for o in ins:
+            rd += _parts(o)
+        d = {"eng": eng, "kind": kind, "args": args, "w": w, "r": rd, "cost": cost, "up": tag[0]}
+        d.update(kw)
+        ops.append(d)
+        return len(ops) - 1
+
+    def vc(out, in0, c):
+        if out["k"] == "i":
+            return 0.06 + out["n"] * 3.8 * 0.00083
+        if in0 is not None and in0["k"] == "i":
+            return 0.06 + out["n"] * 1.56 * 0.00083
+        return 0.06 + max(64, out["n"] * c) * 0.00083
+
+    def tt(out, a, b, op):
+        add("v", "tt", (out, a, b, op), [out], [a, b], vc(out, a, 1 if _ps(a) or _ps(b) else 2))
+
+    def ts(out, a, s1, o0, s2=None, o1=None):
+        add("v", "ts", (out, a, s1, s2, o0, o1), [out], [a, s1, s2], vc(out, a, 0.5 if _two(out) and _two(a) else 1))
+
+    def cp(out, a):
+        add("v", "cp", (out, a), [out], [a], vc(out, a, 0.5 if _two(out) and _two(a) else 1))
+
+    def ms(out, v):
+        add("v", "ms", (out, v), [out], [], vc(out, None, 0.5 if _two(out) else 1))
+
+    def scan(out, d0, d1, init, o0, o1):
+        add("v", "scan", (out, d0, d1, init, o0, o1), [out], [d0, d1], vc(out, d0, 1))
+
+    def act(out, a, fn, bias=0.0, scale=1.0):
+        add("s", "act", (out, a, fn, bias, scale), [out], [a, bias, scale],
+            0.07 + max(64, out["n"] * (1.56 if a["k"] == "i" else 1)) * 0.00083)
+
+    def mm(terms, start=True, stop=True):
+        c = 0.0
+        ins = []
+        for o, l, x in terms:
+            c += max(64, x["n"]) * (1 if _two(x) else 4) * 0.000417
+            ins += [l, x]
+        add("p", "mm", (terms, start, stop), [terms[0][0]], ins, c + 0.02, cont=not start)
+
+    def iota(out, pat, base, cm):
+        add("g", "iota", (out, pat, base, cm), [out], [], 0.13 + out["n"] * 0.00166)
+
+    def dma(q, pairs, acc=False, nb=None):
+        by = 0
+        for o, i in pairs:
+            x = o if o["k"] == "b" else i
+            by += x["n"] * SIZE[SCRATCH[x["name"]][2]] * 128
+        add(q, "dma", (pairs, acc), [o for o, i in pairs], [i for o, i in pairs],
+            (1.0 if q == "g" else 0.1) * len(pairs), by=(nb or by) * (2 if acc else 1))
+
+    def send(src, land, base):
+        s = add("g", "send", (src, land, base), [], [src], 2.0)
+        for d in range(3):
+            add("x", "recv", (base, d), [land[d]], [], 0.0, after=s)
+
+    dma("y", [(r("IA", 0), hbm("ux")), (r("BI"), hbm("bord"))])
+    dma("s", [(r("IA", 1), hbm("uy"))])
+    ms(r("IC"), 0)
+    dma("s", [(r("NBI"), hbm("nb"))])
+    dma("y", [(r("IC", p=(8 + j, 128, 16)), hbm("px" if j < 2 else "py")) for j in range(4)] +
+        [(r("IC", p=(k, 128, 16)), hbm("nb", slice(None), slice(64 * k, 64 * k + 64))) for k in range(8)], nb=800000)
+    iota(r("PI", (0, 1)), [[0, 1]], 0, 1)
+    iota(r("J"), [[1, 144]], 0, -1)
+    iota(r("DIAG"), [[0, 8], [1, 16]], 0, 0)
+    iota(r("S1"), [[16, 8], [0, 16]], 0, -1)
+    iota(r("MASK"), [[0, 129], [1, 8]], 0, 0)
+    iota(r("OAI"), [[1, 64]], 0, 64)
+    ts(r("PI", (1, 2)), r("PI", (0, 1)), 15, A.bitwise_and)
+    ts(r("PI", (2, 3)), r("PI", (0, 1)), 8, A.bitwise_and)
+    cp(col(0), r("PI", (1, 2)))
+    cp(col(1), r("PI", (2, 3)))
+    ts(col(2), col(0), 8.0, A.is_lt)
+    ts(r("DIAG"), r("DIAG"), col(0), A.is_equal)
+
+    def oh(i):
+        return r("DIAG", (i, i + 1))
+
+    def mkcol(c, terms, first=0.0):
+        prev = first
+        for row, v in terms:
+            act(col(c), oh(row), F.Identity, bias=prev, scale=float(v))
+            prev = col(c)
+    mkcol(16, [(8, 1), (9, -1), (10, 1)])
+    mkcol(17, [(11, -1), (14, 1), (15, 1)])
+    tt(col(7), col(16), col(17), A.add)
+    tt(col(15), col(7), oh(12), A.add)
+    ts(col(18), col(0), 8.0, A.is_ge)
+    ts(r("MASK"), r("MASK"), col(0), A.is_equal, col(15), A.add)
+    ts(r("PO"), r("IC"), col(18), A.mult, col(7), A.subtract)
+    cp(r("OB"), r("BI"))
+    ts(r("UW", None, (0, 1024)), r("IA"), 1024.0, A.add)
+    tt(r("PW", (0, 1024)), r("PO"), r("MASK", (0, 1024)), A.add)
+    cp(r("SND", 0), ind(r("UW", 0, (0, 1024)), r("OB")))
+    cp(r("SND", 1), ind(r("UW", 1, (0, 1024)), r("OB")))
+    ts(r("SND", 2), ind(r("PW", (0, 1024)), r("OB")), col(2), A.max)
+    send(r("SND"), [r("LA0", (3 * d, 3 * d + 3)) for d in range(3)], 0)
+    cp(r("ONB"), r("NBI"))
+    ms(r("UW", None, (1792, 1800)), 0.0)
+    ms(r("WW", (1792, 1800)), 0.0)
+    ts(r("PW", (1792, 1800)), r("MASK", (0, 8)), 0.0, A.mult, col(2), A.add)
+    ms(r("LS", (1024, 1152)), 0.0)
+    ts(r("OAI"), r("OAI"), 1023, A.bitwise_and)
+    cp(r("ON"), r("OAI"))
+    ts(r("LS", (0, 1024)), ind(r("IC"), r("ON")), float(E), A.subtract, col(2), A.mult)
+    iota(r("OAI"), [[16, 64]], 0, 0)
+    for t in range(3):
+        ts(r("OA", t), r("OAI"), col(1), A.add, float(7 - t), A.add)
+    ts(mx(BLK), r("S1"), col(0), A.add, 0.0, A.is_equal)
+    ts(r("IW"), r("J", (0, 136)), 8.0, A.is_equal)
+    ts(r("WC"), r("J"), col(0), A.add, 15.0, A.is_equal)
+    I32 = r("IW", (8, 136))
+    act(mx(IB_), I32, F.Identity)
+    act(mx(NI), I32, F.Identity, scale=-1.0)
+    mkcol(3, [(8, 0.25), (9, -0.25)])
+    mkcol(4, [(10, 0.25), (11, -0.25)])
+    mkcol(5, [(8, 32), (9, 32), (10, 32), (11, 32), (15, -128)])
+    mkcol(6, [(12, 32768), (15, -23552)])
+    mkcol(19, [(0, 1024), (1, -1)])
+    mkcol(8, [(15, -BIG + (131072 if CMS else 0)), (14, 1)])
+    for t in range(3):
+        mkcol(9 + t, [(7 - t, -BIG)], first=col(8))
+    mkcol(12, [(15, -1)], first=1.0)
+    mkcol(13, [(15, 200)])
+    ts(col(14), col(0), -2048.0, A.mult, 16128.0, A.add)
+    tt(col(14), col(14), col(2), A.mult)
+    for m, c in ((DXP, 3), (DYP, 4), (MT, 5), (MC, 6), (KC, 14), (BD0, 9), (BD1, 10), (BD2, 11), (MCAP, 19)):
+        act(mx(m), mx(BLK), F.Identity, scale=col(c))
+    for m, s, v in ((DXN, DXP, -1.0), (DYN, DYP, -1.0), (PX_, DXP, 1 / 32), (PY_, DYP, 1 / 32), (ONC, BLK, 1024.0),
+                    (SCO, BLK, 8192.0 if CMS else 16384.0), (NBG, BLK, -BIG), (PBG, BLK, BIG), (NON, BLK, -1.0), (NMT, MT, -1.0)):
+        act(mx(m), mx(s), F.Identity, scale=v)
+    ts(mx(MTMP), r("J", (0, 128)), 0.0, A.is_gt, -2.0, A.mult)
+    tt(mx(MTMP), mx(MTMP), I32, A.add)
+    tt(mx(MTMP), mx(MTMP), mx(BLK), A.mult)
+    ts(mx(TRI), mx(MTMP), col(2), A.mult)
+    iota(r("DUM"), [[-1, 128]], 1152, 0)
+    for t in range(2):
+        iota(r("VID", t), [[8, 128]], 7 - t - E, 0)
+    ts(r("DUMM"), r("DUM"), -1.0, A.add)
+    tt(r("DUMM"), r("DUMM"), r("DIAG"), A.mult)
+    act(r("RS8"), r("MASK", (0, 512)), F.Identity, bias=1e9, scale=0.0)
+    ms(r("RS16"), 1.0)
+    ms(r("RS16", (0, 128, 16)), 0.0)
+    ms(r("MM", (0, 8)), 0.0)
+    ms(r("QE"), 0.0)
+    act(r("AE"), r("MASK", (0, 384)), F.Identity, scale=0.0)
+    act(r("SL"), r("MASK", (0, 1024)), F.Identity, scale=0.0)
+    ms(r("XACC", None, (1024, 1152)), 0.0)
+    dma("y", [(r("IA", 0), hbm("ld"))])
+    dma("y", [(r("WW", (0, 1024)), hbm("wt"))])
+    ts(r("LDF"), r("IA", 0), 0.5, A.add, 1 / 32, A.mult)
+
+    def convert(t):
+        for d in range(3):
+            la, b = (("LA0", 3 * d), ("LA1", 2 * d), ("LA0", 2 * d))[t]
+            cp(r("UW", None, (1024 + 256 * d, 1280 + 256 * d)), r(la, (b, b + 2)))
+            if t == 0:
+                cp(r("PW", (1024 + 256 * d, 1280 + 256 * d)), r(la, b + 2))
+    convert(0)
+
+    def stage_a(c):
+        mm([(c["bx"], mx(DXN if c["neg"] else DXP), c["dd"])])
+        mm([(c["by"], mx(DYN if c["neg"] else DYP), c["dd"])])
+        if "gxy" in c:
+            tt(c["gxy"], c["gxy"], r("DXY"), A.mult)
+        else:
+            tt(c["gx"], c["gx"], c["bx"], A.mult)
+            tt(c["gy"], c["gy"], c["by"], A.mult)
+        last = [(c["bz"], mx(IB_), c["q"])] if c["hasq"] else []
+        if c.get("zh"):
+            dma("g", [(c["gx"], c["gy"])], acc=True)
+            mm(last + [(c["bz"], I32, c["gx"])])
+        else:
+            mm(last + [(c["bz"], I32, c["gx"])], True, False)
+            mm([(c["bz"], I32, c["gy"])], False, True)
+
+    def stage_b(c):
+        act(c["az"], c["bz"], F.Abs)
+        act(c.get("sg") or c["bz"], c["bz"], F.Sign)
+        if c.get("am") == "P":
+            mm([(c["bt"], mx(NMT), c["dd"]), (c["bt"], I32, c["az"])])
+            act(c["az"], c["bt"], F.Relu)
+            act(c["nz"], c["az"], F.Sign, bias=-0.5)
+        else:
+            mm([(c["bt"], mx(MT), c["dd"])])
+            tt(c["az"], c["az"], c["bt"], A.subtract)
+            act(c["nz"], c["az"], F.Sign, bias=-0.5)
+            if c.get("cx"):
+                act(c["az"], c["az"], F.Relu)
+        mm([(c["bc"], mx(MC), c["alive"]), (c["bc"], mx(ONC), c["nz"])])
+        if c.get("cx"):
+            act(c["stay"], c["bc"], F.Sigmoid)
+            mm([(c["bc"], mx(MCAP), c["stay"])])
+            tt(c["aq"], c["az"], c["bc"], A.min)
+        else:
+            tt(c["tt"], c["az"], c["bc"], A.min)
+            ts(c["aq"], c["tt"], 0.0, A.max, 1023.0, A.min)
+        if c.get("bs"):
+            mm([(c["bs"], mx(IB_), c["sg"])])
+        tt(c["q"], c["aq"], c.get("bs") or c.get("sg") or c["bz"], A.mult)
+        if c["stay"] is not None and not c.get("cx"):
+            act(c["stay"], c["bc"], F.Sigmoid, bias=c["sb"], scale=c["ss"])
+
+    def stage_c(c):
+        mm([(c["cx_"], mx(PX_), c["dd"])])
+        tt(c["px"], c["q"], c["cx_"], A.mult)
+        mm([(c["cy_"], mx(PY_), c["dd"])])
+        tt(c["py"], c["q"], c["cy_"], A.mult)
+
+    X0, X1 = r("X0"), r("X1")
+
+    def bank(x):
+        return r("DXY", int(x[1])) if x[0] == "D" else r(x)
+
+    def x0(a, b, s=1):
+        return r("X0", (a, b, s))
+
+    def x1(a, b, s=1):
+        return r("X1", (a, b, s))
+
+    def step1(t):
+        rho = 7 - t
+        LSW = r("LS")
+        act_ls = r("LS", (rho, 1024, 8))
+        mm([(x0(0, 64), I32, r("LS", (rho, 1024, 16))), (x0(0, 64), r("IW", (0, 128)), r("LS", (rho + 8, 1024, 16)))])
+        ts(r("ON"), x0(0, 64), float(E), A.add, 1024.0, A.min)
+        tt(r("GM"), ind(LSW, r("ON")), r("MASK", (t, t + 1024)), A.mult)
+        cp(r("U16"), act_ls)
+        ts(r("EV"), act_ls, 0.0, A.is_equal)
+        mm([(x1(0, 128), mx(TRI), r("EV"))])
+        ts(r("FV"), x1(0, 128), 1.0, A.is_equal)
+        mm([(x0(0, 64), r("WC", (15 - i, 143 - i)), r("GM", (i, 1024, 16))) for i in range(16)])
+        ts(r("OX"), x0(0, 64), float(E), A.add, 1023.0, A.min)
+        ts(r("OC"), x0(0, 64), float(E), A.add)
+        for h in range(2):
+            o = (32 * h, 32 * h + 32)
+            for c in range(2):
+                act(r("UA", c), ind(r("UW", c, (0, 1024)), r("OA", t, o)), F.Identity)
+            for c in range(2):
+                if S1MODE == "S":
+                    act(r("DS", c), ind(r("UW", c, (0, 1024)), r("OX", o)), F.Identity, scale=-1.0)
+                else:
+                    tt(r("DS", c), ind(r("UW", c, (0, 1024)), r("OX", o)), r("UA", c), A.subtract)
+            if S1MODE == "S":
+                dma("g", [(r("DS"), r("UA"))], acc=True)
+            act(r("D1"), ind(r("PW"), r("OC", o)), F.Identity)
+            gm = r("GM", (512 * h, 512 * h + 512))
+            mm([(X1, mx(BLK), gm)] + [(x1(k, 512, 8), mx(NI), r("U16", (64 * h, 64 * h + 64))) for k in range(8)])
+            if MBS:
+                act(X1, X1, F.Square)
+                act(r("MB"), X1, F.Relu, bias=1.0, scale=-1.0)
+            else:
+                ts(r("MB"), X1, 0.0, A.is_equal)
+            mm([(X0, mx(IB_), r("D1"))] +
+               [(x0(k, 512, 8), mx(NI), r("PO", (512 * h + rho, 512 * h + 512, 8))) for k in range(8)])
+            act(r("D1"), X0, F.Square)
+            neg = S1MODE == "S"
+            mm([(X0, mx(DXN if neg else DXP), r("D1"))])
+            mm([(X1, mx(DYN if neg else DYP), r("D1"))])
+            tt(r("DS", 0), r("DS", 0), X0, A.mult)
+            tt(r("DS", 1), r("DS", 1), X1, A.mult)
+            mm([(X0, I32, r("DS", 0))], True, False)
+            mm([(X0, I32, r("DS", 1))], False, True)
+            act(r("DS", 0), X0, F.Abs)
+            if CMS:
+                mm([(X1, mx(NMT), r("D1")), (X1, I32, r("DS", 0))])
+                act(r("CM"), X1, F.Sign, bias=-0.5)
+            else:
+                mm([(X1, mx(MT), r("D1"))])
+                tt(r("CM"), r("DS", 0), X1, A.is_gt)
+            mm([(X0, mx(BLK), gm), (X0, mx(KC), r("MASK", (0, 512))), (X0, mx(BD0 + t), r("D1")), (X0, mx(NBG), r("MB"))] +
+               [(x0(k, 512, 8), mx(PBG), r("FV", (64 * h, 64 * h + 64))) for k in range(8)] + [(X0, mx(SCO), r("CM"))])
+            ts(r("RS8", (0, 512, 8)), r("DUM", (64 * h, 64 * h + 64)), 71.0 * 2048, A.add)
+            scan(r("DS", 1), r("RS8"), X0, 1e9, A.min, A.max)
+            cp(r("KI", (64 * h, 64 * h + 64)), r("DS", 1, (7, 512, 8)))
+        ts(r("NM"), r("KI"), 2047, A.bitwise_and)
+        tt(r("S1"), r("NM"), r("DIAG"), A.mult)
+        cp(r("NF"), r("NM"))
+        scan(r("SCN"), r("RS16"), r("S1"), 0.0, A.mult, A.add)
+        ts(r("OM"), r("SCN", (15, 128, 16)), -1.0, A.add)
+        ts(r("EV"), ind(LSW, r("OM")), 0.0, A.is_equal)
+        mm([(x1(0, 128), mx(TRI), r("EV"))])
+        tt(r("MM", (1, 128)), r("NF", (1, 128)), r("SCN", (0, 127)), A.is_equal)
+        ts(r("MM", (128, 256)), r("NF"), 1025.0, A.is_ge)
+        terms = [(x0(0, 128), mx(NON), r("MM", (0, 128))), (x0(0, 128), mx(NON), r("MM", (128, 256)))]
+        at = 256
+        for j in range(7):
+            a = 16 * (j + 1)
+            ts(r("MM", (at, at + 128 - a)), r("NF", (a, 128)), r("SCN", (a - 1, a)), A.is_equal)
+            terms.append((x0(a, 128), mx(NON), r("MM", (at, at + 128 - a))))
+            at += 128 - a
+        ts(r("FC"), x1(0, 128), 1.0, A.is_equal)
+        tt(r("DF"), r("NF"), r("DUM"), A.subtract)
+        tt(r("DF"), r("DF"), r("DIAG"), A.mult)
+        mm(terms + [(x0(0, 128), mx(BLK), r("FC"))])
+        ts(r("MD"), x0(0, 128), 1.0, A.is_equal)
+        ts(r("SE", (128 * t, 128 * t + 128)), x0(0, 128), 1.0, A.is_equal, oh(15), A.max)
+        tt(r("S2"), r("MD"), r("DF"), A.mult)
+        tt(r("S2"), r("S2"), r("DUMM"), A.add)
+        scan(r("SC2"), r("RS16"), r("S2"), 0.0, A.mult, A.add)
+        cp(r("OT", t), r("SC2", (15, 128, 16)))
+        de = r("DE", (128 * t, 128 * t + 128))
+        tt(de, ind(r("PW"), r("OT", t)), r("PO", (rho, 1024, 8)), A.subtract)
+        act(de, de, F.Square)
+        if t < 2:
+            ts(r("S1"), r("NF"), -1.0 - E, A.add)
+            tt(r("OVV", t), r("S1"), r("FV"), A.mult)
+            tt(r("OVC", t), r("VID", t), r("FC"), A.mult)
+
+    def extras(t):
+        w = (0, 128 * (t + 1))
+        act(r("XACC", 0, (0, 1024)), r("LDF"), F.Identity, bias=1 / 64, scale=0.0)
+        act(r("XACC", 1, (0, 1024)), r("LDF"), F.Identity)
+        dma("g", [(r("XACC", None, (0, 1024)), r("UW", None, (0, 1024)))], acc=True)
+        for b in range(t + 1):
+            for c, n in ((0, "EX"), (1, "EY")):
+                e = r(n, (128 * b, 128 * b + 128))
+                act(e, r("UW", c, (7 - b, 1024, 8)), F.Identity)
+                tt(e, ind(r("UW", c, (0, 1152)), r("OT", b)), e, A.subtract)
+        c = {"bx": r("X0", w), "by": r("X1", w), "bz": r("X0", w), "bt": r("X1", w), "bc": r("X1", w), "neg": False,
+             "cx_": r("X0", w), "cy_": r("X1", w),
+             "dd": r("DE", w), "gx": r("EX", w), "gy": r("EY", w), "q": r("QE", w), "hasq": True, "az": r("EZ", w),
+             "nz": r("EN", w), "alive": r("SE", w), "tt": r("ET", w), "aq": r("EQ", w),
+             "stay": r("SE", w) if t < 2 else None, "sb": col(13), "ss": col(12), "px": r("EX", w), "py": r("EY", w)}
+        stage_a(c)
+        stage_b(c)
+        stage_c(c)
+        tt(r("AE", w), r("AE", w), r("EQ", w), A.add)
+        for b in range(t + 1):
+            for cc, n, tmp in ((0, "EX", "E1"), (1, "EY", "E2")):
+                pe = r(n, (128 * b, 128 * b + 128))
+                own = r("XACC", cc, (7 - b, 1024, 8))
+                tt(own, own, pe, A.add)
+                tt(r(tmp), ind(r("XACC", cc), r("OT", b)), pe, A.subtract)
+                cp(ind(r("XACC", cc), r("OT", b)), r(tmp))
+        if t == 2:
+            act(r("LS", (0, 1024)), r("LDF"), F.Identity, scale=0.0)
+            for b in range(3):
+                ae = r("AE", (128 * b, 128 * b + 128))
+                own = r("LS", (7 - b, 1024, 8))
+                tt(r("E1"), ind(r("WW"), r("OT", b)), ae, A.mult)
+                tt(r("E2"), r("WW", (7 - b, 1024, 8)), ae, A.mult)
+                tt(own, own, r("E1"), A.add)
+                tt(r("E3"), ind(r("LS"), r("OT", b)), r("E2"), A.add)
+                cp(ind(r("LS"), r("OT", b)), r("E3"))
+
+    def rows_update(t):
+        tt(r("LS", (0, 1024)), r("LS", (0, 1024)), r("SL"), A.mult)
+        for b in range(t + 1):
+            se = r("SE", (128 * b, 128 * b + 128))
+            own = r("LS", (7 - b, 1024, 8))
+            tt(r("E3"), r("OVV", b), se, A.mult)
+            tt(r("E4"), r("OVC", b), se, A.mult)
+            tt(own, own, r("E3"), A.add)
+            tt(r("E3"), ind(r("LS"), r("OT", b)), r("E4"), A.add)
+            cp(ind(r("LS"), r("OT", b)), r("E3"))
+
+    for t in range(3):
+        tag[0] = BOOST[t]
+        step1(t)
+        if t == 0:
+            cp(r("EZ", (0, 256)), ind(r("WW", (0, 1024)), r("OB")))
+            send(r("EZ", (0, 256)), [r("WW", (1024 + 256 * d, 1280 + 256 * d)) for d in range(3)], 9)
+        extras(t)
+
+        def piece(j):
+            k, h = divmod(j, 2)
+            cs, hs = (512 * j, 512 * j + 512), (512 * h, 512 * h + 512)
+            g, pb = "G%d" % (k % 2), "PB%d" % (k % 2)
+            c = {"bx": r("DXY", 0), "by": r("DXY", 1), "gxy": r(g, None, hs), "am": AMODE[t][j],
+                 "cx": CAPX[t][j] == "1", "zh": ZHALF[t][j] == "1", "bz": r(ZB[j % len(ZB)]), "bt": bank(BT), "bc": r("CB"),
+                 "neg": GMODE[t][j] == "S", "dd": r("DD", cs), "gx": r(g, 0, hs), "gy": r(g, 1, hs), "q": r("Q", cs),
+                 "hasq": t > 0, "az": r("AZ%d" % (j % len(ZB))), "nz": r("NZ%d" % (j % 2)), "alive": r("DD", cs),
+                 "tt": r("TT%d" % (j % 2)), "aq": r("AQ", cs) if t == 0 else r("AT%d" % (k % 2), hs),
+                 "stay": r("ST%d" % (k % 2), hs) if t < 2 or CAPX[t][j] == "1" else None, "sb": 0.0, "ss": 1.0}
+            c["cx_"], c["cy_"], c["bw"] = [bank(x) for x in BANKS[t][j >= XFROM[t]]]
+            if SMODE != "Z":
+                c["sg"] = r("SG%d" % (j % 2))
+                c["bs"] = None if SMODE == "S" else bank(SMODE)
+            if k == 0:
+                c["px"], c["py"], c["pw"] = r("SACC", 0, hs), r("SACC", 1, hs), r("WACC", hs)
+            elif k == 7:
+                c["px"], c["py"], c["pw"] = c["cx_"], c["cy_"], c["bw"]
+            else:
+                c["px"], c["py"], c["pw"] = r(pb, 0, hs), r(pb, 1, hs), r("WG%d" % (k % 2), hs)
+            c["wg"], c["aqs"] = r("WG%d" % (k % 2), hs), r("AQ", cs)
+            return c
+
+        def fetch(j):
+            o = r("ONB", (32 * j, 32 * j + 32))
+            g, hs = "G%d" % (j // 2 % 2), (512 * (j % 2), 512 * (j % 2) + 512)
+            if GMODE[t][j] == "V":
+                dma("y", [(r(g, None, hs), r("UW", None, hs))])
+            for c in range(2):
+                if GMODE[t][j] == "S":
+                    act(r(g, c, hs), ind(r("UW", c), o), F.Identity, scale=-1.0)
+                else:
+                    tt(r(g, c, hs), ind(r("UW", c), o), r(g, c, hs), A.subtract)
+            if GMODE[t][j] == "S":
+                dma("g", [(r(g, None, hs), r("UW", None, hs))], acc=True)
+
+        def pre(j):
+            po = r("PO", (512 * (j % 2), 512 * (j % 2) + 512))
+            dd = r("DD", (512 * j, 512 * j + 512))
+            o = r("ONB", (32 * j, 32 * j + 32))
+            if DMODE[j] == "V":
+                tt(dd, ind(r("PW"), o), po, A.subtract)
+                act(dd, dd, F.Square)
+            else:
+                act(dd, ind(r("PW"), o), F.Identity)
+                mm([(bank(BT), mx(IB_), dd), (bank(BT), mx(NI), po)])
+                act(dd, bank(BT), F.Square)
+
+        def finish(j):
+            k, h = divmod(j, 2)
+            c = piece(j)
+            stage_c(c)
+            hs = (512 * h, 512 * h + 512)
+            if t == 2:
+                if h == 0:
+                    act(r("WG%d" % (k % 2)), ind(r("WW"), r("ONB", (64 * k, 64 * k + 64))), F.Identity)
+                mm([(c["bw"], mx(IB_), c["aqs"]), (c["bw"], mx(IB_), c["aq"])])
+                tt(c["pw"], c["wg"], c["bw"], A.mult)
+                if k == 7:
+                    tt(r("WACC", hs), r("WACC", hs), c["bw"], A.add)
+                    dma("s", [(hbm("yw", slice(None), slice(*hs)), r("WACC", hs))])
+            if k == 7:
+                for cc in range(2):
+                    s = r("SACC", cc, hs)
+                    tt(s, s, c[("px", "py")[cc]], A.add)
+                    ts(s, s, 1.0, A.max, 2047.0, A.min)
+                    out = r("UW", cc, hs) if t < 2 else s
+                    back = RND if t < 2 else RND + 1024.0
+                    if RNDS[cc] == "v":
+                        ts(out, s, RND, A.add, back, A.subtract)
+                    else:
+                        act(s, s, F.Identity, bias=RND)
+                        act(out, s, F.Identity, bias=-back)
+                    if t == 2:
+                        dma("y", [(hbm(("yx", "yy")[cc], slice(None), slice(*hs)), s)])
+            if h == 1:
+                ks = (1024 * k, 1024 * k + 1024)
+                if t < 2:
+                    st = "ST%d" % (k % 2)
+                    dma("y", [(r("SL", p=(k, 128, 16)), r(st, p=(k, 128, 16))),
+                              (r("DD", ks, p=(12, 128, 16)), r(st, p=(12, 128, 16)))], nb=100000)
+                if t == 1:
+                    dma("g", [(r("AQ", ks), r("AT%d" % (k % 2)))], acc=True)
+                if 0 < k < HK:
+                    dma("g", [(r("SACC"), r("PB%d" % (k % 2)))], acc=True)
+                    if t == 2:
+                        dma("g", [(r("WACC"), r("WG%d" % (k % 2)))], acc=True)
+                if k == XK[t]:
+                    dma("g", [(r("SACC"), r("XACC", None, (0, 1024)))], acc=True)
+                    if t == 2:
+                        dma("g", [(r("WACC"), r("LS", (0, 1024)))], acc=True)
+            if HK <= k < 7:
+                dma("g", [(r("SACC", None, hs), r("PB%d" % (k % 2), None, hs))], acc=True)
+                if t == 2:
+                    dma("g", [(r("WACC", hs), r("WG%d" % (k % 2), hs))], acc=True)
+
+        tag[0] = 0.0
+        for j in range(3):
+            fetch(j)
+        if t == 0:
+            pre(0)
+        for j in range(16 + CSKEW):
+            if j < 16:
+                if j >= 1 and j + 2 < 16 and j + 2 > 2:
+                    fetch(j + 2)
+                if t == 0 and j < 15:
+                    pre(j + 1)
+                stage_a(piece(j))
+            if CFIRST and j >= CSKEW:
+                finish(j - CSKEW)
+            if BSKEW <= j < 16 + BSKEW:
+                stage_b(piece(j - BSKEW))
+            if not CFIRST and j >= CSKEW:
+                finish(j - CSKEW)
+        if t < 2:
+            cp(r("SND", 0), ind(r("UW", 0, (0, 1024)), r("OB")))
+            cp(r("SND", 1), ind(r("UW", 1, (0, 1024)), r("OB")))
+            la = ("LA1", "LA0")[t]
+            send(r("SND", (0, 2)), [r(la, (2 * d, 2 * d + 2)) for d in range(3)], 3 * (t + 1))
+            rows_update(t)
+            convert(t + 1)
+    return ops
+
+
+def hazards(ops):
+    seen = {}
+    for i, o in enumerate(ops):
+        dep = set()
+        acc = [(x, True) for x in o["w"]] + [(x, False) for x in o["r"]]
+        acc = [(x, wr, a, b) for x, wr in acc for a, b in x["spans"]]
+        for x, wr, a, b in acc:
+            ps = _ps(x)
+            for (j, lo, hi, w2) in seen.get(x["name"], []):
+                if lo < b and a < hi and (wr or w2 or (ps and ops[j]["eng"] != o["eng"])):
+                    dep.add(j)
+        if o["kind"] == "recv":
+            dep = {o["after"]}
+        for x, wr, a, b in acc:
+            lst = seen.setdefault(x["name"], [])
+            if wr:
+                lst[:] = [e for e in lst if e[0] == i or not (a <= e[1] and e[2] <= b)]
+            lst.append((i, a, b, wr))
+        dep.discard(i)
+        o["dep"] = sorted(dep)
+
+
+def arrange(ops):
+    hazards(ops)
+    n = len(ops)
+    succ = [[] for _ in ops]
+    for i, o in enumerate(ops):
+        for j in o["dep"]:
+            succ[j].append(i)
+
+    def tail(o):
+        if o["kind"] == "dma":
+            return 1.6 + o["by"] / 600e3
+        return 4.0 if o["kind"] == "send" else 0.0
+    level = [0.0] * n
+    for i in range(n - 1, -1, -1):
+        level[i] = ops[i]["cost"] + tail(ops[i]) + 0.1 + max([level[j] for j in succ[i]] + [0.0])
+    z = SEED
+    for i in range(n):
+        z = (z * 1103515245 + 12345) % 2147483648
+        level[i] += JIT * (z / 2147483648.0)
+    left = [len(o["dep"]) for o in ops]
+    ready = {e: [] for e in "vspgyx"}
+    at = [0.0] * n
+    fin = [0.0] * n
+    for i, o in enumerate(ops):
+        if not left[i]:
+            ready[o["eng"]].append(i)
+    free = {e: 0.0 for e in "vspgyx"}
+    pipe = [0.0]
+    order = []
+    while len(order) < n:
+        best = None
+        for e, lst in ready.items():
+            if not lst:
+                continue
+            s = min(max(free[e], at[i]) for i in lst)
+            i = max((i for i in lst if max(free[e], at[i]) <= s + 0.05), key=lambda q: level[q] + ops[q]["up"])
+            s = max(free[e], at[i])
+            if best is None or s < best[0]:
+                best = (s, i)
+        s, i = best
+        o = ops[i]
+        ready[o["eng"]].remove(i)
+        order.append(i)
+        o["t0"] = s
+        end = s + o["cost"]
+        if o["kind"] != "recv":
+            free[o["eng"]] = end
+        if o["kind"] == "dma":
+            pipe[0] = max(pipe[0], end + 0.8) + o["by"] / 600e3
+            end = pipe[0] + 0.8
+        if o["kind"] == "send":
+            end += 4.0
+        fin[i] = o["t1"] = end
+        for j in succ[i]:
+            lat = 0.0 if ops[j].get("cont") and o["eng"] == "p" else 0.1
+            at[j] = max(at[j], end + lat)
+            left[j] -= 1
+            if not left[j]:
+                ready[ops[j]["eng"]].append(j)
+    return order
+
+
+PLAN = []
+
+
+def rank_program(g, core, T, topo):
+    rank = T.rank_of(core)
+    if rank is None:
+        return
+    if not PLAN:
+        ops = build()
+        PLAN.append((ops, arrange(ops)))
+    ops, order = PLAN[0]
+    n = len(T.cores)
+
+    def engines(src, d):
+        en = topo.engines(T.cores[src], T.cores[(src + d + 1) % n])
+        q = len(en) // 4
+        return (en[0::2][:q], en[0::2][q:2 * q], en[1::2][:2 * q])[d]
+
+    queue = {"v": g.vector, "s": g.scalar, "p": g.tensor, "g": g, "y": g.sync}
+    known = {e: {} for e in queue}
+    count = {e: 0 for e in queue}
+    waited, top, token, clock = {}, {}, {}, {}
+    nd = [0]
+
+    def wait(e, s, v):
+        queue[e].wait_ge(T.sem[s], v)
+        waited[s] = max(waited.get(s, 0), v)
+
+    for i in order:
+        o = ops[i]
+        e, kind, a = o["eng"], o["kind"], o["args"]
+        if kind == "recv":
+            token[i] = ("ar%d" % (a[0] + a[1]), len(engines((rank - a[1] - 1) % n, a[1])))
+            top[token[i][0]] = token[i][1]
+            clock[i] = {}
+            continue
+        kn = known[e]
+        need = {}
+        for j in o["dep"]:
+            if o.get("cont") and ops[j]["eng"] == "p" and ops[j]["w"][0]["name"] == o["w"][0]["name"]:
+                continue
+            s, v = token[j]
+            if kn.get(s, 0) < v and need.get(s, (0, 0))[0] < v:
+                need[s] = (v, j)
+        for s, (v, j) in sorted(need.items(), key=lambda x: -ops[x[1][1]]["t1"]):
+            if kn.get(s, 0) >= v:
+                continue
+            wait(e, s, v)
+            kn[s] = v
+            for s2, v2 in clock[j].items():
+                if kn.get(s2, 0) < v2:
+                    kn[s2] = v2
+        q = queue[e]
+        if kind == "dma":
+            s = "d%d" % nd[0]
+            nd[0] += 1
+            for out, src in a[0]:
+                kw = {"accum_op": A.add} if a[1] else {}
+                q.dma_start(_ap(T, out), _ap(T, src), **kw).then_inc(T.sem[s], 16)
+            token[i] = (s, 16 * len(a[0]))
+        elif kind == "send":
+            trs, tot = [], 0
+            for d in range(n - 1):
+                rid, pid, se = topo.addr(T.cores[(rank + d + 1) % n])
+                en = engines(rank, d)
+                tot += len(en)
+                trs.append(RemoteDMATransfer(dst_ids=[DstId(rid=rid, pnc=pid)], dma_engine_mask=sum(1 << x for x in en),
+                                             remote_sem=T.sem["ar%d" % (a[2] + d)], src=_ap(T, a[0]), dst=_ap(T, a[1][d])))
+            s = "lo%d" % (a[2] // 3)
+            g.remote_dma_fused(trs, local_sem=T.sem[s])
+            token[i] = (s, tot)
+        else:
+            x = [_ap(T, y) for y in a] if kind != "mm" else None
+            if kind == "tt":
+                ins = q.tensor_tensor(*x)
+            elif kind == "ts":
+                ins = q.tensor_scalar(*(x if x[5] is not None else x[:5]))
+            elif kind == "cp":
+                ins = q.tensor_copy(*x)
+            elif kind == "ms":
+                ins = q.memset(*x)
+            elif kind == "scan":
+                ins = q.tensor_tensor_scan(*x)
+            elif kind == "act":
+                ins = q.activation(x[0], x[1], x[2], bias=x[3], scale=x[4])
+            elif kind == "iota":
+                kw = {} if SCRATCH[a[0]["name"]][2] == i32 else {"allow_small_or_imprecise_dtypes": True}
+                ins = q.iota(*x, **kw)
+            else:
+                for m, (out, l, rhs) in enumerate(a[0]):
+                    ins = q.matmul(_ap(T, out), _ap(T, l), _ap(T, rhs), a[1] and m == 0, a[2] and m == len(a[0]) - 1)
+            count[e] += 1
+            ins.then_inc(T.sem["c" + e], 1)
+            token[i] = ("c" + e, count[e])
+        top[token[i][0]] = token[i][1]
+        clock[i] = dict(kn)
+    for s, v in top.items():
+        if waited.get(s, 0) < v:
+            wait("g", s, v)

@@ -28,7 +28,12 @@ XFROM = [99, 99, 99]
 AMODE = ["V" * 16] * 3
 CAPX = ["1" * 16] * 3
 ZHALF = ["0" * 16] * 3
-RNDS = "sv"
+RNDS = "sssv"
+FIN3 = "11"
+LOOK = 0.05
+PASSES = 2
+S1Z = "DDD"
+GLOOK = 0.9
 GMODE = ['VVVSSSSSSSSSSSSS', 'VVVSVVSSSSSSSSVS', 'VVSSSSSSVSSSSSSS']
 CAPX = ['0100000000001100', '1000111111100101', '0000001011010011']
 AMODE = ['PPVVVVVVVPPVVVVV', 'PVVVVVVVVVVPPVVV', 'VVVVVVVVVVVVPPPV']
@@ -39,6 +44,19 @@ HK = 5
 BANKS = [(('D0', 'D1', 'CB'), ('X0', 'X1', 'TB')), (('D0', 'D1', 'TB'), ('X0', 'X1', 'TB')), (('D0', 'D1', 'CB'), ('X0', 'X1', 'TB'))]
 CFIRST = False
 CMS = False
+GMODE = ['VVVSSSSSSSSSSSSS', 'VVSSSSSSSSSSSSSS', 'VVSSVSSSSSSSSSSS']
+CAPX = ['0000000111111000', '0000011000000000', '0000100010001001']
+AMODE = ['VVVVPVVVVVVVVVVV', 'VVVVVVVVVVVVVVVV', 'VVVVVVVVVPPVPPPP']
+DMODE = 'VVVDVVVDVDDDDVVD'
+XK = [4, 5, 5]
+HK = 6
+BANKS = [(('D0', 'D1', 'CB'), ('X0', 'X1', 'TB')), (('TB', 'D1', 'CB'), ('X0', 'X1', 'TB')), (('D0', 'D1', 'CB'), ('X0', 'X1', 'TB'))]
+MBS = False
+RNDS = 'SSvs'
+FIN3 = '01'
+ZHALF = ['0000000000000000', '0000000000000000', '0000000000001000']
+S1Z = 'PVV'
+XFROM = [9, 99, 99]
 
 
 def _sb(shape, d):
@@ -261,7 +279,13 @@ def build():
     ts(r("PO"), r("IC"), col(18), A.mult, col(7), A.subtract)
     cp(r("OB"), r("BI"))
     ts(r("UW", None, (0, 1024)), r("IA"), 1024.0, A.add)
-    tt(r("PW", (0, 1024)), r("PO"), r("MASK", (0, 1024)), A.add)
+    ts(r("IW"), r("J", (0, 136)), 8.0, A.is_equal)
+    I32 = r("IW", (8, 136))
+    act(mx(IB_), I32, F.Identity)
+    for h in range(2):
+        hs, x = (512 * h, 512 * h + 512), r("X%d" % h)
+        mm([(x, mx(IB_), r("MASK", hs)), (x, mx(IB_), r("PO", hs))])
+        act(r("PW", hs), x, F.Identity)
     cp(r("SND", 0), ind(r("UW", 0, (0, 1024)), r("OB")))
     cp(r("SND", 1), ind(r("UW", 1, (0, 1024)), r("OB")))
     ts(r("SND", 2), ind(r("PW", (0, 1024)), r("OB")), col(2), A.max)
@@ -278,14 +302,11 @@ def build():
     for t in range(3):
         ts(r("OA", t), r("OAI"), col(1), A.add, float(7 - t), A.add)
     ts(mx(BLK), r("S1"), col(0), A.add, 0.0, A.is_equal)
-    ts(r("IW"), r("J", (0, 136)), 8.0, A.is_equal)
     ts(r("WC"), r("J"), col(0), A.add, 15.0, A.is_equal)
-    I32 = r("IW", (8, 136))
-    act(mx(IB_), I32, F.Identity)
     act(mx(NI), I32, F.Identity, scale=-1.0)
     mkcol(3, [(8, 0.25), (9, -0.25)])
     mkcol(4, [(10, 0.25), (11, -0.25)])
-    mkcol(5, [(8, 32), (9, 32), (10, 32), (11, 32), (15, -128)])
+    mkcol(5, [(8, 32), (9, 32), (10, 32), (11, 32), (12, -32768), (15, 32640)])
     mkcol(6, [(12, 32768), (15, -23552)])
     mkcol(19, [(0, 1024), (1, -1)])
     mkcol(8, [(15, -BIG + (131072 if CMS else 0)), (14, 1)])
@@ -307,11 +328,11 @@ def build():
     iota(r("DUM"), [[-1, 128]], 1152, 0)
     for t in range(2):
         iota(r("VID", t), [[8, 128]], 7 - t - E, 0)
-    ts(r("DUMM"), r("DUM"), -1.0, A.add)
-    tt(r("DUMM"), r("DUMM"), r("DIAG"), A.mult)
+    tt(r("DUMM"), r("DUM"), r("DIAG"), A.mult)
     act(r("RS8"), r("MASK", (0, 512)), F.Identity, bias=1e9, scale=0.0)
     ms(r("RS16"), 1.0)
     ms(r("RS16", (0, 128, 16)), 0.0)
+    scan(r("MD"), r("RS16"), r("DUMM"), 0.0, A.mult, A.add)
     ms(r("MM", (0, 8)), 0.0)
     ms(r("QE"), 0.0)
     act(r("AE"), r("MASK", (0, 384)), F.Identity, scale=0.0)
@@ -358,9 +379,9 @@ def build():
             act(c["nz"], c["az"], F.Sign, bias=-0.5)
             if c.get("cx"):
                 act(c["az"], c["az"], F.Relu)
-        mm([(c["bc"], mx(MC), c["alive"]), (c["bc"], mx(ONC), c["nz"])])
+        mm(([] if c.get("cx") else [(c["bc"], mx(MC), c["alive"])]) + [(c["bc"], mx(ONC), c["nz"])])
         if c.get("cx"):
-            act(c["stay"], c["bc"], F.Sigmoid)
+            act(c["stay"], c["bc"], F.Sigmoid, bias=9216.0)
             mm([(c["bc"], mx(MCAP), c["stay"])])
             tt(c["aq"], c["az"], c["bc"], A.min)
         else:
@@ -397,9 +418,9 @@ def build():
         ts(r("ON"), x0(0, 64), float(E), A.add, 1024.0, A.min)
         tt(r("GM"), ind(LSW, r("ON")), r("MASK", (t, t + 1024)), A.mult)
         cp(r("U16"), act_ls)
-        ts(r("EV"), act_ls, 0.0, A.is_equal)
+        act(r("EV"), act_ls, F.Relu, bias=1.0)
         mm([(x1(0, 128), mx(TRI), r("EV"))])
-        ts(r("FV"), x1(0, 128), 1.0, A.is_equal)
+        act(r("FV"), x1(0, 128), F.Relu)
         mm([(x0(0, 64), r("WC", (15 - i, 143 - i)), r("GM", (i, 1024, 16))) for i in range(16)])
         ts(r("OX"), x0(0, 64), float(E), A.add, 1023.0, A.min)
         ts(r("OC"), x0(0, 64), float(E), A.add)
@@ -429,10 +450,19 @@ def build():
             mm([(X0, mx(DXN if neg else DXP), r("D1"))])
             mm([(X1, mx(DYN if neg else DYP), r("D1"))])
             tt(r("DS", 0), r("DS", 0), X0, A.mult)
-            tt(r("DS", 1), r("DS", 1), X1, A.mult)
-            mm([(X0, I32, r("DS", 0))], True, False)
-            mm([(X0, I32, r("DS", 1))], False, True)
-            act(r("DS", 0), X0, F.Abs)
+            if S1Z[t] == "V":
+                tt(X1, r("DS", 1), X1, A.mult)
+                tt(r("DS", 0), r("DS", 0), X1, A.add)
+                act(r("DS", 0), r("DS", 0), F.Abs)
+            elif S1Z[t] == "D":
+                tt(r("DS", 1), r("DS", 1), X1, A.mult)
+                dma("g", [(r("DS", 0), r("DS", 1))], acc=True)
+                act(r("DS", 0), r("DS", 0), F.Abs)
+            else:
+                tt(r("DS", 1), r("DS", 1), X1, A.mult)
+                mm([(X0, I32, r("DS", 0))], True, False)
+                mm([(X0, I32, r("DS", 1))], False, True)
+                act(r("DS", 0), X0, F.Abs)
             if CMS:
                 mm([(X1, mx(NMT), r("D1")), (X1, I32, r("DS", 0))])
                 act(r("CM"), X1, F.Sign, bias=-0.5)
@@ -441,7 +471,7 @@ def build():
                 tt(r("CM"), r("DS", 0), X1, A.is_gt)
             mm([(X0, mx(BLK), gm), (X0, mx(KC), r("MASK", (0, 512))), (X0, mx(BD0 + t), r("D1")), (X0, mx(NBG), r("MB"))] +
                [(x0(k, 512, 8), mx(PBG), r("FV", (64 * h, 64 * h + 64))) for k in range(8)] + [(X0, mx(SCO), r("CM"))])
-            ts(r("RS8", (0, 512, 8)), r("DUM", (64 * h, 64 * h + 64)), 71.0 * 2048, A.add)
+            act(r("RS8", (0, 512, 8)), r("DUM", (64 * h, 64 * h + 64)), F.Identity, bias=71.0 * 2048)
             scan(r("DS", 1), r("RS8"), X0, 1e9, A.min, A.max)
             cp(r("KI", (64 * h, 64 * h + 64)), r("DS", 1, (7, 512, 8)))
         ts(r("NM"), r("KI"), 2047, A.bitwise_and)
@@ -452,7 +482,7 @@ def build():
         ts(r("EV"), ind(LSW, r("OM")), 0.0, A.is_equal)
         mm([(x1(0, 128), mx(TRI), r("EV"))])
         tt(r("MM", (1, 128)), r("NF", (1, 128)), r("SCN", (0, 127)), A.is_equal)
-        ts(r("MM", (128, 256)), r("NF"), 1025.0, A.is_ge)
+        act(r("MM", (128, 256)), r("NF"), F.Relu, bias=-1024.0)
         terms = [(x0(0, 128), mx(NON), r("MM", (0, 128))), (x0(0, 128), mx(NON), r("MM", (128, 256)))]
         at = 256
         for j in range(7):
@@ -460,21 +490,20 @@ def build():
             ts(r("MM", (at, at + 128 - a)), r("NF", (a, 128)), r("SCN", (a - 1, a)), A.is_equal)
             terms.append((x0(a, 128), mx(NON), r("MM", (at, at + 128 - a))))
             at += 128 - a
-        ts(r("FC"), x1(0, 128), 1.0, A.is_equal)
-        tt(r("DF"), r("NF"), r("DUM"), A.subtract)
-        tt(r("DF"), r("DF"), r("DIAG"), A.mult)
+        act(r("FC"), x1(0, 128), F.Relu)
+        tt(r("DF"), r("S1"), r("DUMM"), A.subtract)
         mm(terms + [(x0(0, 128), mx(BLK), r("FC"))])
-        ts(r("MD"), x0(0, 128), 1.0, A.is_equal)
-        ts(r("SE", (128 * t, 128 * t + 128)), x0(0, 128), 1.0, A.is_equal, oh(15), A.max)
-        tt(r("S2"), r("MD"), r("DF"), A.mult)
-        tt(r("S2"), r("S2"), r("DUMM"), A.add)
+        act(x0(0, 128), x0(0, 128), F.Relu)
+        tt(r("S2"), r("DF"), x0(0, 128), A.mult)
+        act(r("SE", (128 * t, 128 * t + 128)), x0(0, 128), F.Identity, bias=oh(15), scale=col(12))
         scan(r("SC2"), r("RS16"), r("S2"), 0.0, A.mult, A.add)
-        cp(r("OT", t), r("SC2", (15, 128, 16)))
+        tt(r("S2", (0, 8)), r("SC2", (15, 128, 16)), r("MD", (15, 128, 16)), A.add)
+        ts(r("OT", t), r("S2", (0, 8)), -1.0, A.add)
         de = r("DE", (128 * t, 128 * t + 128))
         tt(de, ind(r("PW"), r("OT", t)), r("PO", (rho, 1024, 8)), A.subtract)
         act(de, de, F.Square)
         if t < 2:
-            ts(r("S1"), r("NF"), -1.0 - E, A.add)
+            act(r("S1"), r("NF"), F.Identity, bias=-1.0 - E)
             tt(r("OVV", t), r("S1"), r("FV"), A.mult)
             tt(r("OVC", t), r("VID", t), r("FC"), A.mult)
 
@@ -516,7 +545,10 @@ def build():
                 cp(ind(r("LS"), r("OT", b)), r("E3"))
 
     def rows_update(t):
-        tt(r("LS", (0, 1024)), r("LS", (0, 1024)), r("SL"), A.mult)
+        for h, x in enumerate((X0, X1)):
+            hs = (512 * h, 512 * h + 512)
+            mm([(x, mx(IB_), r("SL", hs))])
+            tt(r("LS", hs), r("LS", hs), x, A.mult)
         for b in range(t + 1):
             se = r("SE", (128 * b, 128 * b + 128))
             own = r("LS", (7 - b, 1024, 8))
@@ -577,6 +609,10 @@ def build():
             if DMODE[j] == "V":
                 tt(dd, ind(r("PW"), o), po, A.subtract)
                 act(dd, dd, F.Square)
+            elif DMODE[j] == "D":
+                act(dd, ind(r("PW"), o), F.Identity, scale=-1.0)
+                dma("g", [(dd, po)], acc=True)
+                act(dd, dd, F.Square)
             else:
                 act(dd, ind(r("PW"), o), F.Identity)
                 mm([(bank(BT), mx(IB_), dd), (bank(BT), mx(NI), po)])
@@ -596,13 +632,26 @@ def build():
                     tt(r("WACC", hs), r("WACC", hs), c["bw"], A.add)
                     dma("s", [(hbm("yw", slice(None), slice(*hs)), r("WACC", hs))])
             if k == 7:
+                both = FIN3[h] == "1" and c["px"]["name"] == c["py"]["name"]
+                if both:
+                    s = r("SACC", None, hs)
+                    tt(s, s, r("DXY"), A.add)
+                    ts(s, s, 1.0, A.max, 2047.0, A.min)
                 for cc in range(2):
                     s = r("SACC", cc, hs)
-                    tt(s, s, c[("px", "py")[cc]], A.add)
-                    ts(s, s, 1.0, A.max, 2047.0, A.min)
+                    how = RNDS[2 * h + cc]
+                    if not both:
+                        tt(s, s, c[("px", "py")[cc]], A.add)
+                        if how != "S":
+                            ts(s, s, 1.0, A.max, 2047.0, A.min)
                     out = r("UW", cc, hs) if t < 2 else s
                     back = RND if t < 2 else RND + 1024.0
-                    if RNDS[cc] == "v":
+                    if how == "S" and not both:
+                        act(s, s, F.Relu, bias=-1.0)
+                        act(s, s, F.Relu, bias=2046.0, scale=-1.0)
+                        act(s, s, F.Identity, bias=RND + 2047.0, scale=-1.0)
+                        act(out, s, F.Identity, bias=-back)
+                    elif how == "v":
                         ts(out, s, RND, A.add, back, A.subtract)
                     else:
                         act(s, s, F.Identity, bias=RND)
@@ -635,7 +684,7 @@ def build():
             fetch(j)
         if t == 0:
             pre(0)
-        for j in range(16 + CSKEW):
+        for j in range(16 + max(CSKEW, BSKEW)):
             if j < 16:
                 if j >= 1 and j + 2 < 16 and j + 2 > 2:
                     fetch(j + 2)
@@ -699,6 +748,55 @@ def arrange(ops):
     for i in range(n):
         z = (z * 1103515245 + 12345) % 2147483648
         level[i] += JIT * (z / 2147483648.0)
+    best = None
+    for it in range(PASSES + 1):
+        order = forward(ops, succ, level)
+        span = max(o["t1"] for o in ops)
+        if best is None or span < best[0]:
+            best = (span, order, [(o["t0"], o["t1"]) for o in ops])
+        if it < PASSES:
+            level = backward(ops, succ, tail)
+    for o, (a, b) in zip(ops, best[2]):
+        o["t0"], o["t1"] = a, b
+    return best[1]
+
+
+def backward(ops, succ, tail):
+    n = len(ops)
+    left = [len(s) for s in succ]
+    ready = {e: [] for e in "vspgyx"}
+    at = [tail(o) for o in ops]
+    for i, o in enumerate(ops):
+        if not left[i]:
+            ready[o["eng"]].append(i)
+    free = {e: 0.0 for e in "vspgyx"}
+    out = [0.0] * n
+    for step in range(n):
+        best = None
+        for e, lst in ready.items():
+            if not lst:
+                continue
+            s = min(max(free[e], at[i]) for i in lst)
+            i = max((i for i in lst if max(free[e], at[i]) <= s + LOOK), key=lambda q: ops[q]["t1"])
+            s = max(free[e], at[i])
+            if best is None or s < best[0]:
+                best = (s, i)
+        s, i = best
+        o = ops[i]
+        ready[o["eng"]].remove(i)
+        out[i] = s + o["cost"]
+        if o["kind"] != "recv":
+            free[o["eng"]] = out[i]
+        for j in o["dep"]:
+            at[j] = max(at[j], out[i] + 0.1 + tail(ops[j]))
+            left[j] -= 1
+            if not left[j]:
+                ready[ops[j]["eng"]].append(j)
+    return out
+
+
+def forward(ops, succ, level):
+    n = len(ops)
     left = [len(o["dep"]) for o in ops]
     ready = {e: [] for e in "vspgyx"}
     at = [0.0] * n
@@ -709,13 +807,21 @@ def arrange(ops):
     free = {e: 0.0 for e in "vspgyx"}
     pipe = [0.0]
     order = []
+    hold = [None]
+    feeds = {i: [j for j in o["dep"]] for i, o in enumerate(ops) if o["kind"] == "send" and o["args"][2] in (3, 6)}
     while len(order) < n:
+        hold[0] = None
+        for i, d in feeds.items():
+            if 0 < left[i] <= 2 and all(left[j] == 0 for j in d):
+                hold[0] = [max(d, key=lambda q: at[q])]
         best = None
         for e, lst in ready.items():
             if not lst:
                 continue
             s = min(max(free[e], at[i]) for i in lst)
-            i = max((i for i in lst if max(free[e], at[i]) <= s + 0.05), key=lambda q: level[q] + ops[q]["up"])
+            i = max((i for i in lst if max(free[e], at[i]) <= s + LOOK), key=lambda q: level[q] + ops[q]["up"])
+            if e == "g" and ops[i]["kind"] == "dma" and hold[0] and at[hold[0][0]] <= s + GLOOK:
+                continue
             s = max(free[e], at[i])
             if best is None or s < best[0]:
                 best = (s, i)
@@ -765,6 +871,10 @@ def rank_program(g, core, T, topo):
     count = {e: 0 for e in queue}
     waited, top, token, clock = {}, {}, {}, {}
     nd = [0]
+    user, succ = {}, [[] for o in ops]
+    for i, o in enumerate(ops):
+        for j in o["dep"]:
+            succ[j].append(i)
 
     def wait(e, s, v):
         queue[e].wait_ge(T.sem[s], v)
@@ -796,12 +906,22 @@ def rank_program(g, core, T, topo):
                     kn[s2] = v2
         q = queue[e]
         if kind == "dma":
-            s = "d%d" % nd[0]
-            nd[0] += 1
+            s = None
+            if nd[0] >= NDS:
+                for s2, j in user.items():
+                    if (ops[j]["eng"] == "g") == (e == "g") and kn.get(s2, 0) >= top[s2] and \
+                            all(x in token and kn.get(token[x][0], 0) >= token[x][1] for x in succ[j]):
+                        s = s2
+                        break
+            else:
+                s = "d%d" % nd[0]
+                nd[0] += 1
+            user.pop(s, None)
+            user[s] = i
             for out, src in a[0]:
                 kw = {"accum_op": A.add} if a[1] else {}
                 q.dma_start(_ap(T, out), _ap(T, src), **kw).then_inc(T.sem[s], 16)
-            token[i] = (s, 16 * len(a[0]))
+            token[i] = (s, top.get(s, 0) + 16 * len(a[0]))
         elif kind == "send":
             trs, tot = [], 0
             for d in range(n - 1):

@@ -7,56 +7,25 @@ f32, b16, h16, i32, u16 = "float32", "bfloat16", "float16", "int32", "uint16"
 E = 1792
 BIG = float(2 ** 20)
 RND = float(3 * 2 ** 22)
-GMODE = ["V" + "S" * 15] * 3
-DMODE = "V" * 16
-BOOST = [20.0, 20.0, 20.0]
-XK = [4, 4, 4]
-S1MODE = "S"
-CSKEW = 2
-CFIRST = True
-HK = 6
-ZB = ("Z0", "Z1")
-BT = "TB"
-BSKEW = 1
-SMODE = "Z"
-MBS = True
-CMS = True
-SEED = 0
-JIT = 0.0
-BANKS = [(("TB", "CB", "D0"), ("X0", "X1", "TB"))] * 3
-XFROM = [99, 99, 99]
-AMODE = ["V" * 16] * 3
-CAPX = ["1" * 16] * 3
-ZHALF = ["0" * 16] * 3
-RNDS = "sssv"
-FIN3 = "11"
-LOOK = 0.05
-PASSES = 2
-S1Z = "DDD"
-GLOOK = 0.9
-GMODE = ['VVVSSSSSSSSSSSSS', 'VVVSVVSSSSSSSSVS', 'VVSSSSSSVSSSSSSS']
-CAPX = ['0100000000001100', '1000111111100101', '0000001011010011']
-AMODE = ['PPVVVVVVVPPVVVVV', 'PVVVVVVVVVVPPVVV', 'VVVVVVVVVVVVPPPV']
-DMODE = 'SVVVVVVVVSSVVVVS'
-BOOST = [0, 0, 0]
-XK = [5, 5, 5]
-HK = 5
-BANKS = [(('D0', 'D1', 'CB'), ('X0', 'X1', 'TB')), (('D0', 'D1', 'TB'), ('X0', 'X1', 'TB')), (('D0', 'D1', 'CB'), ('X0', 'X1', 'TB'))]
-CFIRST = False
-CMS = False
-GMODE = ['VVVSSSSSSSSSSSSS', 'VVSSSSSSSSSSSSSS', 'VVSSVSSSSSSSSSSS']
-CAPX = ['0000000111111000', '0000011000000000', '0000100010001001']
-AMODE = ['VVVVPVVVVVVVVVVV', 'VVVVVVVVVVVVVVVV', 'VVVVVVVVVPPVPPPP']
-DMODE = 'VVVDVVVDVDDDDVVD'
-XK = [4, 5, 5]
-HK = 6
-BANKS = [(('D0', 'D1', 'CB'), ('X0', 'X1', 'TB')), (('TB', 'D1', 'CB'), ('X0', 'X1', 'TB')), (('D0', 'D1', 'CB'), ('X0', 'X1', 'TB'))]
+GMODE = ["S" * 16] * 3
+DMODE = "S" * 8
+WMODE = "S" * 8
+EVAC = ["S" * 16] * 3
+TRB = [(("TR", "TR"), ("TR", "X0"))] * 3
+WTREE = "DDDP"
+EADD = ["D" * 8] * 3
+S1G = ["SS"] * 3
+CONV = "vvv"
+GMODE = ['FFSSSSSSSSSSSSSS', 'FFSSSSSSSSSSSSSS', 'FSSSSSSSSSSSSSSS']
+EADD = ['VDDDDDDD', 'DDDDDDDD', 'VDDDDDDD']
+S1G = ['VS', 'VV', 'VS']
+CONV = 'svs'
+S1Z = "PVV"
 MBS = False
-RNDS = 'SSvs'
-FIN3 = '01'
-ZHALF = ['0000000000000000', '0000000000000000', '0000000000001000']
-S1Z = 'PVV'
-XFROM = [9, 99, 99]
+CMS = False
+LOOK = 0.05
+GLOOK = 0.9
+PASSES = 2
 
 
 def _sb(shape, d):
@@ -64,76 +33,75 @@ def _sb(shape, d):
 
 
 SCRATCH = {
-    "DD": _sb([8192], b16), "Q": _sb([8192], h16), "AQ": _sb([8192], h16),
-    "AT0": _sb([1024], h16), "AT1": _sb([1024], h16), "ST0": _sb([1024], b16), "ST1": _sb([1024], b16),
-    "UW": _sb([2, 1800], f32), "PW": _sb([1800], b16), "PO": _sb([1024], b16), "WW": _sb([1800], f32),
-    "LS": _sb([1152], f32), "SACC": _sb([2, 1024], f32), "WACC": _sb([1024], f32), "XACC": _sb([2, 1152], f32),
-    "LDF": _sb([1024], f32), "SL": _sb([1024], b16), "LA0": _sb([9, 256], u16), "LA1": _sb([6, 256], u16),
-    "SND": _sb([3, 256], u16),
-    "IA": _sb([2, 1024], i32), "IC": _sb([1024], i32), "NBI": _sb([512], i32),
-    "BI": _sb([16], i32), "ONB": _sb([512], u16), "OB": _sb([16], u16),
-    "G0": _sb([2, 1024], f32), "G1": _sb([2, 1024], f32), "PB0": _sb([2, 1024], f32), "PB1": _sb([2, 1024], f32),
-    "WG0": _sb([1024], f32), "WG1": _sb([1024], f32),
-    "AZ0": _sb([512], f32), "AZ1": _sb([512], f32), "NZ0": _sb([512], b16), "NZ1": _sb([512], b16),
-    "TT0": _sb([512], h16), "TT1": _sb([512], h16), "SG0": _sb([512], b16), "SG1": _sb([512], b16),
+    "DD": _sb([4, 2048], h16), "QC": _sb([4, 2048], h16), "NZ": _sb([2, 1024], b16),
+    "QS": _sb([64, 3, 16], h16), "DM": _sb([2, 16, 512], h16), "AB": _sb([8, 4, 256], h16), "AT": _sb([16, 128], h16),
+    "G": _sb([2, 2, 1024], h16), "EE": _sb([2, 2, 1024], i32), "UR": _sb([2, 2, 1024], h16),
+    "UW": _sb([2, 1800], f32), "PW": _sb([1800], b16), "PO": _sb([1024], h16), "WW": _sb([1800], f32),
+    "LS": _sb([1152], f32), "XACC": _sb([2, 1152], f32), "BASE": _sb([2048], f32), "WB": _sb([2048], f32),
+    "SC": _sb([2, 4, 384], b16), "SS": _sb([4, 128], b16), "D2": _sb([1024], h16), "SD": _sb([256], h16),
+    "SEL": _sb([16, 128], b16), "LA0": _sb([6, 256], h16), "LA1": _sb([6, 256], h16), "SND": _sb([3, 256], h16),
+    "NBI": _sb([8, 4, 16], i32), "BI": _sb([16], i32), "ONB": _sb([512], u16), "OB": _sb([16], u16),
     "PI": _sb([8], i32), "CL": _sb([32], f32), "J": _sb([144], f32), "IW": _sb([136], f32), "WC": _sb([144], b16),
-    "MX": _sb([24, 128], b16), "DIAG": _sb([128], f32), "MASK": _sb([1032], b16), "RS8": _sb([512], f32),
+    "C2": _sb([136], b16), "W2": _sb([136], b16),
+    "MX": _sb([25, 128], b16), "DIAG": _sb([128], f32), "MASK": _sb([1032], b16), "RS8": _sb([512], f32),
     "RS16": _sb([128], f32), "DUM": _sb([128], f32), "DUMM": _sb([128], f32), "VID": _sb([2, 128], f32),
     "OAI": _sb([64], i32), "OA": _sb([3, 64], u16),
-    "UA": _sb([2, 512], f32), "DS": _sb([2, 512], f32), "GM": _sb([1024], h16), "D1": _sb([512], b16),
-    "MB": _sb([512], b16), "CM": _sb([512], b16), "KI": _sb([128], i32), "NM": _sb([128], i32),
+    "GM": _sb([1024], h16), "D1": _sb([512], h16), "MB": _sb([512], b16), "CM": _sb([512], h16),
     "NF": _sb([128], f32), "S1": _sb([128], f32), "SCN": _sb([128], f32), "S2": _sb([128], f32), "SC2": _sb([128], f32),
-    "U16": _sb([128], h16), "EV": _sb([128], b16), "FV": _sb([128], b16), "FC": _sb([128], b16), "MM": _sb([704], b16),
+    "U16": _sb([128], h16), "EV": _sb([128], b16), "FV": _sb([128], b16), "FC": _sb([128], b16),
     "MD": _sb([128], f32), "DF": _sb([128], f32), "ON": _sb([64], u16), "OC": _sb([64], u16), "OX": _sb([64], u16),
-    "OM": _sb([8], u16), "OT": _sb([3, 8], u16), "OVV": _sb([2, 128], f32), "OVC": _sb([2, 128], f32),
+    "OM": _sb([8], u16), "OT": _sb([3, 8], u16), "OVV": _sb([2, 128], h16), "OVC": _sb([2, 128], h16),
+    "UF": _sb([2, 256], f32),
     "DE": _sb([384], b16), "SE": _sb([384], b16), "QE": _sb([384], h16), "AE": _sb([384], f32),
-    "EX": _sb([384], f32), "EY": _sb([384], f32), "EZ": _sb([384], f32), "EN": _sb([384], b16), "ET": _sb([384], h16),
-    "EQ": _sb([384], h16), "E1": _sb([128], f32), "E2": _sb([128], f32), "E3": _sb([128], f32), "E4": _sb([128], f32),
 }
-if SMODE == "Z":
-    SCRATCH.pop("SG0")
-    SCRATCH.pop("SG1")
 SCRATCH["DXY"] = ("psum", [128, 2, 512], f32)
-for _n in ("Z0", "Z1", "TB", "CB", "X0", "X1"):
+for _n in ("UB", "LB", "TR", "X0", "X1"):
     SCRATCH[_n] = ("psum", [128, 512], f32)
+SCRATCH["CNT"] = ("psum", [128, 4, 128], f32)
 SIZE = {f32: 4, i32: 4, b16: 2, h16: 2, u16: 2}
 NDS = 130
 SEMAPHORES = ["cv", "cs", "cp", "cg"] + ["d%d" % i for i in range(NDS)] + \
     ["ar%d" % i for i in range(12)] + ["lo%d" % i for i in range(4)]
-(BLK, IB_, NI, DXP, DXN, DYP, DYN, PX_, PY_, MT, ONC, MC, SCO, NBG, PBG, NON, KC, TRI, BD0, BD1, BD2, MTMP, NMT,
- MCAP) = range(24)
+(BLK, IB_, NI, DXP, DXN, DYP, DYN, PX_, PY_, MT, ONC, MC, SCO, NBG, PBG, NON, KC, TRI, BD0, BD1, BD2, I16, NMT,
+ CX, CY) = range(25)
 
 
-def r(name, *ix, p=None):
+UNIT = {"WB": (0, 128), "BASE": (0, 128), "TR": (0, 128), "X0": (0, 128), "X1": (0, 128), "UB": (0, 128), "LB": (0, 128),
+        "DD": (1, 256), "QC": (1, 256), "NZ": (1, 256)}
+
+
+def r(name, *ix, p=None, raw=False):
     shape = SCRATCH[name][1][1:]
     ix = list(ix) + [None] * (len(shape) - len(ix))
-    lo = hi = 0
+    if name in UNIT and not raw:
+        d, u = UNIT[name]
+        if ix[d] is not None:
+            ix[d] = (u * ix[d], u * ix[d] + u) if isinstance(ix[d], int) else (u * ix[d][0], u * ix[d][1])
     n = 1
     out = []
-    for d, (x, w) in enumerate(zip(ix, shape)):
-        st = 1
-        for y in shape[d + 1:]:
-            st *= y
+    spans = [(0, 1)]
+    st = 1
+    for x, w in reversed(list(zip(ix, shape))):
         if isinstance(x, int):
-            lo += x * st
-            hi += x * st
+            a, c, s = x, 1, 1
             out.append(x)
-            continue
-        a, b, s = (0, w, 1) if x is None else (tuple(x) + (1,))[:3]
-        c = (b - a + s - 1) // s
-        lo += a * st
-        hi += (a + (c - 1) * s) * st
+        else:
+            a, b, s = (0, w, 1) if x is None else (tuple(x) + (1,))[:3]
+            c = (b - a + s - 1) // s
+            out.append(slice(a, b, s) if s != 1 else slice(a, b))
         n *= c
-        out.append(slice(a, b, s) if s != 1 else slice(a, b))
+        lo, hi = spans[0][0], spans[-1][1]
+        if st == 1 or c * len(spans) > 32 or (len(spans) == 1 and s == 1 and hi - lo == st):
+            spans = [(lo + a * st, hi + (a + (c - 1) * s) * st)]
+        else:
+            spans = [(u + (a + q * s) * st, v + (a + q * s) * st) for q in range(c) for u, v in spans]
+        st *= w
     ps = slice(None) if p is None else slice(*p)
+    if name == "DM":
+        spans = [(out[0], out[0] + 1) if isinstance(out[0], int) else (out[0].start, out[0].stop)]
     if SCRATCH[name][0] == "psum":
-        lo, hi = lo // 512 * 512, hi // 512 * 512 + 511
-    spans = [(lo, hi + 1)]
-    if len(shape) == 2 and isinstance(out[0], slice) and SCRATCH[name][0] != "psum":
-        rows = out[0].stop - out[0].start
-        wid = hi + 1 - lo - (rows - 1) * shape[1]
-        spans = [(lo + q * shape[1], lo + q * shape[1] + wid) for q in range(rows)]
-    return {"k": "b", "name": name, "ix": (ps,) + tuple(out), "spans": spans, "n": n}
+        spans = [(spans[0][0] // 512 * 512, (spans[-1][1] - 1) // 512 * 512 + 512)]
+    return {"k": "b", "name": name, "ix": (ps,) + tuple(reversed(out)), "spans": spans, "n": n}
 
 
 def ind(win, off):
@@ -178,7 +146,6 @@ def _ps(x):
 
 def build():
     ops = []
-    tag = [0.0]
 
     def add(eng, kind, args, outs, ins, cost, **kw):
         w, rd = [], []
@@ -188,7 +155,7 @@ def build():
             rd += q[1:]
         for o in ins:
             rd += _parts(o)
-        d = {"eng": eng, "kind": kind, "args": args, "w": w, "r": rd, "cost": cost, "up": tag[0]}
+        d = {"eng": eng, "kind": kind, "args": args, "w": w, "r": rd, "cost": cost}
         d.update(kw)
         ops.append(d)
         return len(ops) - 1
@@ -219,11 +186,17 @@ def build():
         add("s", "act", (out, a, fn, bias, scale), [out], [a, bias, scale],
             0.07 + max(64, out["n"] * (1.56 if a["k"] == "i" else 1)) * 0.00083)
 
+    def lin(who, out, a, scale, bias):
+        if who in "Ss":
+            act(out, a, F.Identity, bias=bias, scale=scale)
+        else:
+            ts(out, a, scale, A.mult, bias, A.add)
+
     def mm(terms, start=True, stop=True):
         c = 0.0
         ins = []
         for o, l, x in terms:
-            c += max(64, x["n"]) * (1 if _two(x) else 4) * 0.000417
+            c += max(min(64, l["n"]), x["n"]) * (1 if _two(x) else 4) * 0.000417
             ins += [l, x]
         add("p", "mm", (terms, start, stop), [terms[0][0]], ins, c + 0.02, cont=not start)
 
@@ -243,12 +216,21 @@ def build():
         for d in range(3):
             add("x", "recv", (base, d), [land[d]], [], 0.0, after=s)
 
-    dma("y", [(r("IA", 0), hbm("ux")), (r("BI"), hbm("bord"))])
-    dma("s", [(r("IA", 1), hbm("uy"))])
-    ms(r("IC"), 0)
+    def x0(a, b, s=1):
+        return r("X0", (a, b, s), raw=True)
+
+    def x1(a, b, s=1):
+        return r("X1", (a, b, s), raw=True)
+
+    X0, X1 = r("X0"), r("X1")
+    IC = r("EE", 1, 0)
+
+    dma("y", [(r("EE", 0, 0), hbm("ux")), (r("BI"), hbm("bord"))])
+    dma("s", [(r("EE", 0, 1), hbm("uy"))])
+    ms(IC, 0)
     dma("s", [(r("NBI"), hbm("nb"))])
-    dma("y", [(r("IC", p=(8 + j, 128, 16)), hbm("px" if j < 2 else "py")) for j in range(4)] +
-        [(r("IC", p=(k, 128, 16)), hbm("nb", slice(None), slice(64 * k, 64 * k + 64))) for k in range(8)], nb=800000)
+    dma("y", [(r("EE", 1, 0, p=(8 + j, 128, 16)), hbm("px" if j < 2 else "py")) for j in range(4)] +
+        [(r("EE", 1, 0, p=(k, 128, 16)), hbm("nb", slice(None), slice(64 * k, 64 * k + 64))) for k in range(8)], nb=800000)
     iota(r("PI", (0, 1)), [[0, 1]], 0, 1)
     iota(r("J"), [[1, 144]], 0, -1)
     iota(r("DIAG"), [[0, 8], [1, 16]], 0, 0)
@@ -276,9 +258,9 @@ def build():
     tt(col(15), col(7), oh(12), A.add)
     ts(col(18), col(0), 8.0, A.is_ge)
     ts(r("MASK"), r("MASK"), col(0), A.is_equal, col(15), A.add)
-    ts(r("PO"), r("IC"), col(18), A.mult, col(7), A.subtract)
+    ts(r("PO"), IC, col(18), A.mult, col(7), A.subtract)
     cp(r("OB"), r("BI"))
-    ts(r("UW", None, (0, 1024)), r("IA"), 1024.0, A.add)
+    ts(r("UW", None, (0, 1024)), r("EE", 0), RND, A.add)
     ts(r("IW"), r("J", (0, 136)), 8.0, A.is_equal)
     I32 = r("IW", (8, 136))
     act(mx(IB_), I32, F.Identity)
@@ -286,18 +268,23 @@ def build():
         hs, x = (512 * h, 512 * h + 512), r("X%d" % h)
         mm([(x, mx(IB_), r("MASK", hs)), (x, mx(IB_), r("PO", hs))])
         act(r("PW", hs), x, F.Identity)
-    cp(r("SND", 0), ind(r("UW", 0, (0, 1024)), r("OB")))
-    cp(r("SND", 1), ind(r("UW", 1, (0, 1024)), r("OB")))
+
+    def border():
+        for c in range(2):
+            ts(r("SND", c), ind(r("UW", c, (0, 1024)), r("OB")), -RND, A.add)
+    border()
     ts(r("SND", 2), ind(r("PW", (0, 1024)), r("OB")), col(2), A.max)
-    send(r("SND"), [r("LA0", (3 * d, 3 * d + 3)) for d in range(3)], 0)
-    cp(r("ONB"), r("NBI"))
-    ms(r("UW", None, (1792, 1800)), 0.0)
+    send(r("SND"), [r("AB", d, (0, 3)) for d in range(3)], 0)
+    for q in range(4):
+        cp(r("ONB", (128 * q, 128 * q + 128)), r("NBI", None, q))
+    dma("y", [(r("AB", (4, 8), k), r("PO")) for k in range(4)])
+    ms(r("UW", None, (1792, 1800)), RND)
     ms(r("WW", (1792, 1800)), 0.0)
     ts(r("PW", (1792, 1800)), r("MASK", (0, 8)), 0.0, A.mult, col(2), A.add)
     ms(r("LS", (1024, 1152)), 0.0)
     ts(r("OAI"), r("OAI"), 1023, A.bitwise_and)
     cp(r("ON"), r("OAI"))
-    ts(r("LS", (0, 1024)), ind(r("IC"), r("ON")), float(E), A.subtract, col(2), A.mult)
+    ts(r("LS", (0, 1024)), ind(IC, r("ON")), float(E), A.subtract, col(2), A.mult)
     iota(r("OAI"), [[16, 64]], 0, 0)
     for t in range(3):
         ts(r("OA", t), r("OAI"), col(1), A.add, float(7 - t), A.add)
@@ -308,7 +295,6 @@ def build():
     mkcol(4, [(10, 0.25), (11, -0.25)])
     mkcol(5, [(8, 32), (9, 32), (10, 32), (11, 32), (12, -32768), (15, 32640)])
     mkcol(6, [(12, 32768), (15, -23552)])
-    mkcol(19, [(0, 1024), (1, -1)])
     mkcol(8, [(15, -BIG + (131072 if CMS else 0)), (14, 1)])
     for t in range(3):
         mkcol(9 + t, [(7 - t, -BIG)], first=col(8))
@@ -316,15 +302,22 @@ def build():
     mkcol(13, [(15, 200)])
     ts(col(14), col(0), -2048.0, A.mult, 16128.0, A.add)
     tt(col(14), col(14), col(2), A.mult)
-    for m, c in ((DXP, 3), (DYP, 4), (MT, 5), (MC, 6), (KC, 14), (BD0, 9), (BD1, 10), (BD2, 11), (MCAP, 19)):
+    act(col(19), col(2), F.Identity, scale=-32.0)
+    act(col(20), col(18), F.Identity, scale=-32.0)
+    for m, c in ((DXP, 3), (DYP, 4), (MT, 5), (MC, 6), (KC, 14), (BD0, 9), (BD1, 10), (BD2, 11), (CX, 19), (CY, 20)):
         act(mx(m), mx(BLK), F.Identity, scale=col(c))
     for m, s, v in ((DXN, DXP, -1.0), (DYN, DYP, -1.0), (PX_, DXP, 1 / 32), (PY_, DYP, 1 / 32), (ONC, BLK, 1024.0),
                     (SCO, BLK, 8192.0 if CMS else 16384.0), (NBG, BLK, -BIG), (PBG, BLK, BIG), (NON, BLK, -1.0), (NMT, MT, -1.0)):
         act(mx(m), mx(s), F.Identity, scale=v)
-    ts(mx(MTMP), r("J", (0, 128)), 0.0, A.is_gt, -2.0, A.mult)
-    tt(mx(MTMP), mx(MTMP), I32, A.add)
-    tt(mx(MTMP), mx(MTMP), mx(BLK), A.mult)
-    ts(mx(TRI), mx(MTMP), col(2), A.mult)
+    ts(mx(I16), r("J", (0, 128)), 0.0, A.is_gt, -2.0, A.mult)
+    tt(mx(I16), mx(I16), I32, A.add)
+    tt(mx(I16), mx(I16), mx(BLK), A.mult)
+    ts(mx(TRI), mx(I16), col(2), A.mult)
+    act(mx(I16), I32, F.Identity, scale=16.0)
+    act(r("W2"), r("WC", (8, 144)), F.Identity, scale=col(3))
+    act(r("C2"), r("WC", (0, 136)), F.Identity, scale=col(4))
+    tt(r("W2"), r("W2"), r("C2"), A.add)
+    tt(r("C2"), r("WC", (0, 136)), r("WC", (8, 144)), A.add)
     iota(r("DUM"), [[-1, 128]], 1152, 0)
     for t in range(2):
         iota(r("VID", t), [[8, 128]], 7 - t - E, 0)
@@ -333,82 +326,32 @@ def build():
     ms(r("RS16"), 1.0)
     ms(r("RS16", (0, 128, 16)), 0.0)
     scan(r("MD"), r("RS16"), r("DUMM"), 0.0, A.mult, A.add)
-    ms(r("MM", (0, 8)), 0.0)
     ms(r("QE"), 0.0)
     act(r("AE"), r("MASK", (0, 384)), F.Identity, scale=0.0)
-    act(r("SL"), r("MASK", (0, 1024)), F.Identity, scale=0.0)
     ms(r("XACC", None, (1024, 1152)), 0.0)
-    dma("y", [(r("IA", 0), hbm("ld"))])
+    dma("y", [(r("EE", 1, 1), hbm("ld"))])
     dma("y", [(r("WW", (0, 1024)), hbm("wt"))])
-    ts(r("LDF"), r("IA", 0), 0.5, A.add, 1 / 32, A.mult)
+    ts(r("BASE", (8, 16)), r("EE", 1, 1), 0.5, A.add, 1 / 32, A.mult)
+    act(r("BASE", (0, 8)), r("MASK", (0, 1024)), F.Identity, bias=1 / 64, scale=0.0)
+    iota(r("SEL"), [[1, 16], [16, 8], [0, 16]], 0, -1)
+    ts(r("SEL"), r("SEL"), 0.0, A.is_equal, 2048.0, A.mult)
+    ms(r("QS", None, 1), 0.0)
+    ms(r("DM", 0, (0, 4)), 0.0)
+    dma("y", [(r("DM", z // 4, (4 * (z % 4), 4 * (z % 4) + 4)), r("DM", 0, (0, 4))) for z in range(1, 8)])
 
     def convert(t):
         for d in range(3):
-            la, b = (("LA0", 3 * d), ("LA1", 2 * d), ("LA0", 2 * d))[t]
-            cp(r("UW", None, (1024 + 256 * d, 1280 + 256 * d)), r(la, (b, b + 2)))
+            la = r(("LA1", "LA0")[t - 1], (2 * d, 2 * d + 2)) if t else r("AB", d, (0, 2))
+            lin(CONV[d], r("UW", None, (1024 + 256 * d, 1280 + 256 * d)), la, 1.0, RND)
             if t == 0:
-                cp(r("PW", (1024 + 256 * d, 1280 + 256 * d)), r(la, b + 2))
+                cp(r("PW", (1024 + 256 * d, 1280 + 256 * d)), r("AB", d, 2))
     convert(0)
 
-    def stage_a(c):
-        mm([(c["bx"], mx(DXN if c["neg"] else DXP), c["dd"])])
-        mm([(c["by"], mx(DYN if c["neg"] else DYP), c["dd"])])
-        if "gxy" in c:
-            tt(c["gxy"], c["gxy"], r("DXY"), A.mult)
-        else:
-            tt(c["gx"], c["gx"], c["bx"], A.mult)
-            tt(c["gy"], c["gy"], c["by"], A.mult)
-        last = [(c["bz"], mx(IB_), c["q"])] if c["hasq"] else []
-        if c.get("zh"):
-            dma("g", [(c["gx"], c["gy"])], acc=True)
-            mm(last + [(c["bz"], I32, c["gx"])])
-        else:
-            mm(last + [(c["bz"], I32, c["gx"])], True, False)
-            mm([(c["bz"], I32, c["gy"])], False, True)
+    def ua(c=None):
+        return r("WB", (0, 8)) if c is None else r("WB", (4 * c, 4 * c + 4))
 
-    def stage_b(c):
-        act(c["az"], c["bz"], F.Abs)
-        act(c.get("sg") or c["bz"], c["bz"], F.Sign)
-        if c.get("am") == "P":
-            mm([(c["bt"], mx(NMT), c["dd"]), (c["bt"], I32, c["az"])])
-            act(c["az"], c["bt"], F.Relu)
-            act(c["nz"], c["az"], F.Sign, bias=-0.5)
-        else:
-            mm([(c["bt"], mx(MT), c["dd"])])
-            tt(c["az"], c["az"], c["bt"], A.subtract)
-            act(c["nz"], c["az"], F.Sign, bias=-0.5)
-            if c.get("cx"):
-                act(c["az"], c["az"], F.Relu)
-        mm(([] if c.get("cx") else [(c["bc"], mx(MC), c["alive"])]) + [(c["bc"], mx(ONC), c["nz"])])
-        if c.get("cx"):
-            act(c["stay"], c["bc"], F.Sigmoid, bias=9216.0)
-            mm([(c["bc"], mx(MCAP), c["stay"])])
-            tt(c["aq"], c["az"], c["bc"], A.min)
-        else:
-            tt(c["tt"], c["az"], c["bc"], A.min)
-            ts(c["aq"], c["tt"], 0.0, A.max, 1023.0, A.min)
-        if c.get("bs"):
-            mm([(c["bs"], mx(IB_), c["sg"])])
-        tt(c["q"], c["aq"], c.get("bs") or c.get("sg") or c["bz"], A.mult)
-        if c["stay"] is not None and not c.get("cx"):
-            act(c["stay"], c["bc"], F.Sigmoid, bias=c["sb"], scale=c["ss"])
-
-    def stage_c(c):
-        mm([(c["cx_"], mx(PX_), c["dd"])])
-        tt(c["px"], c["q"], c["cx_"], A.mult)
-        mm([(c["cy_"], mx(PY_), c["dd"])])
-        tt(c["py"], c["q"], c["cy_"], A.mult)
-
-    X0, X1 = r("X0"), r("X1")
-
-    def bank(x):
-        return r("DXY", int(x[1])) if x[0] == "D" else r(x)
-
-    def x0(a, b, s=1):
-        return r("X0", (a, b, s))
-
-    def x1(a, b, s=1):
-        return r("X1", (a, b, s))
+    def ds(c=None):
+        return r("WB", (8, 16)) if c is None else r("WB", (8 + 4 * c, 12 + 4 * c))
 
     def step1(t):
         rho = 7 - t
@@ -427,14 +370,15 @@ def build():
         for h in range(2):
             o = (32 * h, 32 * h + 32)
             for c in range(2):
-                act(r("UA", c), ind(r("UW", c, (0, 1024)), r("OA", t, o)), F.Identity)
+                act(ua(c), ind(r("UW", c, (0, 1024)), r("OA", t, o)), F.Identity)
+            neg = S1G[t][h] == "S"
             for c in range(2):
-                if S1MODE == "S":
-                    act(r("DS", c), ind(r("UW", c, (0, 1024)), r("OX", o)), F.Identity, scale=-1.0)
+                if neg:
+                    act(ds(c), ind(r("UW", c, (0, 1024)), r("OX", o)), F.Identity, scale=-1.0)
                 else:
-                    tt(r("DS", c), ind(r("UW", c, (0, 1024)), r("OX", o)), r("UA", c), A.subtract)
-            if S1MODE == "S":
-                dma("g", [(r("DS"), r("UA"))], acc=True)
+                    tt(ds(c), ind(r("UW", c, (0, 1024)), r("OX", o)), ua(c), A.subtract)
+            if neg:
+                dma("g", [(ds(), ua())], acc=True)
             act(r("D1"), ind(r("PW"), r("OC", o)), F.Identity)
             gm = r("GM", (512 * h, 512 * h + 512))
             mm([(X1, mx(BLK), gm)] + [(x1(k, 512, 8), mx(NI), r("U16", (64 * h, 64 * h + 64))) for k in range(8)])
@@ -446,49 +390,50 @@ def build():
             mm([(X0, mx(IB_), r("D1"))] +
                [(x0(k, 512, 8), mx(NI), r("PO", (512 * h + rho, 512 * h + 512, 8))) for k in range(8)])
             act(r("D1"), X0, F.Square)
-            neg = S1MODE == "S"
             mm([(X0, mx(DXN if neg else DXP), r("D1"))])
             mm([(X1, mx(DYN if neg else DYP), r("D1"))])
-            tt(r("DS", 0), r("DS", 0), X0, A.mult)
+            tt(ds(0), ds(0), X0, A.mult)
             if S1Z[t] == "V":
-                tt(X1, r("DS", 1), X1, A.mult)
-                tt(r("DS", 0), r("DS", 0), X1, A.add)
-                act(r("DS", 0), r("DS", 0), F.Abs)
+                tt(X1, ds(1), X1, A.mult)
+                tt(ds(0), ds(0), X1, A.add)
+                act(ds(0), ds(0), F.Abs)
             elif S1Z[t] == "D":
-                tt(r("DS", 1), r("DS", 1), X1, A.mult)
-                dma("g", [(r("DS", 0), r("DS", 1))], acc=True)
-                act(r("DS", 0), r("DS", 0), F.Abs)
+                tt(ds(1), ds(1), X1, A.mult)
+                dma("g", [(ds(0), ds(1))], acc=True)
+                act(ds(0), ds(0), F.Abs)
             else:
-                tt(r("DS", 1), r("DS", 1), X1, A.mult)
-                mm([(X0, I32, r("DS", 0))], True, False)
-                mm([(X0, I32, r("DS", 1))], False, True)
-                act(r("DS", 0), X0, F.Abs)
+                tt(ds(1), ds(1), X1, A.mult)
+                mm([(X0, I32, ds(0))], True, False)
+                mm([(X0, I32, ds(1))], False, True)
+                act(ds(0), X0, F.Abs)
             if CMS:
-                mm([(X1, mx(NMT), r("D1")), (X1, I32, r("DS", 0))])
+                mm([(X1, mx(NMT), r("D1")), (X1, I32, ds(0))])
                 act(r("CM"), X1, F.Sign, bias=-0.5)
             else:
                 mm([(X1, mx(MT), r("D1"))])
-                tt(r("CM"), r("DS", 0), X1, A.is_gt)
+                tt(r("CM"), ds(0), X1, A.is_gt)
             mm([(X0, mx(BLK), gm), (X0, mx(KC), r("MASK", (0, 512))), (X0, mx(BD0 + t), r("D1")), (X0, mx(NBG), r("MB"))] +
                [(x0(k, 512, 8), mx(PBG), r("FV", (64 * h, 64 * h + 64))) for k in range(8)] + [(X0, mx(SCO), r("CM"))])
             act(r("RS8", (0, 512, 8)), r("DUM", (64 * h, 64 * h + 64)), F.Identity, bias=71.0 * 2048)
-            scan(r("DS", 1), r("RS8"), X0, 1e9, A.min, A.max)
-            cp(r("KI", (64 * h, 64 * h + 64)), r("DS", 1, (7, 512, 8)))
-        ts(r("NM"), r("KI"), 2047, A.bitwise_and)
-        tt(r("S1"), r("NM"), r("DIAG"), A.mult)
-        cp(r("NF"), r("NM"))
+            scan(ds(1), r("RS8"), X0, 1e9, A.min, A.max)
+            cp(r("NBI", h), r("WB", (1543, 2048, 8), raw=True))
+        nm = r("NBI", (2, 4))
+        ts(nm, r("NBI", (0, 2)), 2047, A.bitwise_and)
+        tt(r("S1"), nm, r("DIAG"), A.mult)
+        cp(r("NF"), nm)
         scan(r("SCN"), r("RS16"), r("S1"), 0.0, A.mult, A.add)
         ts(r("OM"), r("SCN", (15, 128, 16)), -1.0, A.add)
         ts(r("EV"), ind(LSW, r("OM")), 0.0, A.is_equal)
         mm([(x1(0, 128), mx(TRI), r("EV"))])
-        tt(r("MM", (1, 128)), r("NF", (1, 128)), r("SCN", (0, 127)), A.is_equal)
-        act(r("MM", (128, 256)), r("NF"), F.Relu, bias=-1024.0)
-        terms = [(x0(0, 128), mx(NON), r("MM", (0, 128))), (x0(0, 128), mx(NON), r("MM", (128, 256)))]
+        ms(r("GM", (0, 1)), 0.0)
+        tt(r("GM", (1, 128)), r("NF", (1, 128)), r("SCN", (0, 127)), A.is_equal)
+        act(r("GM", (128, 256)), r("NF"), F.Relu, bias=-1024.0)
+        terms = [(x0(0, 128), mx(NON), r("GM", (0, 128))), (x0(0, 128), mx(NON), r("GM", (128, 256)))]
         at = 256
         for j in range(7):
             a = 16 * (j + 1)
-            ts(r("MM", (at, at + 128 - a)), r("NF", (a, 128)), r("SCN", (a - 1, a)), A.is_equal)
-            terms.append((x0(a, 128), mx(NON), r("MM", (at, at + 128 - a))))
+            ts(r("GM", (at, at + 128 - a)), r("NF", (a, 128)), r("SCN", (a - 1, a)), A.is_equal)
+            terms.append((x0(a, 128), mx(NON), r("GM", (at, at + 128 - a))))
             at += 128 - a
         act(r("FC"), x1(0, 128), F.Relu)
         tt(r("DF"), r("S1"), r("DUMM"), A.subtract)
@@ -508,198 +453,231 @@ def build():
             tt(r("OVC", t), r("VID", t), r("FC"), A.mult)
 
     def extras(t):
-        w = (0, 128 * (t + 1))
-        act(r("XACC", 0, (0, 1024)), r("LDF"), F.Identity, bias=1 / 64, scale=0.0)
-        act(r("XACC", 1, (0, 1024)), r("LDF"), F.Identity)
-        dma("g", [(r("XACC", None, (0, 1024)), r("UW", None, (0, 1024)))], acc=True)
-        for b in range(t + 1):
-            for c, n in ((0, "EX"), (1, "EY")):
-                e = r(n, (128 * b, 128 * b + 128))
+        n = t + 1
+        w = (0, 128 * n)
+        dma("y", [(r("XACC", None, (0, 1024)), r("BASE"))])
+        ex, ey, ez = r("WB", (0, n)), r("WB", (4, 4 + n)), r("WB", (8, 8 + n))
+        bx, by = x0(*w), x1(*w)
+        de, se, qe, en, et, eq = [r(x, w) for x in ("DE", "SE", "QE", "MB", "D1", "CM")]
+        for b in range(n):
+            for c in range(2):
+                e = r("WB", 4 * c + b)
                 act(e, r("UW", c, (7 - b, 1024, 8)), F.Identity)
                 tt(e, ind(r("UW", c, (0, 1152)), r("OT", b)), e, A.subtract)
-        c = {"bx": r("X0", w), "by": r("X1", w), "bz": r("X0", w), "bt": r("X1", w), "bc": r("X1", w), "neg": False,
-             "cx_": r("X0", w), "cy_": r("X1", w),
-             "dd": r("DE", w), "gx": r("EX", w), "gy": r("EY", w), "q": r("QE", w), "hasq": True, "az": r("EZ", w),
-             "nz": r("EN", w), "alive": r("SE", w), "tt": r("ET", w), "aq": r("EQ", w),
-             "stay": r("SE", w) if t < 2 else None, "sb": col(13), "ss": col(12), "px": r("EX", w), "py": r("EY", w)}
-        stage_a(c)
-        stage_b(c)
-        stage_c(c)
-        tt(r("AE", w), r("AE", w), r("EQ", w), A.add)
-        for b in range(t + 1):
-            for cc, n, tmp in ((0, "EX", "E1"), (1, "EY", "E2")):
-                pe = r(n, (128 * b, 128 * b + 128))
-                own = r("XACC", cc, (7 - b, 1024, 8))
+        mm([(bx, mx(DXP), de)])
+        mm([(by, mx(DYP), de)])
+        tt(ex, ex, bx, A.mult)
+        tt(ey, ey, by, A.mult)
+        mm([(bx, mx(IB_), qe), (bx, I32, ex)], True, False)
+        mm([(bx, I32, ey)], False, True)
+        act(ez, bx, F.Abs)
+        act(bx, bx, F.Sign)
+        mm([(by, mx(MT), de)])
+        tt(ez, ez, by, A.subtract)
+        act(en, ez, F.Sign, bias=-0.5)
+        mm([(by, mx(MC), se), (by, mx(ONC), en)])
+        tt(et, ez, by, A.min)
+        ts(eq, et, 0.0, A.max, 1023.0, A.min)
+        tt(qe, eq, bx, A.mult)
+        if t < 2:
+            act(se, by, F.Sigmoid, bias=col(13), scale=col(12))
+        mm([(bx, mx(PX_), de)])
+        tt(ex, qe, bx, A.mult)
+        mm([(by, mx(PY_), de)])
+        tt(ey, qe, by, A.mult)
+        tt(r("AE", w), r("AE", w), eq, A.add)
+        for b in range(n):
+            for c, tmp in ((0, "S1"), (1, "SCN")):
+                pe = r("WB", 4 * c + b)
+                own = r("XACC", c, (7 - b, 1024, 8))
                 tt(own, own, pe, A.add)
-                tt(r(tmp), ind(r("XACC", cc), r("OT", b)), pe, A.subtract)
-                cp(ind(r("XACC", cc), r("OT", b)), r(tmp))
+                tt(r(tmp), ind(r("XACC", c), r("OT", b)), pe, A.subtract)
+                cp(ind(r("XACC", c), r("OT", b)), r(tmp))
         if t == 2:
-            act(r("LS", (0, 1024)), r("LDF"), F.Identity, scale=0.0)
+            act(r("LS", (0, 1024)), r("MASK", (0, 1024)), F.Identity, scale=0.0)
             for b in range(3):
                 ae = r("AE", (128 * b, 128 * b + 128))
                 own = r("LS", (7 - b, 1024, 8))
-                tt(r("E1"), ind(r("WW"), r("OT", b)), ae, A.mult)
-                tt(r("E2"), r("WW", (7 - b, 1024, 8)), ae, A.mult)
-                tt(own, own, r("E1"), A.add)
-                tt(r("E3"), ind(r("LS"), r("OT", b)), r("E2"), A.add)
-                cp(ind(r("LS"), r("OT", b)), r("E3"))
+                tt(r("S1"), ind(r("WW"), r("OT", b)), ae, A.mult)
+                tt(r("SCN"), r("WW", (7 - b, 1024, 8)), ae, A.mult)
+                tt(own, own, r("S1"), A.add)
+                tt(r("S2"), ind(r("LS"), r("OT", b)), r("SCN"), A.add)
+                cp(ind(r("LS"), r("OT", b)), r("S2"))
 
     def rows_update(t):
-        for h, x in enumerate((X0, X1)):
-            hs = (512 * h, 512 * h + 512)
-            mm([(x, mx(IB_), r("SL", hs))])
-            tt(r("LS", hs), r("LS", hs), x, A.mult)
         for b in range(t + 1):
             se = r("SE", (128 * b, 128 * b + 128))
             own = r("LS", (7 - b, 1024, 8))
-            tt(r("E3"), r("OVV", b), se, A.mult)
-            tt(r("E4"), r("OVC", b), se, A.mult)
-            tt(own, own, r("E3"), A.add)
-            tt(r("E3"), ind(r("LS"), r("OT", b)), r("E4"), A.add)
-            cp(ind(r("LS"), r("OT", b)), r("E3"))
+            tt(r("S2"), r("OVV", b), se, A.mult)
+            tt(r("SC2"), r("OVC", b), se, A.mult)
+            tt(own, own, r("S2"), A.add)
+            tt(r("S2"), ind(r("LS"), r("OT", b)), r("SC2"), A.add)
+            cp(ind(r("LS"), r("OT", b)), r("S2"))
+
+    def tile(name, q, j):
+        return r(name, q, (j, SCRATCH[name][1][2], 16), raw=True)
+
+    def positions(sp):
+        q, kh = divmod(sp, 2)
+        dd = r("DD", q, (4 * kh, 4 * kh + 4))
+        lin(DMODE[sp], dd, ind(r("PW"), r("ONB", (64 * sp, 64 * sp + 64))), -1.0, 0.0)
+        dma("g", [(dd, r("AB", 4 + q))], acc=True)
+        act(dd, dd, F.Square)
+        if kh == 1:
+            mm([(r("CNT", (0, 2), (8 * j, 8 * j + 8)), tile("DD", q, j), r("MX", (PX_, PY_ + 1), (0, 128, 16)))
+                for j in range(16)] +
+               [(r("CNT", (2, 4)), r("W2", (7 - k, 135 - k)), r("DD", q, k)) for k in range(8)])
+            act(r("AT", (q, 8, 4)), r("CNT", (0, 2)), F.Identity)
+            act(r("D2", (256 * q, 256 * q + 256)), r("CNT", (2, 4)), F.Identity)
+            if q % 2:
+                u = q - 1
+                dma("y", [(r("DM", c, j, (128 * u, 128 * u + 256), p=(j, 128, 16)),
+                           r("AT", (4 * c + u, 4 * c + u + 2), p=(j, 128, 16))) for j in range(16) for c in range(2)], nb=300000)
+
+    def forces(t, sp):
+        q, kh = divmod(sp, 2)
+        b = sp % 2
+        if kh == 0:
+            own = r("UR", q % 2, None, (0, 256))
+            act(own, r("UW", None, (256 * q, 256 * q + 256)), F.Identity, bias=-RND)
+            dma("y", [(r("UR", q % 2, None, (256 * k, 256 * k + 256)), own) for k in range(1, 4)])
+        how = GMODE[t][2 * sp:2 * sp + 2]
+        if "F" in how and (kh == 0 or "F" not in GMODE[t][2 * sp - 2:2 * sp]):
+            dma("y", [(r("UF"), r("UW", None, (256 * q, 256 * q + 256)))])
+        for c in range(2):
+            if how[c] == "F":
+                for k in range(4):
+                    tt(r("G", b, c, (256 * k, 256 * k + 256)), ind(r("UW", c), r("ONB", (64 * sp + 16 * k, 64 * sp + 16 * k + 16))),
+                       r("UF", c), A.subtract)
+            else:
+                lin(how[c], r("G", b, c), ind(r("UW", c), r("ONB", (64 * sp, 64 * sp + 64))), -1.0, RND)
+        if how != "FF":
+            cs = (int(how[0] == "F"), 2 - int(how[1] == "F"))
+            dma("g", [(r("G", b, cs), r("UR", q % 2, cs))], acc=True)
+        for h in range(2):
+            hs, dd = (512 * h, 512 * h + 512), r("DD", q, (4 * kh + 2 * h, 4 * kh + 2 * h + 2))
+            mm([(r("DXY", 0), mx(DXP if how[0] == "F" else DXN), dd)])
+            mm([(r("DXY", 1), mx(DYP if how[1] == "F" else DYN), dd)])
+            if EADD[t][sp] == "V":
+                tt(r("EE", b, 0, hs), r("G", b, 0, hs), r("DXY", 0), A.mult)
+                tt(r("DXY", 1), r("G", b, 1, hs), r("DXY", 1), A.mult)
+                tt(r("EE", b, 0, hs), r("EE", b, 0, hs), r("DXY", 1), A.add)
+            else:
+                tt(r("EE", b, None, hs), r("G", b, None, hs), r("DXY"), A.mult)
+        if EADD[t][sp] != "V":
+            dma("g", [(r("EE", b, 0), r("EE", b, 1))], acc=True)
+        for h in range(2):
+            hs, ks = (512 * h, 512 * h + 512), (4 * kh + 2 * h, 4 * kh + 2 * h + 2)
+            dd, qc, e, m = r("DD", q, ks), r("QC", q, ks), r("EE", b, 0, hs), r("EE", b, 1, hs)
+            for x, mt in ((r("UB"), MT), (r("LB"), NMT)):
+                mm([(x, mx(mt), dd)] + ([(x, mx(NI), qc)] if t else []))
+            tt(m, e, r("UB"), A.min)
+            tt(r("LB"), m, r("LB"), A.max)
+            tt(qc, e, r("LB"), A.subtract)
+        qc = r("QC", q, (4 * kh, 4 * kh + 4))
+        ts(r("NZ", b), qc, 0.0, A.not_equal)
+        ts(qc, qc, -1023.0, A.max, 1023.0, A.min)
+        first = [(r("CNT", (0, 3)), mx(I16), r("SC", (t + 1) % 2, q))] if t and kh == 0 else []
+        mm(first + [(r("CNT", (1, 3)), r("C2", (7 - 4 * kh - k, 135 - 4 * kh - k)), r("NZ", b, k)) for k in range(4)] +
+           [(r("CNT", 0, (64 * kh, 64 * kh + 64)), r("WC", (15 - j, 143 - j)), tile("NZ", b, j)) for j in range(16)],
+           kh == 0, kh == 1)
+
+    def atile(q, j):
+        return r("AB", 2 * q + j // 8, j % 8 // 2, (128 * (j % 2), 128 * (j % 2) + 128))
+
+    def sums(t, q):
+        js = (256 * q, 256 * q + 256)
+        sa, sb = r("SC", t % 2, q, (0, 128)), r("SC", t % 2, q, (128, 384))
+        act(r("SC", t % 2, q), r("CNT", (0, 3)), F.Sigmoid, bias=-256.0 * (19.5 if t else 3.5), scale=256.0)
+        tt(r("SD"), sb, r("D2", js), A.mult)
+        mm([(r("X1", (0, 2)), mx(CX), r("SD")), (r("X1", (2, 4)), mx(CY), r("SD"))], True, False)
+        if t < 2:
+            tt(r("LS", js), r("LS", js), sb, A.mult)
+        if t:
+            mm([(r("CNT", 3), mx(IB_), sa), (r("CNT", 3), mx(IB_), r("SC", 0, q, (0, 128)) if t == 1 else r("SS", q))])
+            act(r("SS", q), r("CNT", 3), F.Identity, bias=0.0 if t == 1 else -1.5, scale=1.0 if t == 1 else 0.5)
+        for b in range(4):
+            tr = TRB[t][q == 3][b % 2]
+            mm([(r(tr), sa, r("SEL", (4 * b, 4 * b + 4)))] +
+               [(r(tr, j), tile("QC", q, 4 * b + j), mx(IB_)) for j in range(4)])
+            qs = r("QS", (16 * b, 16 * b + 16), (0, 3, 2))
+            if EVAC[t][4 * q + b] == "S":
+                act(qs, r(tr), F.Relu, bias=-1024.0)
+            else:
+                ts(qs, r(tr), -1024.0, A.add, 0.0, A.max)
+            terms = []
+            for j in range(4 * b, 4 * b + 4):
+                for gg in range(8):
+                    pr, odd = divmod(gg, 2)
+                    terms.append((r("X1", (j, 512, 16), p=(32 * pr, 32 * pr + 32), raw=True),
+                                  r("QS", 4 * j + pr, (odd, odd + 2)), r("DM", None, None, 128 * q + 8 * j + gg)))
+            mm(terms, False, False)
+            if b % 2:
+                out = r("AB", 2 * q + b // 2) if t == 0 else r("AT", (4 * b - 4, 4 * b + 4))
+                act(out, r("QS", (16 * b - 16, 16 * b + 16), (0, 3, 2)), F.Abs, bias=-1024.0)
+        if t == 1:
+            dma("g", [(r("AB", (2 * q, 2 * q + 2)), r("AT"))], acc=True)
+        s = r("XACC", None, js)
+        mm([(X1, I32, s)], False, True)
+        tt(s, r("UW", None, js), X1, A.add)
+
+    def update(t, q):
+        js = (256 * q, 256 * q + 256)
+        s = r("XACC", None, js)
+        ts(r("UW", None, js) if t < 2 else s, s, RND - 1023.0, A.max, RND + 1023.0, A.min)
+        if t == 2:
+            act(s, s, F.Identity, bias=-RND)
+            dma("y", [(hbm(("yx", "yy")[c], slice(None), slice(*js)), r("XACC", c, js)) for c in range(2)])
+
+    def weights(q):
+        js = (256 * q, 256 * q + 256)
+        wg = ("BASE", "WB")[q % 2]
+        for kh in range(2):
+            o = r("ONB", (128 * q + 64 * kh, 128 * q + 64 * kh + 64))
+            lin(WMODE[2 * q + kh], r(wg, (8 * kh, 8 * kh + 8)), ind(r("WW"), o), 1.0, 0.0)
+            ks = (64 * kh, 64 * kh + 64)
+            for h in range(2):
+                terms = []
+                for j in range(h, 16, 2):
+                    out = x0(j // 2, 512, 8)
+                    terms += [(out, r("SEL", j), r("SS", q, ks)), (out, atile(q, j), r("MX", IB_, ks)),
+                              (out, r("AT", j), r("MX", IB_, ks))]
+                mm(terms)
+                x = r(wg, (1024 * kh + h, 1024 * kh + 1024, 2), raw=True)
+                tt(x, x, X0, A.mult)
+            if WTREE[q] == "P":
+                x = r("TR", (0, 2))
+                mm(([(x, I32, r("LS", js))] if kh == 0 else []) +
+                   [(x, I32, r(wg, (8 * kh + 2 * k, 8 * kh + 2 * k + 2))) for k in range(4)], kh == 0, kh == 1)
+        if WTREE[q] == "P":
+            act(r("LS", js), r("TR", (0, 2)), F.Identity)
+        else:
+            dma("g", [(r(wg, (0, 8)), r(wg, (8, 16)))], acc=True)
+            dma("g", [(r(wg, (0, 4)), r(wg, (4, 8)))], acc=True)
+            dma("g", [(r("LS", js), r(wg, (0, 2)))], acc=True)
+            dma("g", [(r("LS", js), r(wg, (2, 4)))], acc=True)
+        dma("s", [(hbm("yw", slice(None), slice(*js)), r("LS", js))])
 
     for t in range(3):
-        tag[0] = BOOST[t]
         step1(t)
         if t == 0:
-            cp(r("EZ", (0, 256)), ind(r("WW", (0, 1024)), r("OB")))
-            send(r("EZ", (0, 256)), [r("WW", (1024 + 256 * d, 1280 + 256 * d)) for d in range(3)], 9)
+            cp(r("WB", (8, 10)), ind(r("WW", (0, 1024)), r("OB")))
+            send(r("WB", (8, 10)), [r("WW", (1024 + 256 * d, 1280 + 256 * d)) for d in range(3)], 9)
         extras(t)
-
-        def piece(j):
-            k, h = divmod(j, 2)
-            cs, hs = (512 * j, 512 * j + 512), (512 * h, 512 * h + 512)
-            g, pb = "G%d" % (k % 2), "PB%d" % (k % 2)
-            c = {"bx": r("DXY", 0), "by": r("DXY", 1), "gxy": r(g, None, hs), "am": AMODE[t][j],
-                 "cx": CAPX[t][j] == "1", "zh": ZHALF[t][j] == "1", "bz": r(ZB[j % len(ZB)]), "bt": bank(BT), "bc": r("CB"),
-                 "neg": GMODE[t][j] == "S", "dd": r("DD", cs), "gx": r(g, 0, hs), "gy": r(g, 1, hs), "q": r("Q", cs),
-                 "hasq": t > 0, "az": r("AZ%d" % (j % len(ZB))), "nz": r("NZ%d" % (j % 2)), "alive": r("DD", cs),
-                 "tt": r("TT%d" % (j % 2)), "aq": r("AQ", cs) if t == 0 else r("AT%d" % (k % 2), hs),
-                 "stay": r("ST%d" % (k % 2), hs) if t < 2 or CAPX[t][j] == "1" else None, "sb": 0.0, "ss": 1.0}
-            c["cx_"], c["cy_"], c["bw"] = [bank(x) for x in BANKS[t][j >= XFROM[t]]]
-            if SMODE != "Z":
-                c["sg"] = r("SG%d" % (j % 2))
-                c["bs"] = None if SMODE == "S" else bank(SMODE)
-            if k == 0:
-                c["px"], c["py"], c["pw"] = r("SACC", 0, hs), r("SACC", 1, hs), r("WACC", hs)
-            elif k == 7:
-                c["px"], c["py"], c["pw"] = c["cx_"], c["cy_"], c["bw"]
-            else:
-                c["px"], c["py"], c["pw"] = r(pb, 0, hs), r(pb, 1, hs), r("WG%d" % (k % 2), hs)
-            c["wg"], c["aqs"] = r("WG%d" % (k % 2), hs), r("AQ", cs)
-            return c
-
-        def fetch(j):
-            o = r("ONB", (32 * j, 32 * j + 32))
-            g, hs = "G%d" % (j // 2 % 2), (512 * (j % 2), 512 * (j % 2) + 512)
-            if GMODE[t][j] == "V":
-                dma("y", [(r(g, None, hs), r("UW", None, hs))])
-            for c in range(2):
-                if GMODE[t][j] == "S":
-                    act(r(g, c, hs), ind(r("UW", c), o), F.Identity, scale=-1.0)
-                else:
-                    tt(r(g, c, hs), ind(r("UW", c), o), r(g, c, hs), A.subtract)
-            if GMODE[t][j] == "S":
-                dma("g", [(r(g, None, hs), r("UW", None, hs))], acc=True)
-
-        def pre(j):
-            po = r("PO", (512 * (j % 2), 512 * (j % 2) + 512))
-            dd = r("DD", (512 * j, 512 * j + 512))
-            o = r("ONB", (32 * j, 32 * j + 32))
-            if DMODE[j] == "V":
-                tt(dd, ind(r("PW"), o), po, A.subtract)
-                act(dd, dd, F.Square)
-            elif DMODE[j] == "D":
-                act(dd, ind(r("PW"), o), F.Identity, scale=-1.0)
-                dma("g", [(dd, po)], acc=True)
-                act(dd, dd, F.Square)
-            else:
-                act(dd, ind(r("PW"), o), F.Identity)
-                mm([(bank(BT), mx(IB_), dd), (bank(BT), mx(NI), po)])
-                act(dd, bank(BT), F.Square)
-
-        def finish(j):
-            k, h = divmod(j, 2)
-            c = piece(j)
-            stage_c(c)
-            hs = (512 * h, 512 * h + 512)
+        for q in range(4):
+            if t == 0 and q % 2 == 0:
+                for sp in range(2 * q, 2 * q + 4):
+                    positions(sp)
+            forces(t, 2 * q)
+            forces(t, 2 * q + 1)
+            sums(t, q)
             if t == 2:
-                if h == 0:
-                    act(r("WG%d" % (k % 2)), ind(r("WW"), r("ONB", (64 * k, 64 * k + 64))), F.Identity)
-                mm([(c["bw"], mx(IB_), c["aqs"]), (c["bw"], mx(IB_), c["aq"])])
-                tt(c["pw"], c["wg"], c["bw"], A.mult)
-                if k == 7:
-                    tt(r("WACC", hs), r("WACC", hs), c["bw"], A.add)
-                    dma("s", [(hbm("yw", slice(None), slice(*hs)), r("WACC", hs))])
-            if k == 7:
-                both = FIN3[h] == "1" and c["px"]["name"] == c["py"]["name"]
-                if both:
-                    s = r("SACC", None, hs)
-                    tt(s, s, r("DXY"), A.add)
-                    ts(s, s, 1.0, A.max, 2047.0, A.min)
-                for cc in range(2):
-                    s = r("SACC", cc, hs)
-                    how = RNDS[2 * h + cc]
-                    if not both:
-                        tt(s, s, c[("px", "py")[cc]], A.add)
-                        if how != "S":
-                            ts(s, s, 1.0, A.max, 2047.0, A.min)
-                    out = r("UW", cc, hs) if t < 2 else s
-                    back = RND if t < 2 else RND + 1024.0
-                    if how == "S" and not both:
-                        act(s, s, F.Relu, bias=-1.0)
-                        act(s, s, F.Relu, bias=2046.0, scale=-1.0)
-                        act(s, s, F.Identity, bias=RND + 2047.0, scale=-1.0)
-                        act(out, s, F.Identity, bias=-back)
-                    elif how == "v":
-                        ts(out, s, RND, A.add, back, A.subtract)
-                    else:
-                        act(s, s, F.Identity, bias=RND)
-                        act(out, s, F.Identity, bias=-back)
-                    if t == 2:
-                        dma("y", [(hbm(("yx", "yy")[cc], slice(None), slice(*hs)), s)])
-            if h == 1:
-                ks = (1024 * k, 1024 * k + 1024)
-                if t < 2:
-                    st = "ST%d" % (k % 2)
-                    dma("y", [(r("SL", p=(k, 128, 16)), r(st, p=(k, 128, 16))),
-                              (r("DD", ks, p=(12, 128, 16)), r(st, p=(12, 128, 16)))], nb=100000)
-                if t == 1:
-                    dma("g", [(r("AQ", ks), r("AT%d" % (k % 2)))], acc=True)
-                if 0 < k < HK:
-                    dma("g", [(r("SACC"), r("PB%d" % (k % 2)))], acc=True)
-                    if t == 2:
-                        dma("g", [(r("WACC"), r("WG%d" % (k % 2)))], acc=True)
-                if k == XK[t]:
-                    dma("g", [(r("SACC"), r("XACC", None, (0, 1024)))], acc=True)
-                    if t == 2:
-                        dma("g", [(r("WACC"), r("LS", (0, 1024)))], acc=True)
-            if HK <= k < 7:
-                dma("g", [(r("SACC", None, hs), r("PB%d" % (k % 2), None, hs))], acc=True)
-                if t == 2:
-                    dma("g", [(r("WACC", hs), r("WG%d" % (k % 2), hs))], acc=True)
-
-        tag[0] = 0.0
-        for j in range(3):
-            fetch(j)
-        if t == 0:
-            pre(0)
-        for j in range(16 + max(CSKEW, BSKEW)):
-            if j < 16:
-                if j >= 1 and j + 2 < 16 and j + 2 > 2:
-                    fetch(j + 2)
-                if t == 0 and j < 15:
-                    pre(j + 1)
-                stage_a(piece(j))
-            if CFIRST and j >= CSKEW:
-                finish(j - CSKEW)
-            if BSKEW <= j < 16 + BSKEW:
-                stage_b(piece(j - BSKEW))
-            if not CFIRST and j >= CSKEW:
-                finish(j - CSKEW)
+                update(t, q)
+                weights(q)
         if t < 2:
-            cp(r("SND", 0), ind(r("UW", 0, (0, 1024)), r("OB")))
-            cp(r("SND", 1), ind(r("UW", 1, (0, 1024)), r("OB")))
+            for q in range(4):
+                update(t, q)
+            border()
             la = ("LA1", "LA0")[t]
             send(r("SND", (0, 2)), [r(la, (2 * d, 2 * d + 2)) for d in range(3)], 3 * (t + 1))
             rows_update(t)
@@ -711,17 +689,27 @@ def hazards(ops):
     seen = {}
     for i, o in enumerate(ops):
         dep = set()
-        acc = [(x, True) for x in o["w"]] + [(x, False) for x in o["r"]]
-        acc = [(x, wr, a, b) for x, wr in acc for a, b in x["spans"]]
+        acc = set()
+        for xs, wr in ((o["w"], True), (o["r"], False)):
+            for x in xs:
+                for a, b in x["spans"]:
+                    acc.add((x["name"], wr, a, b))
+        joined = []
+        for x, wr, a, b in sorted(acc, key=lambda y: (not y[1], y[0], y[2])):
+            if joined and joined[-1][:2] == (x, wr) and a <= joined[-1][3]:
+                joined[-1] = (x, wr, joined[-1][2], max(b, joined[-1][3]))
+            else:
+                joined.append((x, wr, a, b))
+        acc = joined
         for x, wr, a, b in acc:
-            ps = _ps(x)
-            for (j, lo, hi, w2) in seen.get(x["name"], []):
+            ps = SCRATCH[x][0] == "psum"
+            for (j, lo, hi, w2) in seen.get(x, []):
                 if lo < b and a < hi and (wr or w2 or (ps and ops[j]["eng"] != o["eng"])):
                     dep.add(j)
         if o["kind"] == "recv":
             dep = {o["after"]}
         for x, wr, a, b in acc:
-            lst = seen.setdefault(x["name"], [])
+            lst = seen.setdefault(x, [])
             if wr:
                 lst[:] = [e for e in lst if e[0] == i or not (a <= e[1] and e[2] <= b)]
             lst.append((i, a, b, wr))
@@ -744,10 +732,6 @@ def arrange(ops):
     level = [0.0] * n
     for i in range(n - 1, -1, -1):
         level[i] = ops[i]["cost"] + tail(ops[i]) + 0.1 + max([level[j] for j in succ[i]] + [0.0])
-    z = SEED
-    for i in range(n):
-        z = (z * 1103515245 + 12345) % 2147483648
-        level[i] += JIT * (z / 2147483648.0)
     best = None
     for it in range(PASSES + 1):
         order = forward(ops, succ, level)
@@ -800,7 +784,6 @@ def forward(ops, succ, level):
     left = [len(o["dep"]) for o in ops]
     ready = {e: [] for e in "vspgyx"}
     at = [0.0] * n
-    fin = [0.0] * n
     for i, o in enumerate(ops):
         if not left[i]:
             ready[o["eng"]].append(i)
@@ -819,7 +802,7 @@ def forward(ops, succ, level):
             if not lst:
                 continue
             s = min(max(free[e], at[i]) for i in lst)
-            i = max((i for i in lst if max(free[e], at[i]) <= s + LOOK), key=lambda q: level[q] + ops[q]["up"])
+            i = max((i for i in lst if max(free[e], at[i]) <= s + LOOK), key=lambda q: level[q])
             if e == "g" and ops[i]["kind"] == "dma" and hold[0] and at[hold[0][0]] <= s + GLOOK:
                 continue
             s = max(free[e], at[i])
@@ -838,7 +821,7 @@ def forward(ops, succ, level):
             end = pipe[0] + 0.8
         if o["kind"] == "send":
             end += 4.0
-        fin[i] = o["t1"] = end
+        o["t1"] = end
         for j in succ[i]:
             lat = 0.0 if ops[j].get("cont") and o["eng"] == "p" else 0.1
             at[j] = max(at[j], end + lat)

@@ -16,16 +16,55 @@ WTREE = "DDDP"
 EADD = ["D" * 8] * 3
 S1G = ["SS"] * 3
 CONV = "vvv"
-GMODE = ['FFSSSSSSSSSSSSSS', 'FFSSSSSSSSSSSSSS', 'FSSSSSSSSSSSSSSS']
+GMODE = ['RRSSSSSSSSSSSSSS', 'RRSSSSSSSSSSSSSS', 'RSSSSSSSSSSSSSSS']
 EADD = ['VDDDDDDD', 'DDDDDDDD', 'VDDDDDDD']
-S1G = ['VS', 'VV', 'VS']
+S1G = ['VS', 'VS', 'VS']
+DMODE = "VVSSSSSS"
+FAST = ["FDDD"] * 3
+CUT = ["SSSV"] * 3
+MARK = ["VVVVVVVV"] * 3
 CONV = 'svs'
-S1Z = "PVV"
-MBS = False
-CMS = False
-LOOK = 0.05
+S1Z = ["PP", "VP", "VP"]
+S1C = ["VS", "VS", "VS"]
+CONS = "V"
+CPU = "VV"
+WT3 = "PV"
+CLOSE = "SSS"
+GMG = "VVV"
+WBUF = ("BASE", "WB", "BASE", "UW")
+TALL = (3,)
+PAR = [1, 1, 1]
+FIN = ["PPPP"] * 3
+UAC = ["GG"] * 3
+CLIP = ["DDDDDDDV"] * 3
+NG, NE, NR, NU = 2, 3, 3, 5
+OWN = ["SSSS"] * 3
+BORD = "VS"
+EVG = "S"
+PACE = {"ga": 1.56, "sc": 3.8, "wake": 0.1, "dlat": 1.6, "rate": 700e3, "gi": 1.0, "yi": 0.12, "rem": 4.0, "row": 1600}
+LOOK = {"v": 0.05, "s": 0.05, "p": 0.05, "g": 0.05, "y": 0.05, "x": 0.05}
+EARLY = [2, 2, 1]
+RUN = 0.4
+UP = [0.0, 0.0, 0.0]
+UP2 = [0.0, 0.0, 0.0]
+UP3 = [0.0, 0.0, 0.0]
 GLOOK = 0.9
-PASSES = 2
+PASSES = 1
+GMODE = ['FFSSSSSSSSSSSSSS', 'FRSSSSSSSSSSSSSS', 'FFSSSSSSSSSSSSSS']
+FAST = ["DDDD"] * 3
+EARLY, WT3, CLOSE, CONV = [0, 2, 0], "VV", "AAV", "svv"
+S1G, S1Z, S1C = ['VS', 'VV', 'VV'], ['PV', 'VV', 'VD'], ['SS', 'VS', 'SS']
+FIN = ['PVSP', 'PSVP', 'PAAP']
+CUT = ['SSSV'] * 3
+MARK = ['VVVVVVVV', 'VVVVVSVV', 'VVVVVVVV']
+CLIP = ['VVVDVVVV', 'DVVVVVVV', 'DVVVVVVV']
+EADD = ['DDDVDDDV', 'DDDDDDDD', 'DDDDDDDD']
+LOOKS = [(0.05, 0.05, 0.05, 0.05, 0.05), (0.0, 0.1, 0.1, 0.3, 0.05)]
+SWAPS, SLACK = 4000, 0.0
+PACES = [{"work": 1.0, "pe": 1.05, "pick": 1.0, "dma": 1.0, "wait": 1.0, "all": 1.0},
+         {"work": 1.1, "pe": 1.15, "pick": 1.4, "dma": 1.2, "wait": 1.5, "all": 1.2},
+         {"work": 1.0, "pe": 1.05, "pick": 0.8, "dma": 1.5, "wait": 1.8, "all": 1.15},
+         {"work": 1.4, "pe": 1.45, "pick": 1.4, "dma": 1.2, "wait": 1.4, "all": 1.4}]
 
 
 def _sb(shape, d):
@@ -33,41 +72,45 @@ def _sb(shape, d):
 
 
 SCRATCH = {
-    "DD": _sb([4, 2048], h16), "QC": _sb([4, 2048], h16), "NZ": _sb([2, 1024], b16),
-    "QS": _sb([64, 3, 16], h16), "DM": _sb([2, 16, 512], h16), "AB": _sb([8, 4, 256], h16), "AT": _sb([16, 128], h16),
-    "G": _sb([2, 2, 1024], h16), "EE": _sb([2, 2, 1024], i32), "UR": _sb([2, 2, 1024], h16),
+    "QC": _sb([4, 2048], h16), "NZ": _sb([2, 1024], b16), "AP": _sb([2, 1024], h16), "TT": _sb([1024], h16),
+    "EQ": _sb([1152], b16),
+    "QS": _sb([32, 3, 16], h16), "DM": _sb([2, 16, 512], h16), "AB": _sb([8, 1024], h16), "AT": _sb([16, 128], h16),
+    "G": _sb([NG, 2, 1024], h16), "EE": _sb([5, 1024], i32), "UR": _sb([NR, 2, 1024], h16),
     "UW": _sb([2, 1800], f32), "PW": _sb([1800], b16), "PO": _sb([1024], h16), "WW": _sb([1800], f32),
     "LS": _sb([1152], f32), "XACC": _sb([2, 1152], f32), "BASE": _sb([2048], f32), "WB": _sb([2048], f32),
-    "SC": _sb([2, 4, 384], b16), "SS": _sb([4, 128], b16), "D2": _sb([1024], h16), "SD": _sb([256], h16),
+    "SC": _sb([2, 4 + len(TALL), 128], b16), "SS": _sb([4 + len(TALL), 128], b16), "D2": _sb([1024], h16),
     "SEL": _sb([16, 128], b16), "LA0": _sb([6, 256], h16), "LA1": _sb([6, 256], h16), "SND": _sb([3, 256], h16),
     "NBI": _sb([8, 4, 16], i32), "BI": _sb([16], i32), "ONB": _sb([512], u16), "OB": _sb([16], u16),
     "PI": _sb([8], i32), "CL": _sb([32], f32), "J": _sb([144], f32), "IW": _sb([136], f32), "WC": _sb([144], b16),
-    "C2": _sb([136], b16), "W2": _sb([136], b16),
-    "MX": _sb([25, 128], b16), "DIAG": _sb([128], f32), "MASK": _sb([1032], b16), "RS8": _sb([512], f32),
+    "C2": _sb([136], b16), "W2": _sb([136], b16), "PL": _sb([2, 8], b16), "UP": _sb([128], b16),
+    "MX": _sb([32, 128], b16), "DIAG": _sb([128], f32), "MASK": _sb([1032], b16), "RS8": _sb([512], b16),
+    "DK": _sb([2, 128], f32),
     "RS16": _sb([128], f32), "DUM": _sb([128], f32), "DUMM": _sb([128], f32), "VID": _sb([2, 128], f32),
     "OAI": _sb([64], i32), "OA": _sb([3, 64], u16),
     "GM": _sb([1024], h16), "D1": _sb([512], h16), "MB": _sb([512], b16), "CM": _sb([512], h16),
     "NF": _sb([128], f32), "S1": _sb([128], f32), "SCN": _sb([128], f32), "S2": _sb([128], f32), "SC2": _sb([128], f32),
     "U16": _sb([128], h16), "EV": _sb([128], b16), "FV": _sb([128], b16), "FC": _sb([128], b16),
     "MD": _sb([128], f32), "DF": _sb([128], f32), "ON": _sb([64], u16), "OC": _sb([64], u16), "OX": _sb([64], u16),
-    "OM": _sb([8], u16), "OT": _sb([3, 8], u16), "OVV": _sb([2, 128], h16), "OVC": _sb([2, 128], h16),
-    "UF": _sb([2, 256], f32),
-    "DE": _sb([384], b16), "SE": _sb([384], b16), "QE": _sb([384], h16), "AE": _sb([384], f32),
+    "OM": _sb([8], u16), "OT": _sb([24], u16), "OVV": _sb([2, 128], h16), "OVC": _sb([2, 128], h16),
+    "DE": _sb([384], b16), "SE": _sb([384], b16), "QE": _sb([384], h16),
+    "WX": _sb([3, 384], f32), "EN": _sb([384], b16), "ET": _sb([384], h16), "EC": _sb([768], h16),
 }
 SCRATCH["DXY"] = ("psum", [128, 2, 512], f32)
-for _n in ("UB", "LB", "TR", "X0", "X1"):
+SCRATCH["UL"] = ("psum", [128, 2, 512], f32)
+SCRATCH["XS"] = ("psum", [128, 2, 256], f32)
+for _n in ("TR", "X0"):
     SCRATCH[_n] = ("psum", [128, 512], f32)
 SCRATCH["CNT"] = ("psum", [128, 4, 128], f32)
 SIZE = {f32: 4, i32: 4, b16: 2, h16: 2, u16: 2}
 NDS = 130
 SEMAPHORES = ["cv", "cs", "cp", "cg"] + ["d%d" % i for i in range(NDS)] + \
     ["ar%d" % i for i in range(12)] + ["lo%d" % i for i in range(4)]
-(BLK, IB_, NI, DXP, DXN, DYP, DYN, PX_, PY_, MT, ONC, MC, SCO, NBG, PBG, NON, KC, TRI, BD0, BD1, BD2, I16, NMT,
- CX, CY) = range(25)
+(BLK, IB_, NI, DXP, D8, DYP, ND8, PX_, PY_, MT, ONC, MC, SCO, NBG, PBG, NON, KC, TRI, BD0, BD1, BD2, I16, QE8,
+ CX, CY, RN, NRN, SC2, NMT, D16, C64, OW) = range(32)
 
 
-UNIT = {"WB": (0, 128), "BASE": (0, 128), "TR": (0, 128), "X0": (0, 128), "X1": (0, 128), "UB": (0, 128), "LB": (0, 128),
-        "DD": (1, 256), "QC": (1, 256), "NZ": (1, 256)}
+UNIT = {"WB": (0, 128), "BASE": (0, 128), "TR": (0, 128), "X0": (0, 128),
+        "QC": (1, 256), "NZ": (1, 256)}
 
 
 def r(name, *ix, p=None, raw=False):
@@ -146,6 +189,7 @@ def _ps(x):
 
 def build():
     ops = []
+    up = [0.0]
 
     def add(eng, kind, args, outs, ins, cost, **kw):
         w, rd = [], []
@@ -155,17 +199,19 @@ def build():
             rd += q[1:]
         for o in ins:
             rd += _parts(o)
-        d = {"eng": eng, "kind": kind, "args": args, "w": w, "r": rd, "cost": cost}
+        d = {"eng": eng, "kind": kind, "args": args, "w": w, "r": rd, "cost": cost, "up": up[0]}
+        d["sort"] = "dma" if kind in ("dma", "send") else "pick" if any(
+            isinstance(x, dict) and x["k"] == "i" for x in list(outs) + list(ins)) else "work"
         d.update(kw)
         ops.append(d)
         return len(ops) - 1
 
     def vc(out, in0, c):
         if out["k"] == "i":
-            return 0.06 + out["n"] * 3.8 * 0.00083
+            return 0.05 + out["n"] * PACE["sc"] * 0.00083
         if in0 is not None and in0["k"] == "i":
-            return 0.06 + out["n"] * 1.56 * 0.00083
-        return 0.06 + max(64, out["n"] * c) * 0.00083
+            return 0.05 + out["n"] * PACE["ga"] * 0.00083
+        return 0.045 + max(64, out["n"] * c) * 0.00083
 
     def tt(out, a, b, op):
         add("v", "tt", (out, a, b, op), [out], [a, b], vc(out, a, 1 if _ps(a) or _ps(b) else 2))
@@ -184,7 +230,7 @@ def build():
 
     def act(out, a, fn, bias=0.0, scale=1.0):
         add("s", "act", (out, a, fn, bias, scale), [out], [a, bias, scale],
-            0.07 + max(64, out["n"] * (1.56 if a["k"] == "i" else 1)) * 0.00083)
+            0.065 + max(64, out["n"] * (PACE["ga"] if a["k"] == "i" else 1)) * 0.00083)
 
     def lin(who, out, a, scale, bias):
         if who in "Ss":
@@ -193,23 +239,26 @@ def build():
             ts(out, a, scale, A.mult, bias, A.add)
 
     def mm(terms, start=True, stop=True):
-        c = 0.0
-        ins = []
-        for o, l, x in terms:
+        c, ins, run = 0.0, [], []
+        for m, (o, l, x) in enumerate(terms):
             c += max(min(64, l["n"]), x["n"]) * (1 if _two(x) else 4) * 0.000417
             ins += [l, x]
-        add("p", "mm", (terms, start, stop), [terms[0][0]], ins, c + 0.02, cont=not start)
+            run.append((o, l, x))
+            if c >= RUN or m == len(terms) - 1:
+                add("p", "mm", (run, start, stop and m == len(terms) - 1), [o], ins, c + 0.02, cont=not start)
+                c, ins, run, start = 0.0, [], [], False
 
     def iota(out, pat, base, cm):
         add("g", "iota", (out, pat, base, cm), [out], [], 0.13 + out["n"] * 0.00166)
 
     def dma(q, pairs, acc=False, nb=None):
-        by = 0
+        by = rows = 0
         for o, i in pairs:
             x = o if o["k"] == "b" else i
             by += x["n"] * SIZE[SCRATCH[x["name"]][2]] * 128
+            rows += max(len(y["spans"]) for y in (o, i) if y["k"] == "b") * (128 if x["ix"][0].step is None else 8)
         add(q, "dma", (pairs, acc), [o for o, i in pairs], [i for o, i in pairs],
-            (1.0 if q == "g" else 0.1) * len(pairs), by=(nb or by) * (2 if acc else 1))
+            PACE["gi" if q == "g" else "yi"] * len(pairs), by=(nb or by) * (2 if acc else 1) + rows * PACE["row"], rows=rows)
 
     def send(src, land, base):
         s = add("g", "send", (src, land, base), [], [src], 2.0)
@@ -220,17 +269,17 @@ def build():
         return r("X0", (a, b, s), raw=True)
 
     def x1(a, b, s=1):
-        return r("X1", (a, b, s), raw=True)
+        return r("TR", (a, b, s), raw=True)
 
-    X0, X1 = r("X0"), r("X1")
-    IC = r("EE", 1, 0)
+    X0, X1 = r("X0"), r("TR")
+    IC = r("EE", 2)
 
-    dma("y", [(r("EE", 0, 0), hbm("ux")), (r("BI"), hbm("bord"))])
-    dma("s", [(r("EE", 0, 1), hbm("uy"))])
-    ms(IC, 0)
+    dma("s", [(r("EE", 2, p=(8 + j, 128, 16)), hbm("py" if j & 2 else "px")) for j in range(8)], nb=400000)
+    dma("y", [(r("EE", 2, p=(k, 128, 16)), hbm("nb", slice(None), slice(64 * k, 64 * k + 64))) for k in range(8)], nb=600000)
+    ops[1]["beside"] = 0
+    dma("y", [(r("EE", 0), hbm("ux")), (r("BI"), hbm("bord"))])
+    dma("s", [(r("EE", 1), hbm("uy"))])
     dma("s", [(r("NBI"), hbm("nb"))])
-    dma("y", [(r("EE", 1, 0, p=(8 + j, 128, 16)), hbm("px" if j < 2 else "py")) for j in range(4)] +
-        [(r("EE", 1, 0, p=(k, 128, 16)), hbm("nb", slice(None), slice(64 * k, 64 * k + 64))) for k in range(8)], nb=800000)
     iota(r("PI", (0, 1)), [[0, 1]], 0, 1)
     iota(r("J"), [[1, 144]], 0, -1)
     iota(r("DIAG"), [[0, 8], [1, 16]], 0, 0)
@@ -252,33 +301,40 @@ def build():
         for row, v in terms:
             act(col(c), oh(row), F.Identity, bias=prev, scale=float(v))
             prev = col(c)
-    mkcol(16, [(8, 1), (9, -1), (10, 1)])
-    mkcol(17, [(11, -1), (14, 1), (15, 1)])
-    tt(col(7), col(16), col(17), A.add)
-    tt(col(15), col(7), oh(12), A.add)
+    tt(r("CL", (3, 5)), r("DIAG", (8, 12, 2)), r("DIAG", (9, 12, 2)), A.subtract)
+    tt(r("CL", (21, 23)), r("DIAG", (8, 12, 2)), r("DIAG", (9, 12, 2)), A.add)
+    ts(col(16), col(0), 14.0, A.is_ge, col(3), A.add)
+    act(col(7), col(4), F.Identity, bias=col(16))
+    act(col(15), oh(12), F.Identity, bias=col(7))
     ts(col(18), col(0), 8.0, A.is_ge)
     ts(r("MASK"), r("MASK"), col(0), A.is_equal, col(15), A.add)
-    ts(r("PO"), IC, col(18), A.mult, col(7), A.subtract)
+    ts(col(30), col(0), 12.0, A.is_ge, col(18), A.subtract)
+    ts(r("PO"), IC, col(30), A.mult, col(7), A.add)
     cp(r("OB"), r("BI"))
-    ts(r("UW", None, (0, 1024)), r("EE", 0), RND, A.add)
+    for c in range(2):
+        lin(CPU[c], r("UW", c, (0, 1024)), r("EE", c), 1.0, 0.0)
     ts(r("IW"), r("J", (0, 136)), 8.0, A.is_equal)
     I32 = r("IW", (8, 136))
     act(mx(IB_), I32, F.Identity)
+    act(mx(NI), I32, F.Identity, scale=-1.0)
     for h in range(2):
-        hs, x = (512 * h, 512 * h + 512), r("X%d" % h)
-        mm([(x, mx(IB_), r("MASK", hs)), (x, mx(IB_), r("PO", hs))])
+        hs, x = (512 * h, 512 * h + 512), (X0, X1)[h]
+        mm([(x, mx(IB_), r("MASK", hs)), (x, mx(NI), r("PO", hs))])
         act(r("PW", hs), x, F.Identity)
 
     def border():
         for c in range(2):
-            ts(r("SND", c), ind(r("UW", c, (0, 1024)), r("OB")), -RND, A.add)
+            lin(BORD[c], r("SND", c), ind(r("UW", c, (0, 1024)), r("OB")), 1.0, 0.0)
     border()
     ts(r("SND", 2), ind(r("PW", (0, 1024)), r("OB")), col(2), A.max)
-    send(r("SND"), [r("AB", d, (0, 3)) for d in range(3)], 0)
+    send(r("SND"), [r("AB", d, (0, 768)) for d in range(3)], 0)
     for q in range(4):
-        cp(r("ONB", (128 * q, 128 * q + 128)), r("NBI", None, q))
-    dma("y", [(r("AB", (4, 8), k), r("PO")) for k in range(4)])
-    ms(r("UW", None, (1792, 1800)), RND)
+        if q in TALL:
+            for h in range(2):
+                cp(r("ONB", (128 * q + 64 * h, 128 * q + 64 * h + 64)), r("NBI", None, q, (8 * h, 8 * h + 8)))
+        else:
+            cp(r("ONB", (128 * q, 128 * q + 128)), r("NBI", None, q))
+    ms(r("UW", None, (1792, 1800)), 0.0)
     ms(r("WW", (1792, 1800)), 0.0)
     ts(r("PW", (1792, 1800)), r("MASK", (0, 8)), 0.0, A.mult, col(2), A.add)
     ms(r("LS", (1024, 1152)), 0.0)
@@ -290,49 +346,62 @@ def build():
         ts(r("OA", t), r("OAI"), col(1), A.add, float(7 - t), A.add)
     ts(mx(BLK), r("S1"), col(0), A.add, 0.0, A.is_equal)
     ts(r("WC"), r("J"), col(0), A.add, 15.0, A.is_equal)
-    act(mx(NI), I32, F.Identity, scale=-1.0)
-    mkcol(3, [(8, 0.25), (9, -0.25)])
-    mkcol(4, [(10, 0.25), (11, -0.25)])
-    mkcol(5, [(8, 32), (9, 32), (10, 32), (11, 32), (12, -32768), (15, 32640)])
+    act(col(5), col(30), F.Identity, scale=-32.0)
+    mkcol(5, [(12, -32768), (15, 32640)], first=col(5))
     mkcol(6, [(12, 32768), (15, -23552)])
-    mkcol(8, [(15, -BIG + (131072 if CMS else 0)), (14, 1)])
-    for t in range(3):
-        mkcol(9 + t, [(7 - t, -BIG)], first=col(8))
+    mkcol(8, [(15, -BIG), (14, 1)])
+    act(r("CL", (9, 12)), r("DIAG", (5, 8)), F.Identity, bias=col(8), scale=-BIG)
     mkcol(12, [(15, -1)], first=1.0)
     mkcol(13, [(15, 200)])
     ts(col(14), col(0), -2048.0, A.mult, 16128.0, A.add)
-    tt(col(14), col(14), col(2), A.mult)
-    act(col(19), col(2), F.Identity, scale=-32.0)
-    act(col(20), col(18), F.Identity, scale=-32.0)
-    for m, c in ((DXP, 3), (DYP, 4), (MT, 5), (MC, 6), (KC, 14), (BD0, 9), (BD1, 10), (BD2, 11), (CX, 19), (CY, 20)):
-        act(mx(m), mx(BLK), F.Identity, scale=col(c))
-    for m, s, v in ((DXN, DXP, -1.0), (DYN, DYP, -1.0), (PX_, DXP, 1 / 32), (PY_, DYP, 1 / 32), (ONC, BLK, 1024.0),
-                    (SCO, BLK, 8192.0 if CMS else 16384.0), (NBG, BLK, -BIG), (PBG, BLK, BIG), (NON, BLK, -1.0), (NMT, MT, -1.0)):
-        act(mx(m), mx(s), F.Identity, scale=v)
-    ts(mx(I16), r("J", (0, 128)), 0.0, A.is_gt, -2.0, A.mult)
-    tt(mx(I16), mx(I16), I32, A.add)
-    tt(mx(I16), mx(I16), mx(BLK), A.mult)
-    ts(mx(TRI), mx(I16), col(2), A.mult)
-    act(mx(I16), I32, F.Identity, scale=16.0)
-    act(r("W2"), r("WC", (8, 144)), F.Identity, scale=col(3))
-    act(r("C2"), r("WC", (0, 136)), F.Identity, scale=col(4))
+    act(col(23), col(18), F.Identity, bias=-0.5)
+    act(col(25), col(23), F.Identity, scale=-1 / 16)
+    ts(col(27), col(0), col(1), A.subtract)
+    iota(r("S2"), [[0, 16], [1, 8]], 0, 0)
+    ts(r("S2"), r("S2"), col(27), A.is_equal)
+    tt(mx(D8), r("S2"), mx(BLK), A.mult)
+    act(r("UP"), r("IW", (0, 128)), F.Identity)
+    act(mx(D16), r("DIAG"), F.Identity)
+    for c in range(2):
+        ts(r("PL", c), r("MX", BLK, (0, 128, 16)), col(21 + c), A.mult, 1 / 64, A.mult)
+    for m, s, c, v in ((DXP, BLK, col(3), 0.25), (DYP, BLK, col(4), 0.25), (PX_, BLK, col(3), 1 / 128), (PY_, BLK, col(4), 1 / 128),
+                       (KC, BLK, col(14), col(2)), (CX, BLK, col(2), -65536.0), (CY, BLK, col(18), -65536.0),
+                       (NBG, BLK, col(23), -BIG), (RN, BLK, oh(15), RND), (NRN, BLK, oh(15), -RND), (C64, BLK, oh(15), 1 / 64),
+                       (ND8, D8, col(2), -1.0), (QE8, D8, col(2), 512.0)):
+        ts(mx(m), mx(s), c, A.mult, v, A.mult)
+    for m, s, v in ((MT, BLK, col(5)), (MC, BLK, col(6)), (BD0, BLK, col(11)), (BD1, BLK, col(10)), (BD2, BLK, col(9)),
+                    (ONC, BLK, 1024.0), (SCO, BLK, 16384.0), (PBG, BLK, BIG), (NON, BLK, -1.0), (SC2, BLK, 8192.0),
+                    (NMT, MT, -1.0), (I16, IB_, 16.0)):
+        if (m not in (SC2, NMT) or "S" in "".join(S1C)) and (m != SCO or "V" in "".join(S1C)):
+            ts(mx(m), mx(s), v, A.mult) if CONS == "V" else act(mx(m), mx(s), F.Identity, scale=v)
+    ts(mx(TRI), r("J", (0, 128)), 0.0, A.is_gt, -2.0, A.mult)
+    tt(mx(TRI), mx(TRI), I32, A.add)
+    ts(r("S2"), mx(BLK), col(2), A.mult)
+    tt(mx(TRI), mx(TRI), r("S2"), A.mult)
+    ts(r("W2"), r("WC", (8, 144)), col(21), A.mult, 1 / 4096, A.mult)
+    ts(r("C2"), r("WC", (0, 136)), col(22), A.mult, 1 / 4096, A.mult)
     tt(r("W2"), r("W2"), r("C2"), A.add)
+    mm([(x0(0, 128), r("W2", (7 - k, 135 - k)), mx(IB_)) for k in range(8)])
+    act(mx(OW), x0(0, 128), F.Identity)
+    mm([(x0(0, 128), mx(OW), mx(IB_))])
+    act(mx(OW), x0(0, 128), F.Identity)
     tt(r("C2"), r("WC", (0, 136)), r("WC", (8, 144)), A.add)
     iota(r("DUM"), [[-1, 128]], 1152, 0)
     for t in range(2):
         iota(r("VID", t), [[8, 128]], 7 - t - E, 0)
     tt(r("DUMM"), r("DUM"), r("DIAG"), A.mult)
-    act(r("RS8"), r("MASK", (0, 512)), F.Identity, bias=1e9, scale=0.0)
+    iota(r("RS8"), [[0, 64], [1, 8]], 0, 0)
+    ts(r("RS8"), r("RS8"), 1.0, A.min)
+    iota(r("DK", 0), [[-1, 128]], 1152 + 71 * 2048, 0)
+    iota(r("DK", 1), [[-1, 128]], 1152 + 7 * 2048, 0)
     ms(r("RS16"), 1.0)
     ms(r("RS16", (0, 128, 16)), 0.0)
     scan(r("MD"), r("RS16"), r("DUMM"), 0.0, A.mult, A.add)
     ms(r("QE"), 0.0)
-    act(r("AE"), r("MASK", (0, 384)), F.Identity, scale=0.0)
     ms(r("XACC", None, (1024, 1152)), 0.0)
-    dma("y", [(r("EE", 1, 1), hbm("ld"))])
+    dma("y", [(r("EE", 4), hbm("ld"))])
     dma("y", [(r("WW", (0, 1024)), hbm("wt"))])
-    ts(r("BASE", (8, 16)), r("EE", 1, 1), 0.5, A.add, 1 / 32, A.mult)
-    act(r("BASE", (0, 8)), r("MASK", (0, 1024)), F.Identity, bias=1 / 64, scale=0.0)
+    ts(r("BASE", (8, 16)), r("EE", 4), 0.5, A.add, 1 / 32, A.mult)
     iota(r("SEL"), [[1, 16], [16, 8], [0, 16]], 0, -1)
     ts(r("SEL"), r("SEL"), 0.0, A.is_equal, 2048.0, A.mult)
     ms(r("QS", None, 1), 0.0)
@@ -341,90 +410,107 @@ def build():
 
     def convert(t):
         for d in range(3):
-            la = r(("LA1", "LA0")[t - 1], (2 * d, 2 * d + 2)) if t else r("AB", d, (0, 2))
-            lin(CONV[d], r("UW", None, (1024 + 256 * d, 1280 + 256 * d)), la, 1.0, RND)
+            la = r(("LA1", "LA0")[t - 1], (2 * d, 2 * d + 2)) if t else r("AB", d, (0, 512))
+            lin(CONV[d], r("UW", None, (1024 + 256 * d, 1280 + 256 * d)), la, 1.0, 0.0)
             if t == 0:
-                cp(r("PW", (1024 + 256 * d, 1280 + 256 * d)), r("AB", d, 2))
+                cp(r("PW", (1024 + 256 * d, 1280 + 256 * d)), r("AB", d, (512, 768)))
     convert(0)
-
-    def ua(c=None):
-        return r("WB", (0, 8)) if c is None else r("WB", (4 * c, 4 * c + 4))
-
-    def ds(c=None):
-        return r("WB", (8, 16)) if c is None else r("WB", (8 + 4 * c, 12 + 4 * c))
 
     def step1(t):
         rho = 7 - t
         LSW = r("LS")
         act_ls = r("LS", (rho, 1024, 8))
-        mm([(x0(0, 64), I32, r("LS", (rho, 1024, 16))), (x0(0, 64), r("IW", (0, 128)), r("LS", (rho + 8, 1024, 16)))])
-        ts(r("ON"), x0(0, 64), float(E), A.add, 1024.0, A.min)
-        tt(r("GM"), ind(LSW, r("ON")), r("MASK", (t, t + 1024)), A.mult)
         cp(r("U16"), act_ls)
-        act(r("EV"), act_ls, F.Relu, bias=1.0)
-        mm([(x1(0, 128), mx(TRI), r("EV"))])
+        mm([(x0(0, 64), mx(IB_), r("U16", (0, 128, 2))), (x0(0, 64), r("UP"), r("U16", (1, 128, 2)))])
+        ts(r("ON"), x0(0, 64), float(E), A.add, 1024.0, A.min)
+        if GMG[t] == "V":
+            tt(r("GM"), ind(LSW, r("ON")), r("MASK", (t, t + 1024)), A.mult)
+        else:
+            act(r("AP", 0), ind(LSW, r("ON")), F.Identity, scale=1 / 2048)
+            for h in range(2):
+                mm([((x0, x1)[h](k, 512, 8), r("SEL", (k + t) % 8), r("AP", 0, (512 * h + k, 512 * h + 512, 8))) for k in range(8)])
+                act(r("GM", (512 * h, 512 * h + 512)), (X0, X1)[h], F.Identity, scale=oh(0))
+        act(r("EQ"), LSW, F.Relu, bias=1.0, scale=2.0)
+        mm([(x1(0, 128), mx(TRI), r("EQ", (rho, 1024, 8)))])
         act(r("FV"), x1(0, 128), F.Relu)
         mm([(x0(0, 64), r("WC", (15 - i, 143 - i)), r("GM", (i, 1024, 16))) for i in range(16)])
         ts(r("OX"), x0(0, 64), float(E), A.add, 1023.0, A.min)
         ts(r("OC"), x0(0, 64), float(E), A.add)
         for h in range(2):
             o = (32 * h, 32 * h + 32)
-            for c in range(2):
-                act(ua(c), ind(r("UW", c, (0, 1024)), r("OA", t, o)), F.Identity)
             neg = S1G[t][h] == "S"
+            if h == 0 or not PAR[t]:
+                ua, ds = [[r("WB", (a, a + 4)), r("WB", (a + 4, a + 8)), r("WB", (a, a + 8))] for a in (0, 8)]
+                ex, ey, at = ds[0], ds[1], 12
+                d1, mb, cm = r("D1"), r("MB"), r("CM")
+                y0, y1 = x0, x1
+            else:
+                ua, ds = [[r("AP", a, (0, 512)), r("AP", a, (512, 1024)), r("AP", a)] for a in (0, 1)]
+                ex, ey, at = r("WB", (0, 4)), r("WB", (4, 8)), 4
+                d1, mb, cm = r("NZ", 0, (0, 2)), r("NZ", 0, (2, 4)), r("NZ", 1, (0, 2))
+                y0, y1 = [lambda a, b, s=1, z=z: r("UL", z, (a, b, s)) for z in range(2)]
+            Y0, Y1 = y0(0, 512), y1(0, 512)
+            byt = S1G[t][h] == "T"
+            if byt and (h == 0 or not PAR[t]):
+                ua, ds = [[r("G1", a), r("G1", a + 1)] for a in (0, 2)]
+            if byt and (h == 0 or S1G[t][0] != "T"):
+                act(r("UA"), r("UW", None, (rho, 1024, 8)), F.Identity, scale=-1.0)
             for c in range(2):
+                act(ua[c], ind(r("UW", c, (0, 1024)), r("OX", o) if byt else r("OA", t, o)), F.Identity, scale=-1.0 if neg else 1.0)
+            for c in range(0 if byt else 2):
                 if neg:
-                    act(ds(c), ind(r("UW", c, (0, 1024)), r("OX", o)), F.Identity, scale=-1.0)
+                    act(ds[c], ind(r("UW", c, (0, 1024)), r("OX", o)), F.Identity)
                 else:
-                    tt(ds(c), ind(r("UW", c, (0, 1024)), r("OX", o)), ua(c), A.subtract)
+                    tt(ds[c], ind(r("UW", c, (0, 1024)), r("OX", o)), ua[c], A.subtract)
             if neg:
-                dma("g", [(ds(), ua())], acc=True)
-            act(r("D1"), ind(r("PW"), r("OC", o)), F.Identity)
+                dma("g", [(ds[2], ua[2])], acc=True)
+            act(d1, ind(r("PW"), r("OC", o)), F.Identity)
             gm = r("GM", (512 * h, 512 * h + 512))
-            mm([(X1, mx(BLK), gm)] + [(x1(k, 512, 8), mx(NI), r("U16", (64 * h, 64 * h + 64))) for k in range(8)])
-            if MBS:
-                act(X1, X1, F.Square)
-                act(r("MB"), X1, F.Relu, bias=1.0, scale=-1.0)
+            mm([(Y1, mx(BLK), gm)] + [(y1(k, 512, 8), mx(ND8), r("U16", (64 * h, 64 * h + 64))) for k in range(8)])
+            act(mb, Y1, F.Sign, bias=col(23))
+            mm([(Y0, mx(IB_), d1)] +
+               [(y0(k, 512, 8), mx(IB_), r("PO", (512 * h + rho, 512 * h + 512, 8))) for k in range(8)])
+            act(d1, Y0, F.Square)
+            mm([(Y0, mx(DXP), d1)])
+            mm([(Y1, mx(DYP), d1)])
+            for c in range(2 if byt else 0):
+                y = (y0, y1)[c]
+                act(ds[c], y(0, 512), F.Identity)
+                mm([(y(0, 512), mx(IB_), ua[c])] + [(y(k, 512, 8), mx(IB_), r("UA", c, (64 * h, 64 * h + 64))) for k in range(8)])
+            tt(ex, ds[0], Y0, A.mult)
+            if S1Z[t][h] == "V":
+                tt(Y1, ds[1], Y1, A.mult)
+                tt(ex, ex, Y1, A.add)
+                act(ex, ex, F.Abs)
+            elif S1Z[t][h] == "D":
+                tt(ey, ds[1], Y1, A.mult)
+                dma("g", [(ex, ey)], acc=True)
+                act(ex, ex, F.Abs)
             else:
-                ts(r("MB"), X1, 0.0, A.is_equal)
-            mm([(X0, mx(IB_), r("D1"))] +
-               [(x0(k, 512, 8), mx(NI), r("PO", (512 * h + rho, 512 * h + 512, 8))) for k in range(8)])
-            act(r("D1"), X0, F.Square)
-            mm([(X0, mx(DXN if neg else DXP), r("D1"))])
-            mm([(X1, mx(DYN if neg else DYP), r("D1"))])
-            tt(ds(0), ds(0), X0, A.mult)
-            if S1Z[t] == "V":
-                tt(X1, ds(1), X1, A.mult)
-                tt(ds(0), ds(0), X1, A.add)
-                act(ds(0), ds(0), F.Abs)
-            elif S1Z[t] == "D":
-                tt(ds(1), ds(1), X1, A.mult)
-                dma("g", [(ds(0), ds(1))], acc=True)
-                act(ds(0), ds(0), F.Abs)
+                tt(ey, ds[1], Y1, A.mult)
+                mm([(Y0, I32, ex)], True, False)
+                mm([(Y0, I32, ey)], False, True)
+                act(ex, Y0, F.Abs)
+            if S1C[t][h] == "S":
+                mm([(Y1, mx(NMT), d1), (Y1, I32, ex)])
+                act(cm, Y1, F.Sign, bias=-0.5)
             else:
-                tt(ds(1), ds(1), X1, A.mult)
-                mm([(X0, I32, ds(0))], True, False)
-                mm([(X0, I32, ds(1))], False, True)
-                act(ds(0), X0, F.Abs)
-            if CMS:
-                mm([(X1, mx(NMT), r("D1")), (X1, I32, ds(0))])
-                act(r("CM"), X1, F.Sign, bias=-0.5)
-            else:
-                mm([(X1, mx(MT), r("D1"))])
-                tt(r("CM"), ds(0), X1, A.is_gt)
-            mm([(X0, mx(BLK), gm), (X0, mx(KC), r("MASK", (0, 512))), (X0, mx(BD0 + t), r("D1")), (X0, mx(NBG), r("MB"))] +
-               [(x0(k, 512, 8), mx(PBG), r("FV", (64 * h, 64 * h + 64))) for k in range(8)] + [(X0, mx(SCO), r("CM"))])
-            act(r("RS8", (0, 512, 8)), r("DUM", (64 * h, 64 * h + 64)), F.Identity, bias=71.0 * 2048)
-            scan(ds(1), r("RS8"), X0, 1e9, A.min, A.max)
-            cp(r("NBI", h), r("WB", (1543, 2048, 8), raw=True))
+                mm([(Y1, mx(MT), d1)])
+                tt(cm, ex, Y1, A.is_gt)
+            mm([(Y0, mx(BLK), gm), (Y0, mx(KC), r("MASK", (0, 512))), (Y0, mx(BD0 + t), d1), (Y0, mx(NBG), mb)] +
+               [(y0(k, 512, 8), mx(PBG), r("FV", (64 * h, 64 * h + 64))) for k in range(8)] +
+               [(Y0, mx(SC2 if S1C[t][h] == "S" else SCO), cm)])
+            scan(ey, r("RS8"), Y0, 0.0, A.mult, A.max)
+            tt(r("NBI", h), r("WB", (128 * at + 7, 128 * at + 512, 8), raw=True), r("DK", int(S1C[t][h] == "S"), (64 * h, 64 * h + 64)), A.max)
+        up[0] = UP2[t]
         nm = r("NBI", (2, 4))
         ts(nm, r("NBI", (0, 2)), 2047, A.bitwise_and)
         tt(r("S1"), nm, r("DIAG"), A.mult)
         cp(r("NF"), nm)
         scan(r("SCN"), r("RS16"), r("S1"), 0.0, A.mult, A.add)
         ts(r("OM"), r("SCN", (15, 128, 16)), -1.0, A.add)
-        ts(r("EV"), ind(LSW, r("OM")), 0.0, A.is_equal)
-        mm([(x1(0, 128), mx(TRI), r("EV"))])
+        lin(EVG, r("EV"), ind(r("EQ"), r("OM")), 1.0, 0.0)
+        mm([(x0(128, 256), mx(TRI), r("EV"))])
         ms(r("GM", (0, 1)), 0.0)
         tt(r("GM", (1, 128)), r("NF", (1, 128)), r("SCN", (0, 127)), A.is_equal)
         act(r("GM", (128, 256)), r("NF"), F.Relu, bias=-1024.0)
@@ -435,7 +521,7 @@ def build():
             ts(r("GM", (at, at + 128 - a)), r("NF", (a, 128)), r("SCN", (a - 1, a)), A.is_equal)
             terms.append((x0(a, 128), mx(NON), r("GM", (at, at + 128 - a))))
             at += 128 - a
-        act(r("FC"), x1(0, 128), F.Relu)
+        act(r("FC"), x0(128, 256), F.Relu)
         tt(r("DF"), r("S1"), r("DUMM"), A.subtract)
         mm(terms + [(x0(0, 128), mx(BLK), r("FC"))])
         act(x0(0, 128), x0(0, 128), F.Relu)
@@ -443,27 +529,28 @@ def build():
         act(r("SE", (128 * t, 128 * t + 128)), x0(0, 128), F.Identity, bias=oh(15), scale=col(12))
         scan(r("SC2"), r("RS16"), r("S2"), 0.0, A.mult, A.add)
         tt(r("S2", (0, 8)), r("SC2", (15, 128, 16)), r("MD", (15, 128, 16)), A.add)
-        ts(r("OT", t), r("S2", (0, 8)), -1.0, A.add)
+        ts(ot(t), r("S2", (0, 8)), -1.0, A.add)
         de = r("DE", (128 * t, 128 * t + 128))
-        tt(de, ind(r("PW"), r("OT", t)), r("PO", (rho, 1024, 8)), A.subtract)
+        tt(de, ind(r("PW"), ot(t)), r("PO", (rho, 1024, 8)), A.add)
         act(de, de, F.Square)
         if t < 2:
             act(r("S1"), r("NF"), F.Identity, bias=-1.0 - E)
             tt(r("OVV", t), r("S1"), r("FV"), A.mult)
             tt(r("OVC", t), r("VID", t), r("FC"), A.mult)
 
-    def extras(t):
-        n = t + 1
-        w = (0, 128 * n)
-        dma("y", [(r("XACC", None, (0, 1024)), r("BASE"))])
-        ex, ey, ez = r("WB", (0, n)), r("WB", (4, 4 + n)), r("WB", (8, 8 + n))
-        bx, by = x0(*w), x1(*w)
-        de, se, qe, en, et, eq = [r(x, w) for x in ("DE", "SE", "QE", "MB", "D1", "CM")]
-        for b in range(n):
-            for c in range(2):
-                e = r("WB", 4 * c + b)
-                act(e, r("UW", c, (7 - b, 1024, 8)), F.Identity)
-                tt(e, ind(r("UW", c, (0, 1152)), r("OT", b)), e, A.subtract)
+    def ec(t, lo, hi):
+        return r("EC", (64 * t * (t + 1) + 128 * lo, 64 * t * (t + 1) + 128 * hi))
+
+    def extras(t, lo, hi, banks):
+        w = (128 * lo, 128 * hi)
+        ex, ey, ez = r("WX", 0, w), r("WX", 1, w), r("WX", 2, w)
+        bx, by = banks
+        de, se, qe, en, et = [r(x, w) for x in ("DE", "SE", "QE", "EN", "ET")]
+        eq = ec(t, lo, hi)
+        for b in range(lo, hi):
+            act(r("WX", (0, 2), (128 * b, 128 * b + 128)), r("UW", None, (7 - b, 1024, 8)), F.Identity)
+        for c in range(2):
+            tt(r("WX", c, w), ind(r("UW", c, (0, 1152)), r("OT", (8 * lo, 8 * hi))), r("WX", c, w), A.subtract)
         mm([(bx, mx(DXP), de)])
         mm([(by, mx(DYP), de)])
         tt(ex, ex, bx, A.mult)
@@ -485,24 +572,34 @@ def build():
         tt(ex, qe, bx, A.mult)
         mm([(by, mx(PY_), de)])
         tt(ey, qe, by, A.mult)
-        tt(r("AE", w), r("AE", w), eq, A.add)
-        for b in range(n):
-            for c, tmp in ((0, "S1"), (1, "SCN")):
-                pe = r("WB", 4 * c + b)
-                own = r("XACC", c, (7 - b, 1024, 8))
-                tt(own, own, pe, A.add)
-                tt(r(tmp), ind(r("XACC", c), r("OT", b)), pe, A.subtract)
-                cp(ind(r("XACC", c), r("OT", b)), r(tmp))
-        if t == 2:
-            act(r("LS", (0, 1024)), r("MASK", (0, 1024)), F.Identity, scale=0.0)
-            for b in range(3):
-                ae = r("AE", (128 * b, 128 * b + 128))
+
+    def ot(b):
+        return r("OT", (8 * b, 8 * b + 8))
+
+    def ends(t, lo, hi):
+        for b in range(lo, hi):
+            bs = (128 * b, 128 * b + 128)
+            own = r("XACC", None, (7 - b, 1024, 8))
+            tt(own, own, r("WX", (0, 2), bs), A.add)
+            for c in range(2):
+                tmp = (r("WX", 2, bs), r("SC2"))[c]
+                tt(tmp, ind(r("XACC", c), ot(b)), r("WX", c, bs), A.subtract)
+                cp(ind(r("XACC", c), ot(b)), tmp)
+            if t == 2:
+                if b == 0:
+                    act(r("LS", (0, 1024)), r("MASK", (0, 1024)), F.Identity, scale=0.0)
+                ae = ec(2, b, b + 1)
+                if b < 2:
+                    x = r("CNT", 3)
+                    mm([(x, mx(IB_), ec(u, b, b + 1)) for u in range(b, 3)])
+                    ae = r("MD" if b else "DUMM")
+                    act(ae, x, F.Identity)
                 own = r("LS", (7 - b, 1024, 8))
-                tt(r("S1"), ind(r("WW"), r("OT", b)), ae, A.mult)
-                tt(r("SCN"), r("WW", (7 - b, 1024, 8)), ae, A.mult)
-                tt(own, own, r("S1"), A.add)
-                tt(r("S2"), ind(r("LS"), r("OT", b)), r("SCN"), A.add)
-                cp(ind(r("LS"), r("OT", b)), r("S2"))
+                tt(r("WX", 0, bs), ind(r("WW"), ot(b)), ae, A.mult)
+                tt(r("WX", 1, bs), r("WW", (7 - b, 1024, 8)), ae, A.mult)
+                tt(own, own, r("WX", 0, bs), A.add)
+                tt(r("WX", 2, bs), ind(r("LS"), ot(b)), r("WX", 1, bs), A.add)
+                cp(ind(r("LS"), ot(b)), r("WX", 2, bs))
 
     def rows_update(t):
         for b in range(t + 1):
@@ -511,24 +608,48 @@ def build():
             tt(r("S2"), r("OVV", b), se, A.mult)
             tt(r("SC2"), r("OVC", b), se, A.mult)
             tt(own, own, r("S2"), A.add)
-            tt(r("S2"), ind(r("LS"), r("OT", b)), r("SC2"), A.add)
-            cp(ind(r("LS"), r("OT", b)), r("S2"))
+            tt(r("S2"), ind(r("LS"), ot(b)), r("SC2"), A.add)
+            cp(ind(r("LS"), ot(b)), r("S2"))
 
-    def tile(name, q, j):
-        return r(name, q, (j, SCRATCH[name][1][2], 16), raw=True)
+    def blocks(sp):
+        q, kh = divmod(sp, 2)
+        if q not in TALL:
+            return [(4 * kh + m, 256 * q, 256 * m, 256) for m in range(4)]
+        return [(k, 256 * q + 128 * kh, 128 * k, 128) for k in range(8)]
+
+    def unit(q, h):
+        return q + sum(x < q for x in TALL) + (h if q in TALL else 0)
+
+    def tile(q, j):
+        if q not in TALL:
+            return r("QC", q, (j, 2048, 16), raw=True)
+        return r("QC", q, (1024 * (j // 8) + j % 8, 1024 * (j // 8) + 1024, 8), raw=True)
+
+    def onb(sp, a=0, w=1024):
+        return r("ONB", (64 * sp + a // 16, 64 * sp + (a + w) // 16))
 
     def positions(sp):
         q, kh = divmod(sp, 2)
-        dd = r("DD", q, (4 * kh, 4 * kh + 4))
-        lin(DMODE[sp], dd, ind(r("PW"), r("ONB", (64 * sp, 64 * sp + 64))), -1.0, 0.0)
-        dma("g", [(dd, r("AB", 4 + q))], acc=True)
-        act(dd, dd, F.Square)
+        dd = r("QC", q, (4 * kh, 4 * kh + 4))
+        js = (256 * q, 256 * q + 256)
+        lin(DMODE[sp], dd, ind(r("PW"), onb(sp)), 1.0, 0.0)
         if kh == 1:
-            mm([(r("CNT", (0, 2), (8 * j, 8 * j + 8)), tile("DD", q, j), r("MX", (PX_, PY_ + 1), (0, 128, 16)))
-                for j in range(16)] +
-               [(r("CNT", (2, 4)), r("W2", (7 - k, 135 - k)), r("DD", q, k)) for k in range(8)])
-            act(r("AT", (q, 8, 4)), r("CNT", (0, 2)), F.Identity)
-            act(r("D2", (256 * q, 256 * q + 256)), r("CNT", (2, 4)), F.Identity)
+            lo, hi = r("XS", 0), r("XS", 1)
+            pt = r("AB", 4, js, p=(0, 16))
+            mm([(r("CNT", (0, 2), (8 * j, 8 * j + 8), p=(0, 16)),
+                 r("PO", (256 * q + 128 * (j // 8) + j % 8, 256 * q + 128 * (j // 8) + 128, 8) if q in TALL else (256 * q + j, 256 * q + 256, 16)),
+                 r("PL")) for j in range(16)])
+            act(pt, r("CNT", (0, 2), p=(0, 16)), F.Identity)
+            mm([(hi, mx(OW), r("PO", js))] +
+               [(r("XS", 1, (v % 256, v % 256 + w)), r("W2", (7 - k, 135 - k)),
+                 r("QC", q, (1024 * h + a, 1024 * h + a + w), raw=True)) for h in range(2) for k, v, a, w in blocks(2 * q + h)])
+            act(r("EC", (384, 640)), hi, F.Square, scale=2048.0)
+            act(r("D2", js), hi, F.Identity)
+            mm([(lo, mx(D8), r("EC", (384, 640))), (lo, mx(QE8), r("EQ", js))])
+            act(r("TT", js), lo, F.Identity, scale=col(25))
+            mm([(r("CNT", (2, 4)), r("MX", D16, p=(0, 16)), pt)] +
+               [(r("CNT", (2, 4), (8 * j, 8 * j + 8)), tile(q, j), r("PL")) for j in range(16)])
+            act(r("AT", (q, 8, 4)), r("CNT", (2, 4)), F.Identity)
             if q % 2:
                 u = q - 1
                 dma("y", [(r("DM", c, j, (128 * u, 128 * u + 256), p=(j, 128, 16)),
@@ -536,147 +657,251 @@ def build():
 
     def forces(t, sp):
         q, kh = divmod(sp, 2)
-        b = sp % 2
-        if kh == 0:
-            own = r("UR", q % 2, None, (0, 256))
-            act(own, r("UW", None, (256 * q, 256 * q + 256)), F.Identity, bias=-RND)
-            dma("y", [(r("UR", q % 2, None, (256 * k, 256 * k + 256)), own) for k in range(1, 4)])
+        b, bg, be = sp % 2, (8 * t + sp) % NG, (8 * t + sp) % NE
+        js = (256 * q, 256 * q + 256)
+        bl = blocks(sp)
+        ur = (NU * t + unit(q, kh)) % NR
+        if kh == 0 or q in TALL:
+            v, w = bl[0][1], bl[0][3]
+            lin(OWN[t][q], r("UR", ur, None, (0, w)), r("UW", None, (v, v + w)), -1.0, 0.0)
+            if FAST[t][q] == "F":
+                dma("y", [(r("UR", ur, None, (a, a + w)), r("UR", ur, None, (0, w))) for a in range(w, 1024, w)])
+            while w < 1024 and FAST[t][q] != "F":
+                dma("y", [(r("UR", ur, None, (w, 2 * w)), r("UR", ur, None, (0, w)))])
+                w *= 2
         how = GMODE[t][2 * sp:2 * sp + 2]
-        if "F" in how and (kh == 0 or "F" not in GMODE[t][2 * sp - 2:2 * sp]):
-            dma("y", [(r("UF"), r("UW", None, (256 * q, 256 * q + 256)))])
         for c in range(2):
-            if how[c] == "F":
-                for k in range(4):
-                    tt(r("G", b, c, (256 * k, 256 * k + 256)), ind(r("UW", c), r("ONB", (64 * sp + 16 * k, 64 * sp + 16 * k + 16))),
-                       r("UF", c), A.subtract)
+            if how[c] == "R":
+                tt(r("G", bg, c), ind(r("UW", c), onb(sp)), r("UR", ur, c), A.add)
+            elif how[c] == "F":
+                for k, v, a, w in bl:
+                    tt(r("G", bg, c, (a, a + w)), ind(r("UW", c), onb(sp, a, w)), r("UR", ur, c, (0, w)), A.add)
             else:
-                lin(how[c], r("G", b, c), ind(r("UW", c), r("ONB", (64 * sp, 64 * sp + 64))), -1.0, RND)
-        if how != "FF":
-            cs = (int(how[0] == "F"), 2 - int(how[1] == "F"))
-            dma("g", [(r("G", b, cs), r("UR", q % 2, cs))], acc=True)
-        for h in range(2):
-            hs, dd = (512 * h, 512 * h + 512), r("DD", q, (4 * kh + 2 * h, 4 * kh + 2 * h + 2))
-            mm([(r("DXY", 0), mx(DXP if how[0] == "F" else DXN), dd)])
-            mm([(r("DXY", 1), mx(DYP if how[1] == "F" else DYN), dd)])
-            if EADD[t][sp] == "V":
-                tt(r("EE", b, 0, hs), r("G", b, 0, hs), r("DXY", 0), A.mult)
-                tt(r("DXY", 1), r("G", b, 1, hs), r("DXY", 1), A.mult)
-                tt(r("EE", b, 0, hs), r("EE", b, 0, hs), r("DXY", 1), A.add)
+                lin(how[c], r("G", bg, c), ind(r("UW", c), onb(sp)), 1.0, 0.0)
+        cs = (int(how[0] in "FR"), 2 - int(how[1] in "FR"))
+        if cs[0] < cs[1]:
+            dma("g", [(r("G", bg, cs), r("UR", ur, cs))], acc=True)
+        for c in range(2):
+            for h in range(2):
+                mm([(r("DXY", h, (a % 512, a % 512 + w)), r("SEL", 8 * c + k), r("D2", (v, v + w))) for k, v, a, w in bl if a // 512 == h])
+            if EADD[t][sp] == "V" and c:
+                tt(r("DXY"), r("G", bg, c), r("DXY"), A.mult)
+                tt(r("EE", be), r("EE", be), r("DXY"), A.add)
             else:
-                tt(r("EE", b, None, hs), r("G", b, None, hs), r("DXY"), A.mult)
+                tt(r("EE", (be, 3 + b)[c]), r("G", bg, c), r("DXY"), A.mult)
         if EADD[t][sp] != "V":
-            dma("g", [(r("EE", b, 0), r("EE", b, 1))], acc=True)
-        for h in range(2):
-            hs, ks = (512 * h, 512 * h + 512), (4 * kh + 2 * h, 4 * kh + 2 * h + 2)
-            dd, qc, e, m = r("DD", q, ks), r("QC", q, ks), r("EE", b, 0, hs), r("EE", b, 1, hs)
-            for x, mt in ((r("UB"), MT), (r("LB"), NMT)):
-                mm([(x, mx(mt), dd)] + ([(x, mx(NI), qc)] if t else []))
-            tt(m, e, r("UB"), A.min)
-            tt(r("LB"), m, r("LB"), A.max)
-            tt(qc, e, r("LB"), A.subtract)
-        qc = r("QC", q, (4 * kh, 4 * kh + 4))
-        ts(r("NZ", b), qc, 0.0, A.not_equal)
-        ts(qc, qc, -1023.0, A.max, 1023.0, A.min)
-        first = [(r("CNT", (0, 3)), mx(I16), r("SC", (t + 1) % 2, q))] if t and kh == 0 else []
-        mm(first + [(r("CNT", (1, 3)), r("C2", (7 - 4 * kh - k, 135 - 4 * kh - k)), r("NZ", b, k)) for k in range(4)] +
-           [(r("CNT", 0, (64 * kh, 64 * kh + 64)), r("WC", (15 - j, 143 - j)), tile("NZ", b, j)) for j in range(16)],
-           kh == 0, kh == 1)
+            dma("g", [(r("EE", be), r("EE", 3 + b))], acc=True)
+        qc, e, m, ap = r("QC", q, (4 * kh, 4 * kh + 4)), r("EE", be), r("EE", 3 + b), r("AP", b)
+
+        def bound(s):
+            for h in range(2):
+                ks = (4 * kh + 2 * h, 4 * kh + 2 * h + 2)
+                mm([(r("UL", h, (a % 512, a % 512 + w)), r("SEL", 8 * s + k), r("TT", (v, v + w))) for k, v, a, w in bl if a // 512 == h] +
+                   ([(r("UL", h), mx(NI), r("QC", q, ks))] if t else []))
+        bound(0)
+        if CLIP[t][sp] == "D":
+            tt(ap, e, r("UL"), A.subtract)
+            bound(1)
+            ts(ap, ap, 0.0, A.max, 1023.0, A.min)
+            tt(qc, e, r("UL"), A.subtract)
+            ts(qc, qc, 0.0, A.min, -1023.0, A.max)
+            dma("g", [(qc, ap)], acc=True)
+        else:
+            tt(m, e, r("UL"), A.min)
+            bound(1)
+            tt(r("UL"), m, r("UL"), A.max)
+            tt(qc, e, r("UL"), A.subtract)
+        if MARK[t][sp] == "S":
+            act(r("NZ", b), qc, F.Sign)
+            act(r("NZ", b), r("NZ", b), F.Abs)
+        else:
+            ts(r("NZ", b), qc, 0.0, A.not_equal)
+        if CLIP[t][sp] != "D":
+            ts(qc, qc, -1023.0, A.max, 1023.0, A.min)
+        tall = q in TALL
+        first = [(r("CNT", 0), mx(I16), r("SC", (t + 1) % 2, unit(q, kh)))] if t and (kh == 0 or tall) else []
+        if tall:
+            sa = [(r("CNT", 0), r("WC", (15 - 8 * kh - j, 143 - 8 * kh - j)), r("NZ", b, (j, 1024, 8), raw=True)) for j in range(8)]
+        else:
+            sa = [(r("CNT", 0, (64 * kh, 64 * kh + 64)), r("WC", (15 - j, 143 - j)), r("NZ", b, (j, 1024, 16), raw=True))
+                  for j in range(16)]
+        mm(first + sa + [(r("CNT", (1, 1 + w // 128)), r("C2", (7 - k, 135 - k)), r("NZ", b, (a, a + w), raw=True)) for k, v, a, w in bl],
+           kh == 0 or tall, kh == 1 or tall)
 
     def atile(q, j):
-        return r("AB", 2 * q + j // 8, j % 8 // 2, (128 * (j % 2), 128 * (j % 2) + 128))
+        return r("AB", 2 * q + j // 8, (128 * (j % 8), 128 * (j % 8) + 128))
 
-    def sums(t, q):
+    def sums(t, q, h=None):
         js = (256 * q, 256 * q + 256)
-        sa, sb = r("SC", t % 2, q, (0, 128)), r("SC", t % 2, q, (128, 384))
-        act(r("SC", t % 2, q), r("CNT", (0, 3)), F.Sigmoid, bias=-256.0 * (19.5 if t else 3.5), scale=256.0)
-        tt(r("SD"), sb, r("D2", js), A.mult)
-        mm([(r("X1", (0, 2)), mx(CX), r("SD")), (r("X1", (2, 4)), mx(CY), r("SD"))], True, False)
+        vs = js if h is None else (256 * q + 128 * h, 256 * q + 128 * h + 128)
+        u = unit(q, h)
+        sa, sb = r("SC", t % 2, u), r("CNT", (1, 3 if h is None else 2))
+        act(sa, r("CNT", 0), F.Sigmoid, bias=-256.0 * (19.5 if t else 3.5), scale=256.0)
+        act(sb, sb, F.Sigmoid, bias=-256.0 * 3.5, scale=256.0)
+        tt(r("D2", vs), r("D2", vs), sb, A.mult)
+        X1 = r("XS")
+        s = r("XACC", None, js)
+        cs = (vs[0] % 256, (vs[1] - 1) % 256 + 1)
+        off = [(r("XS", 0, cs), mx(CX), r("D2", vs)), (r("XS", 1, cs), mx(CY), r("D2", vs))]
+        half = (r("XS", 0), mx(C64), r("MASK", (0, 256)))
+        byv = q < EARLY[t] or (FIN[t][q] in "VSA" and q < 3)
+        if not h:
+            mm([(X1, I32, s), half] if q == 3 else off, True, False)
         if t < 2:
-            tt(r("LS", js), r("LS", js), sb, A.mult)
+            tt(r("LS", vs), r("LS", vs), sb, A.mult)
         if t:
-            mm([(r("CNT", 3), mx(IB_), sa), (r("CNT", 3), mx(IB_), r("SC", 0, q, (0, 128)) if t == 1 else r("SS", q))])
-            act(r("SS", q), r("CNT", 3), F.Identity, bias=0.0 if t == 1 else -1.5, scale=1.0 if t == 1 else 0.5)
-        for b in range(4):
+            mm([(r("CNT", 3), mx(IB_), sa), (r("CNT", 3), mx(IB_), r("SC", 0, u) if t == 1 else r("SS", u))])
+            act(r("SS", u), r("CNT", 3), F.Identity, bias=0.0 if t == 1 else -1.5, scale=1.0 if t == 1 else 0.5)
+        for b in range(4) if h is None else (2 * h, 2 * h + 1):
             tr = TRB[t][q == 3][b % 2]
             mm([(r(tr), sa, r("SEL", (4 * b, 4 * b + 4)))] +
-               [(r(tr, j), tile("QC", q, 4 * b + j), mx(IB_)) for j in range(4)])
-            qs = r("QS", (16 * b, 16 * b + 16), (0, 3, 2))
+               [(r(tr, j), tile(q, 4 * b + j), mx(IB_)) for j in range(4)])
+            qs = r("QS", (16 * (b % 2), 16 * (b % 2) + 16), (0, 3, 2))
             if EVAC[t][4 * q + b] == "S":
                 act(qs, r(tr), F.Relu, bias=-1024.0)
             else:
                 ts(qs, r(tr), -1024.0, A.add, 0.0, A.max)
             terms = []
             for j in range(4 * b, 4 * b + 4):
+                cs = (j, 256, 16) if h is None else (128 * h + j % 8, 128 * h + 128, 8)
                 for gg in range(8):
                     pr, odd = divmod(gg, 2)
-                    terms.append((r("X1", (j, 512, 16), p=(32 * pr, 32 * pr + 32), raw=True),
-                                  r("QS", 4 * j + pr, (odd, odd + 2)), r("DM", None, None, 128 * q + 8 * j + gg)))
+                    terms.append((r("XS", None, cs, p=(32 * pr, 32 * pr + 32)),
+                                  r("QS", 4 * (j % 8) + pr, (odd, odd + 2)), r("DM", None, None, 128 * q + 8 * j + gg)))
             mm(terms, False, False)
             if b % 2:
                 out = r("AB", 2 * q + b // 2) if t == 0 else r("AT", (4 * b - 4, 4 * b + 4))
-                act(out, r("QS", (16 * b - 16, 16 * b + 16), (0, 3, 2)), F.Abs, bias=-1024.0)
+                act(out, r("QS", None, (0, 3, 2)), F.Abs, bias=-1024.0)
         if t == 1:
-            dma("g", [(r("AB", (2 * q, 2 * q + 2)), r("AT"))], acc=True)
-        s = r("XACC", None, js)
-        mm([(X1, I32, s)], False, True)
-        tt(s, r("UW", None, js), X1, A.add)
+            dma("g", [(r("AB", (2 * q, 2 * q + 2)), r("AT")) if h is None else (r("AB", 2 * q + h), r("AT", (8 * h, 8 * h + 8)))], acc=True)
+        plain = FIN[t][q] == "Q" and not byv
+        mm(off if q == 3 else [half] + [(X1, I32, s)] * plain, False, byv or (plain and h != 0))
+        if h == 0:
+            return
+        if byv:
+            tt(s, s, X1, A.add)
+            if q >= EARLY[t]:
+                close(s, FIN[t][q])
+        elif plain:
+            ts(s, X1, RND, A.add, RND - 1023.0, A.max)
+            ts(r("UW", None, js) if t < 2 and q == 3 else s, s, RND + 1023.0, A.min, RND, A.subtract)
+        else:
+            mm(([(X1, I32, s)] if q < 3 else []) +
+               [(X1, mx(RN), r("MASK", (0, 512))), (X1, mx(NRN), r("MASK", (0, 512)))], False, True)
+            out = r("UW", None, js) if t < 2 and q == 3 else s
+            if CUT[t][q] == "S":
+                cut(out, X1, 0.0)
+            else:
+                ts(out, X1, -1023.0, A.max, 1023.0, A.min)
+
+    def cut(s, x, off):
+        act(s, x, F.Relu, bias=1023.0 - off)
+        act(s, s, F.Relu, bias=2046.0, scale=-1.0)
+        act(s, s, F.Identity, bias=1023.0, scale=-1.0)
+
+    def close(s, how):
+        if how == "V":
+            ts(s, s, RND, A.add, RND - 1023.0, A.max)
+            ts(s, s, RND + 1023.0, A.min, RND, A.subtract)
+        elif how == "S":
+            act(s, s, F.Identity, bias=RND)
+            ts(s, s, RND + 1023.0, A.min, RND - 1023.0, A.max)
+            act(s, s, F.Identity, bias=-RND)
+        else:
+            act(s, s, F.Identity, bias=RND)
+            cut(s, s, RND)
 
     def update(t, q):
         js = (256 * q, 256 * q + 256)
-        s = r("XACC", None, js)
-        ts(r("UW", None, js) if t < 2 else s, s, RND - 1023.0, A.max, RND + 1023.0, A.min)
-        if t == 2:
-            act(s, s, F.Identity, bias=-RND)
+        if t < 2:
+            dma("y", [(r("UW", None, (0, 768)), r("XACC", None, (0, 768)))])
+        else:
             dma("y", [(hbm(("yx", "yy")[c], slice(None), slice(*js)), r("XACC", c, js)) for c in range(2)])
 
     def weights(q):
         js = (256 * q, 256 * q + 256)
-        wg = ("BASE", "WB")[q % 2]
+
+        def wg(kh, a, b):
+            return r("UW", kh, (a, b))
+
+        def back(out, j, u, ks):
+            return [(out, r("SEL", j), r("SS", u, ks)), (out, atile(q, j), r("MX", IB_, ks)), (out, r("AT", j), r("MX", IB_, ks))]
+        w = WBUF[q]
         for kh in range(2):
-            o = r("ONB", (128 * q + 64 * kh, 128 * q + 64 * kh + 64))
-            lin(WMODE[2 * q + kh], r(wg, (8 * kh, 8 * kh + 8)), ind(r("WW"), o), 1.0, 0.0)
-            ks = (64 * kh, 64 * kh + 64)
+            out = wg(kh, 0, 1024) if q == 3 else r(w, (8 * kh, 8 * kh + 8))
+            lin(WMODE[2 * q + kh], out, ind(r("WW"), onb(2 * q + kh)), 1.0, 0.0)
+            if q == 3:
+                vs, x = (768 + 128 * kh, 896 + 128 * kh), r("UL", kh, (0, 128))
+                for h in range(2):
+                    mm([y for j in range(8 * kh, 8 * kh + 8)
+                        for y in back(r("DXY", h, (j % 8, 512, 8)), j, unit(q, kh), (64 * h, 64 * h + 64))])
+                    tt(wg(kh, 512 * h, 512 * h + 512), wg(kh, 512 * h, 512 * h + 512), r("DXY", h), A.mult)
+                    if WT3[kh] == "P":
+                        mm(([] if h else [(x, I32, r("LS", vs))]) +
+                           [(x, I32, wg(kh, 128 * k, 128 * k + 128)) for k in range(4 * h, 4 * h + 4)], h == 0, h == 1)
+                    else:
+                        a = 512 * h
+                        tt(wg(kh, a, a + 256), wg(kh, a, a + 256), wg(kh, a + 256, a + 512), A.add)
+                        tt(wg(kh, a, a + 128), wg(kh, a, a + 128), wg(kh, a + 128, a + 256), A.add)
+                        tt(r("LS", vs), r("LS", vs), wg(kh, a, a + 128), A.add)
+                if WT3[kh] == "P":
+                    act(r("LS", vs), x, F.Identity)
+                dma("s", [(hbm("yw", slice(None), slice(*vs)), r("LS", vs))])
+                continue
             for h in range(2):
-                terms = []
-                for j in range(h, 16, 2):
-                    out = x0(j // 2, 512, 8)
-                    terms += [(out, r("SEL", j), r("SS", q, ks)), (out, atile(q, j), r("MX", IB_, ks)),
-                              (out, r("AT", j), r("MX", IB_, ks))]
-                mm(terms)
-                x = r(wg, (1024 * kh + h, 1024 * kh + 1024, 2), raw=True)
+                mm([x for j in range(h, 16, 2) for x in back(x0(j // 2, 512, 8), j, unit(q, 0), (64 * kh, 64 * kh + 64))])
+                x = r(w, (1024 * kh + h, 1024 * kh + 1024, 2), raw=True)
                 tt(x, x, X0, A.mult)
-            if WTREE[q] == "P":
-                x = r("TR", (0, 2))
-                mm(([(x, I32, r("LS", js))] if kh == 0 else []) +
-                   [(x, I32, r(wg, (8 * kh + 2 * k, 8 * kh + 2 * k + 2))) for k in range(4)], kh == 0, kh == 1)
-        if WTREE[q] == "P":
-            act(r("LS", js), r("TR", (0, 2)), F.Identity)
-        else:
-            dma("g", [(r(wg, (0, 8)), r(wg, (8, 16)))], acc=True)
-            dma("g", [(r(wg, (0, 4)), r(wg, (4, 8)))], acc=True)
-            dma("g", [(r("LS", js), r(wg, (0, 2)))], acc=True)
-            dma("g", [(r("LS", js), r(wg, (2, 4)))], acc=True)
+        if q == 3:
+            return
+        dma("g", [(r(w, (0, 8)), r(w, (8, 16)))], acc=True)
+        if WTREE[q] == "M":
+            mm([(x0(0, 256), I32, r("LS", js))] + [(x0(0, 256), I32, r(w, (2 * k, 2 * k + 2))) for k in range(4)])
+            act(r("LS", js), x0(0, 256), F.Identity)
+        if WTREE[q] == "D":
+            dma("g", [(r(w, (0, 4)), r(w, (4, 8)))], acc=True)
+            dma("g", [(r("LS", js), r(w, (0, 2)))], acc=True)
+            dma("g", [(r("LS", js), r(w, (2, 4)))], acc=True)
         dma("s", [(hbm("yw", slice(None), slice(*js)), r("LS", js))])
 
     for t in range(3):
+        up[0] = UP[t]
+        dma("y", [(r("XACC", None, (768 if t else 0, 1024)), r("UW", None, (768 if t else 0, 1024)))])
+        dma("g", [(r("XACC", 1, (0, 1024)), r("BASE", (8, 16)))], acc=True)
         step1(t)
-        if t == 0:
-            cp(r("WB", (8, 10)), ind(r("WW", (0, 1024)), r("OB")))
-            send(r("WB", (8, 10)), [r("WW", (1024 + 256 * d, 1280 + 256 * d)) for d in range(3)], 9)
-        extras(t)
+        if t:
+            up[0] = UP3[t]
+            extras(t, 0, t, (r("XS", 0, (0, 128 * t)), r("CNT", (0, t))))
+            ends(t, 0, t)
+            up[0] = UP2[t]
+        else:
+            cp(r("WX", 2, (128, 384)), ind(r("WW", (0, 1024)), r("OB")))
+            send(r("WX", 2, (128, 384)), [r("WW", (1024 + 256 * d, 1280 + 256 * d)) for d in range(3)], 9)
+        extras(t, t, t + 1, (x0(0, 128), x0(128, 256)))
+        up[0] = 0.0
         for q in range(4):
-            if t == 0 and q % 2 == 0:
-                for sp in range(2 * q, 2 * q + 4):
+            if t == 0 and q == 0:
+                for sp in range(8):
                     positions(sp)
+            if q == EARLY[t]:
+                up[0] = UP2[t]
+                ends(t, t, t + 1)
+                up[0] = 0.0
+                if q:
+                    close(r("XACC", None, (0, 256 * q)), CLOSE[t])
+                for p in range(q if t == 2 else 0):
+                    update(t, p)
+                    weights(p)
             forces(t, 2 * q)
+            if q in TALL:
+                sums(t, q, 0)
             forces(t, 2 * q + 1)
-            sums(t, q)
-            if t == 2:
+            sums(t, q, 1 if q in TALL else None)
+            if t == 2 and q >= EARLY[t]:
                 update(t, q)
                 weights(q)
         if t < 2:
-            for q in range(4):
-                update(t, q)
+            update(t, 0)
             border()
             la = ("LA1", "LA0")[t]
             send(r("SND", (0, 2)), [r(la, (2 * d, 2 * d + 2)) for d in range(3)], 3 * (t + 1))
@@ -711,9 +936,10 @@ def hazards(ops):
         for x, wr, a, b in acc:
             lst = seen.setdefault(x, [])
             if wr:
-                lst[:] = [e for e in lst if e[0] == i or not (a <= e[1] and e[2] <= b)]
+                lst[:] = [e for e in lst if e[0] in (i, o.get("beside")) or not (a <= e[1] and e[2] <= b)]
             lst.append((i, a, b, wr))
         dep.discard(i)
+        dep.discard(o.get("beside"))
         o["dep"] = sorted(dep)
 
 
@@ -727,22 +953,153 @@ def arrange(ops):
 
     def tail(o):
         if o["kind"] == "dma":
-            return 1.6 + o["by"] / 600e3
-        return 4.0 if o["kind"] == "send" else 0.0
+            return PACE["dlat"] + o["by"] / PACE["rate"]
+        return PACE["rem"] if o["kind"] == "send" else 0.0
     level = [0.0] * n
     for i in range(n - 1, -1, -1):
-        level[i] = ops[i]["cost"] + tail(ops[i]) + 0.1 + max([level[j] for j in succ[i]] + [0.0])
+        level[i] = ops[i]["cost"] + tail(ops[i]) + PACE["wake"] + max([level[j] for j in succ[i]] + [0.0])
     best = None
-    for it in range(PASSES + 1):
-        order = forward(ops, succ, level)
-        span = max(o["t1"] for o in ops)
-        if best is None or span < best[0]:
-            best = (span, order, [(o["t0"], o["t1"]) for o in ops])
-        if it < PASSES:
-            level = backward(ops, succ, tail)
-    for o, (a, b) in zip(ops, best[2]):
+    first = level
+    paces = [pace(ops, p) for p in PACES]
+    for look in LOOKS:
+        LOOK.update(zip("vspgy", look))
+        level = first
+        for it in range(PASSES + 1):
+            order = forward(ops, succ, level)
+            t0 = place(ops, [o["dep"] for o in ops], succ, [o["t0"] for o in ops], False)[0]
+            for od in (order, sorted(range(n), key=lambda i: (t0[i], i))):
+                span = sum(max(replay(od, m)[1]) / m[6] for m in paces)
+                if best is None or span < best[0]:
+                    best = (span, od)
+            if it < PASSES:
+                level = backward(ops, succ, tail)
+    order = smooth(ops, best[1], paces)
+    for o, a, b in zip(ops, *replay(order, paces[0])[:2]):
         o["t0"], o["t1"] = a, b
-    return best[1]
+    return order
+
+
+def pace(ops, p):
+    wake = PACE["wake"] * p["wait"]
+    return (["vspgyx".index(o["eng"]) for o in ops], [o["cost"] * p["pe" if o["eng"] == "p" else o["sort"]] for o in ops],
+            [o["by"] / PACE["rate"] * p["dma"] if o["kind"] == "dma" else 0.0 for o in ops],
+            [PACE["rem"] * p["wait"] if o["kind"] == "send" else 0.0 for o in ops],
+            [[(j, 0.0 if o.get("cont") and ops[j]["eng"] == "p" else wake) for j in o["dep"]] for o in ops],
+            PACE["dlat"] * p["wait"] / 2, p["all"])
+
+
+def replay(order, m):
+    eng, cost, dur, tail, lat, half = m[:6]
+    n = len(order)
+    free, last = [0.0] * 6, [-1] * 6
+    t0, t1, par, own = [0.0] * n, [0.0] * n, [-1] * n, [False] * n
+    pipe, lastd = 0.0, -1
+    for i in order:
+        e = eng[i]
+        s, p, w = free[e], last[e], True
+        for j, l in lat[i]:
+            x = t1[j] + l
+            if x > s:
+                s, p, w = x, j, False
+        t0[i] = s
+        s += cost[i]
+        free[e], last[e] = s, i
+        if dur[i]:
+            if pipe > s + half:
+                p, w = lastd, False
+            else:
+                pipe = s + half
+            pipe += dur[i]
+            s, lastd = pipe + half, i
+        t1[i], par[i], own[i] = s + tail[i], p, w
+    return t0, t1, par, own
+
+
+def smooth(ops, order, paces):
+    eng, dep = paces[0][0], [set(o["dep"]) for o in ops]
+    runs = [replay(order, m) for m in paces]
+    cur = sum(max(x[1]) / m[6] for x, m in zip(runs, paces))
+    seed = 1
+    for it in range(SWAPS):
+        seed = (seed * 1103515245 + 12345) % 2 ** 31
+        t0, t1, par, own = runs[it % len(runs)]
+        i, pairs = t1.index(max(t1)), []
+        while i >= 0:
+            if own[i] and par[i] >= 0:
+                pairs.append((par[i], i))
+            i = par[i]
+        a, b = pairs[(seed >> 8) % len(pairs)]
+        pa, pb = order.index(a), order.index(b)
+        seg = order[pa:pb + 1]
+        if seed >> 7 & 1:
+            mv, qs = {a}, set()
+            for x in seg[1:]:
+                if dep[x] & mv or eng[x] in qs:
+                    mv.add(x)
+                    qs.add(eng[x])
+            new = [x for x in seg if x not in mv] + [x for x in seg if x in mv]
+        else:
+            mv, qs, need = {b}, set(), set(dep[b])
+            for x in reversed(seg[:-1]):
+                if x in need or eng[x] in qs:
+                    mv.add(x)
+                    qs.add(eng[x])
+                    need |= dep[x]
+            new = [x for x in seg if x in mv] + [x for x in seg if x not in mv]
+        if a in mv and b in mv:
+            continue
+        od = order[:pa] + new + order[pb + 1:]
+        rs = [replay(od, m) for m in paces]
+        s = sum(max(x[1]) / m[6] for x, m in zip(rs, paces))
+        if s <= cur + SLACK * (1 - it / SWAPS):
+            cur, runs, order = s, rs, od
+    return order
+
+
+def place(ops, pre, nxt, key, back):
+    n = len(ops)
+    left = [len(p) for p in pre]
+    busy = {e: [] for e in "vspgyD"}
+    t0, t1 = [0.0] * n, [0.0] * n
+    ready = sorted((key[i], i) for i in range(n) if not left[i])
+
+    def fit(e, at, c):
+        lst = busy[e]
+        k = len(lst)
+        while k and lst[k - 1][1] > at:
+            k -= 1
+        while k < len(lst) and lst[k][0] < at + c - 1e-9:
+            at = max(at, lst[k][1])
+            k += 1
+        lst.insert(k, (at, at + c))
+        return at
+    while ready:
+        i = ready.pop(0)[1]
+        o = ops[i]
+        at = 0.0
+        for j in pre[i]:
+            a, b = (i, j) if back else (j, i)
+            at = max(at, t1[j] + (0.0 if ops[b].get("cont") and ops[a]["eng"] == "p" else PACE["wake"]))
+        c, half = o["cost"], PACE["dlat"] / 2
+        if o["kind"] == "recv":
+            t0[i] = t1[i] = at
+        elif o["kind"] == "dma":
+            d = o["by"] / PACE["rate"]
+            if back:
+                t1[i] = fit(o["eng"], fit("D", at + half, d) + d + half, c) + c
+            else:
+                t0[i] = fit(o["eng"], at, c)
+                t1[i] = fit("D", t0[i] + c + half, d) + d + half
+        else:
+            rem = PACE["rem"] if o["kind"] == "send" else 0.0
+            t0[i] = fit(o["eng"], at + (rem if back else 0.0), c)
+            t1[i] = t0[i] + c + (0.0 if back else rem)
+        for j in nxt[i]:
+            left[j] -= 1
+            if not left[j]:
+                ready.append((key[j], j))
+                ready.sort()
+    return t0, t1
 
 
 def backward(ops, succ, tail):
@@ -761,7 +1118,7 @@ def backward(ops, succ, tail):
             if not lst:
                 continue
             s = min(max(free[e], at[i]) for i in lst)
-            i = max((i for i in lst if max(free[e], at[i]) <= s + LOOK), key=lambda q: ops[q]["t1"])
+            i = max((i for i in lst if max(free[e], at[i]) <= s + LOOK[e]), key=lambda q: ops[q]["t1"])
             s = max(free[e], at[i])
             if best is None or s < best[0]:
                 best = (s, i)
@@ -772,7 +1129,7 @@ def backward(ops, succ, tail):
         if o["kind"] != "recv":
             free[o["eng"]] = out[i]
         for j in o["dep"]:
-            at[j] = max(at[j], out[i] + 0.1 + tail(ops[j]))
+            at[j] = max(at[j], out[i] + PACE["wake"] + tail(ops[j]))
             left[j] -= 1
             if not left[j]:
                 ready[ops[j]["eng"]].append(j)
@@ -802,7 +1159,7 @@ def forward(ops, succ, level):
             if not lst:
                 continue
             s = min(max(free[e], at[i]) for i in lst)
-            i = max((i for i in lst if max(free[e], at[i]) <= s + LOOK), key=lambda q: level[q])
+            i = max((i for i in lst if max(free[e], at[i]) <= s + LOOK[e]), key=lambda q: level[q] + ops[q]["up"])
             if e == "g" and ops[i]["kind"] == "dma" and hold[0] and at[hold[0][0]] <= s + GLOOK:
                 continue
             s = max(free[e], at[i])
@@ -817,13 +1174,13 @@ def forward(ops, succ, level):
         if o["kind"] != "recv":
             free[o["eng"]] = end
         if o["kind"] == "dma":
-            pipe[0] = max(pipe[0], end + 0.8) + o["by"] / 600e3
-            end = pipe[0] + 0.8
+            pipe[0] = max(pipe[0], end + PACE["dlat"] / 2) + o["by"] / PACE["rate"]
+            end = pipe[0] + PACE["dlat"] / 2
         if o["kind"] == "send":
-            end += 4.0
+            end += PACE["rem"]
         o["t1"] = end
         for j in succ[i]:
-            lat = 0.0 if ops[j].get("cont") and o["eng"] == "p" else 0.1
+            lat = 0.0 if ops[j].get("cont") and o["eng"] == "p" else PACE["wake"]
             at[j] = max(at[j], end + lat)
             left[j] -= 1
             if not left[j]:

@@ -59,12 +59,52 @@ CUT = ['SSSV'] * 3
 MARK = ['VVVVVVVV', 'VVVVVSVV', 'VVVVVVVV']
 CLIP = ['VVVDVVVV', 'DVVVVVVV', 'DVVVVVVV']
 EADD = ['DDDVDDDV', 'DDDDDDDD', 'DDDDDDDD']
+LOAD = "V"
+GMODE = ['FSSSSSSS'] * 3
+UAM = "GGG"
+OWN = ["GGGG"] * 3
+EQM = "SSS"
+INIT = "SSV"
+ENDP = ["VVV"] * 3
+ENDG = ["SSS"] * 3
+ROWG = "SS"
+AHEAD = [0, 0, 0]
+FILL = "V"
+EMP = "S"
+LAY = ["VVVV"] * 3
+YW = "y"
+URG = [[1] * 5] * 3
+EBUF = [("BASE", "WB")] * 3
+BORD = ["VSV", "VS", "VS"]
+S1S = ["SS"] * 3
+PAR = [1, 1, 1]
+INIT, ENDP, LOAD, CONV, EVG, EQM, CLOSE, CPU = 'VSV', ['PPV', 'VPV', 'VPV'], 'G', 'svv', 'S', 'SLL', 'AAA', 'SV'
+EADD = ['DDDVDDDV', 'DDDDDDDV', 'DDDDDDDD']
+BORD, UP3, UP2, EARLY = ['SSV', 'VS', 'VS'], [-5.0, 0.0, 0.0], [10.0, 0.0, 10.0], [1, 2, 0]
+CLIP, ROWG, WT3, UAM = ['VVVDVVVV', 'DVDVVVVV', 'DVVDVVVV'], 'VV', 'VP', 'SVV'
+S1G, OWN, S1S, DMODE, CONS = ['VS', 'SV', 'VV'], ['GGGG', 'GGGS', 'GGGG'], ['SS', 'GS', 'SS'], 'VSSVSSSS', 'S'
+ENDG, CUT, MARK = ['SVS', 'SSV', 'SVS'], ['VSSS', 'SVSV', 'SSSS'], ['VVSVVVSV', 'SSVVVVSV', 'VVSVVVSS']
+S1Z, S1C, FIN = ['DV', 'VV', 'VP'], ['VS', 'VV', 'SS'], ['SVSA', 'VSVP', 'PAAS']
+WIDE = ["WWWWWWWW"] * 3
+MARK = ["VVVVVVVV", "SVVVVVVV", "VVSVVVVV"]
+URG = [[0, 1, 1, 2, 2]] * 3
+WTREE = ["TDDDD", "TDDDD", "HDDVVV"]
+SPLIT = [(2, 4)]
+WT3, CUT, FIN, AHEAD = "VV", ['VSSS', 'SVSV', 'SSSV'], ['SVSA', 'VSVP', 'AAAP'], [0, 1, 1]
+GMODE, CONV, UAM = ["FSSSSSSS", "RSSSSSSS", "RSSSSSSS"], "svs", "SSS"
+ENDP, URG = ['VPV', 'VVV', 'VPV'], [[0, 3, 2, 3, 3], [1, 2, 2, 3, 3], [1, 2, 2, 3, 3]]
+BORD, CLOSE, CPU, ROWG = ['SSV', 'VV', 'VS'], 'AVV', 'VV', 'VS'
+CLIP, WTREE = ['VVVVVVVV', 'DVVVVVVV', 'DVVVVVVV'], ['TDDDD', 'HDDDVV', 'HDVVVV']
+WIDE, OWN, S1S = ['WWWWWWWW', 'WWWWWWWW', 'WWWWWWHW'], ['GGVG', 'GGGS', 'GGGG'], ['SG', 'GS', 'SS']
+DMODE, ENDG, CUT, MARK = 'VSSVSVSS', ['SSV', 'SSV', 'SVS'], ['VVSS', 'SVSV', 'SSVV'], ['VVVVVVVV'] * 3
+S1C, FIN = ['VV'] * 3, ['QVSS', 'VSVA', 'AAAP']
 LOOKS = [(0.05, 0.05, 0.05, 0.05, 0.05), (0.0, 0.1, 0.1, 0.3, 0.05)]
-SWAPS, SLACK = 4000, 0.0
-PACES = [{"work": 1.0, "pe": 1.05, "pick": 1.0, "dma": 1.0, "wait": 1.0, "all": 1.0},
-         {"work": 1.1, "pe": 1.15, "pick": 1.4, "dma": 1.2, "wait": 1.5, "all": 1.2},
-         {"work": 1.0, "pe": 1.05, "pick": 0.8, "dma": 1.5, "wait": 1.8, "all": 1.15},
-         {"work": 1.4, "pe": 1.45, "pick": 1.4, "dma": 1.2, "wait": 1.4, "all": 1.4}]
+SWAPS, SLACK, LEVEL = 70000, 0.8, 3
+PACES = [{"work": 1.0, "pe": 1.05, "pick": 1.0, "dma": 1.05, "wait": 1.0, "wake": 1.2, "all": 1.0},
+         {"work": 1.25, "pe": 1.25, "pick": 1.65, "dma": 1.2, "wait": 1.3, "wake": 2.5, "all": 1.35},
+         {"work": 1.1, "pe": 1.1, "pick": 0.9, "dma": 1.6, "wait": 1.6, "wake": 2.0, "all": 1.3},
+         {"work": 1.4, "pe": 1.4, "pick": 1.3, "dma": 1.3, "wait": 1.3, "wake": 3.5, "all": 1.45}]
+FIXED = 0.015
 
 
 def _sb(shape, d):
@@ -73,20 +113,20 @@ def _sb(shape, d):
 
 SCRATCH = {
     "QC": _sb([4, 2048], h16), "NZ": _sb([2, 1024], b16), "AP": _sb([2, 1024], h16), "TT": _sb([1024], h16),
-    "EQ": _sb([1152], b16),
-    "QS": _sb([32, 3, 16], h16), "DM": _sb([2, 16, 512], h16), "AB": _sb([8, 1024], h16), "AT": _sb([16, 128], h16),
+    "T2": _sb([1024], b16),
+    "QS": _sb([32, 3, 16], h16), "DM": _sb([2, 16, 512], h16), "AB": _sb([8, 1024], h16), "AT": _sb([2, 1024], h16),
     "G": _sb([NG, 2, 1024], h16), "EE": _sb([5, 1024], i32), "UR": _sb([NR, 2, 1024], h16),
     "UW": _sb([2, 1800], f32), "PW": _sb([1800], b16), "PO": _sb([1024], h16), "WW": _sb([1800], f32),
-    "LS": _sb([1152], f32), "XACC": _sb([2, 1152], f32), "BASE": _sb([2048], f32), "WB": _sb([2048], f32),
+    "LS": _sb([1152], f32), "XACC": _sb([2, 1152], f32), "BASE": _sb([2, 1024], f32), "WB": _sb([2, 1024], f32),
     "SC": _sb([2, 4 + len(TALL), 128], b16), "SS": _sb([4 + len(TALL), 128], b16), "D2": _sb([1024], h16),
     "SEL": _sb([16, 128], b16), "LA0": _sb([6, 256], h16), "LA1": _sb([6, 256], h16), "SND": _sb([3, 256], h16),
     "NBI": _sb([8, 4, 16], i32), "BI": _sb([16], i32), "ONB": _sb([512], u16), "OB": _sb([16], u16),
-    "PI": _sb([8], i32), "CL": _sb([32], f32), "J": _sb([144], f32), "IW": _sb([136], f32), "WC": _sb([144], b16),
+    "PI": _sb([8], i32), "CL": _sb([32], f32), "IW": _sb([136], f32), "WC": _sb([144], b16),
     "C2": _sb([136], b16), "W2": _sb([136], b16), "PL": _sb([2, 8], b16), "UP": _sb([128], b16),
     "MX": _sb([32, 128], b16), "DIAG": _sb([128], f32), "MASK": _sb([1032], b16), "RS8": _sb([512], b16),
     "DK": _sb([2, 128], f32),
-    "RS16": _sb([128], f32), "DUM": _sb([128], f32), "DUMM": _sb([128], f32), "VID": _sb([2, 128], f32),
-    "OAI": _sb([64], i32), "OA": _sb([3, 64], u16),
+    "RS16": _sb([128], f32), "DUMM": _sb([128], f32), "VID": _sb([128], f32),
+    "LD": _sb([1024], h16), "I5": _sb([128], b16),
     "GM": _sb([1024], h16), "D1": _sb([512], h16), "MB": _sb([512], b16), "CM": _sb([512], h16),
     "NF": _sb([128], f32), "S1": _sb([128], f32), "SCN": _sb([128], f32), "S2": _sb([128], f32), "SC2": _sb([128], f32),
     "U16": _sb([128], h16), "EV": _sb([128], b16), "FV": _sb([128], b16), "FC": _sb([128], b16),
@@ -109,7 +149,7 @@ SEMAPHORES = ["cv", "cs", "cp", "cg"] + ["d%d" % i for i in range(NDS)] + \
  CX, CY, RN, NRN, SC2, NMT, D16, C64, OW) = range(32)
 
 
-UNIT = {"WB": (0, 128), "BASE": (0, 128), "TR": (0, 128), "X0": (0, 128),
+UNIT = {"TR": (0, 128), "X0": (0, 128),
         "QC": (1, 256), "NZ": (1, 256)}
 
 
@@ -211,7 +251,7 @@ def build():
             return 0.05 + out["n"] * PACE["sc"] * 0.00083
         if in0 is not None and in0["k"] == "i":
             return 0.05 + out["n"] * PACE["ga"] * 0.00083
-        return 0.045 + max(64, out["n"] * c) * 0.00083
+        return FIXED + max(64, out["n"] * c) * 0.00083
 
     def tt(out, a, b, op):
         add("v", "tt", (out, a, b, op), [out], [a, b], vc(out, a, 1 if _ps(a) or _ps(b) else 2))
@@ -230,10 +270,12 @@ def build():
 
     def act(out, a, fn, bias=0.0, scale=1.0):
         add("s", "act", (out, a, fn, bias, scale), [out], [a, bias, scale],
-            0.065 + max(64, out["n"] * (PACE["ga"] if a["k"] == "i" else 1)) * 0.00083)
+            (0.065 if a["k"] == "i" else FIXED) + max(64, out["n"] * (PACE["ga"] if a["k"] == "i" else 1)) * 0.00083)
 
     def lin(who, out, a, scale, bias):
-        if who in "Ss":
+        if who == "G":
+            sel(out, a)
+        elif who in "Ss":
             act(out, a, F.Identity, bias=bias, scale=scale)
         else:
             ts(out, a, scale, A.mult, bias, A.add)
@@ -250,6 +292,9 @@ def build():
 
     def iota(out, pat, base, cm):
         add("g", "iota", (out, pat, base, cm), [out], [], 0.13 + out["n"] * 0.00166)
+
+    def sel(out, a):
+        add("g", "sel", (out, a, [[0, out["n"]]], A.is_gt, 0.0, 1, 0), [out], [a], 0.17 + out["n"] * 0.00166)
 
     def dma(q, pairs, acc=False, nb=None):
         by = rows = 0
@@ -281,13 +326,14 @@ def build():
     dma("s", [(r("EE", 1), hbm("uy"))])
     dma("s", [(r("NBI"), hbm("nb"))])
     iota(r("PI", (0, 1)), [[0, 1]], 0, 1)
-    iota(r("J"), [[1, 144]], 0, -1)
+    iota(r("WX", 2, (0, 144)), [[1, 144]], 0, -1)
     iota(r("DIAG"), [[0, 8], [1, 16]], 0, 0)
     iota(r("S1"), [[16, 8], [0, 16]], 0, -1)
     iota(r("MASK"), [[0, 129], [1, 8]], 0, 0)
-    iota(r("OAI"), [[1, 64]], 0, 64)
+    iota(r("NF", (0, 64)), [[1, 64]], 0, 64)
     ts(r("PI", (1, 2)), r("PI", (0, 1)), 15, A.bitwise_and)
     ts(r("PI", (2, 3)), r("PI", (0, 1)), 8, A.bitwise_and)
+    ts(r("PI", (3, 4)), r("PI", (0, 1)), 112, A.bitwise_and)
     cp(col(0), r("PI", (1, 2)))
     cp(col(1), r("PI", (2, 3)))
     ts(col(2), col(0), 8.0, A.is_lt)
@@ -309,11 +355,11 @@ def build():
     ts(col(18), col(0), 8.0, A.is_ge)
     ts(r("MASK"), r("MASK"), col(0), A.is_equal, col(15), A.add)
     ts(col(30), col(0), 12.0, A.is_ge, col(18), A.subtract)
-    ts(r("PO"), IC, col(30), A.mult, col(7), A.add)
+    lin(INIT[0], r("PO"), IC, col(30), col(7))
     cp(r("OB"), r("BI"))
     for c in range(2):
         lin(CPU[c], r("UW", c, (0, 1024)), r("EE", c), 1.0, 0.0)
-    ts(r("IW"), r("J", (0, 136)), 8.0, A.is_equal)
+    ts(r("IW"), r("WX", 2, (0, 136)), 8.0, A.is_equal)
     I32 = r("IW", (8, 136))
     act(mx(IB_), I32, F.Identity)
     act(mx(NI), I32, F.Identity, scale=-1.0)
@@ -322,11 +368,13 @@ def build():
         mm([(x, mx(IB_), r("MASK", hs)), (x, mx(NI), r("PO", hs))])
         act(r("PW", hs), x, F.Identity)
 
-    def border():
+    def border(t):
         for c in range(2):
-            lin(BORD[c], r("SND", c), ind(r("UW", c, (0, 1024)), r("OB")), 1.0, 0.0)
-    border()
-    ts(r("SND", 2), ind(r("PW", (0, 1024)), r("OB")), col(2), A.max)
+            lin(BORD[t][c], r("SND", c), ind(r("UW", c, (0, 1024)) if t else r("EE", c), r("OB")), 1.0, 0.0)
+    border(0)
+    ts(col(17), col(30), -1.0, A.mult)
+    ts(col(19), oh(12), col(2), A.add)
+    lin(BORD[0][2], r("SND", 2), ind(IC, r("OB")), col(17), col(19))
     send(r("SND"), [r("AB", d, (0, 768)) for d in range(3)], 0)
     for q in range(4):
         if q in TALL:
@@ -334,18 +382,18 @@ def build():
                 cp(r("ONB", (128 * q + 64 * h, 128 * q + 64 * h + 64)), r("NBI", None, q, (8 * h, 8 * h + 8)))
         else:
             cp(r("ONB", (128 * q, 128 * q + 128)), r("NBI", None, q))
-    ms(r("UW", None, (1792, 1800)), 0.0)
-    ms(r("WW", (1792, 1800)), 0.0)
+    def zero(out):
+        iota(out, [[0, out["n"]]], 0, 0) if FILL == "G" else ms(out, 0.0)
+    zero(r("UW", None, (1792, 1800)))
+    zero(r("WW", (1792, 1800)))
     ts(r("PW", (1792, 1800)), r("MASK", (0, 8)), 0.0, A.mult, col(2), A.add)
-    ms(r("LS", (1024, 1152)), 0.0)
-    ts(r("OAI"), r("OAI"), 1023, A.bitwise_and)
-    cp(r("ON"), r("OAI"))
-    ts(r("LS", (0, 1024)), ind(IC, r("ON")), float(E), A.subtract, col(2), A.mult)
-    iota(r("OAI"), [[16, 64]], 0, 0)
-    for t in range(3):
-        ts(r("OA", t), r("OAI"), col(1), A.add, float(7 - t), A.add)
+    zero(r("LS", (1024, 1152)))
+    ts(col(28), r("PI", (3, 4)), -64.0, A.mult)
+    ts(r("ON"), r("NF", (0, 64)), col(28), A.add)
+    act(col(29), col(2), F.Identity, scale=-float(E))
+    lin(INIT[1], r("LS", (0, 1024)), ind(IC, r("ON")), col(2), col(29))
     ts(mx(BLK), r("S1"), col(0), A.add, 0.0, A.is_equal)
-    ts(r("WC"), r("J"), col(0), A.add, 15.0, A.is_equal)
+    ts(r("WC"), r("WX", 2, (0, 144)), col(0), A.add, 15.0, A.is_equal)
     act(col(5), col(30), F.Identity, scale=-32.0)
     mkcol(5, [(12, -32768), (15, 32640)], first=col(5))
     mkcol(6, [(12, 32768), (15, -23552)])
@@ -374,7 +422,7 @@ def build():
                     (NMT, MT, -1.0), (I16, IB_, 16.0)):
         if (m not in (SC2, NMT) or "S" in "".join(S1C)) and (m != SCO or "V" in "".join(S1C)):
             ts(mx(m), mx(s), v, A.mult) if CONS == "V" else act(mx(m), mx(s), F.Identity, scale=v)
-    ts(mx(TRI), r("J", (0, 128)), 0.0, A.is_gt, -2.0, A.mult)
+    ts(mx(TRI), r("WX", 2, (0, 128)), 0.0, A.is_gt, -2.0, A.mult)
     tt(mx(TRI), mx(TRI), I32, A.add)
     ts(r("S2"), mx(BLK), col(2), A.mult)
     tt(mx(TRI), mx(TRI), r("S2"), A.mult)
@@ -386,27 +434,29 @@ def build():
     mm([(x0(0, 128), mx(OW), mx(IB_))])
     act(mx(OW), x0(0, 128), F.Identity)
     tt(r("C2"), r("WC", (0, 136)), r("WC", (8, 144)), A.add)
-    iota(r("DUM"), [[-1, 128]], 1152, 0)
-    for t in range(2):
-        iota(r("VID", t), [[8, 128]], 7 - t - E, 0)
-    tt(r("DUMM"), r("DUM"), r("DIAG"), A.mult)
-    iota(r("RS8"), [[0, 64], [1, 8]], 0, 0)
-    ts(r("RS8"), r("RS8"), 1.0, A.min)
+    iota(r("DF"), [[-1, 128]], 1152, 0)
+    tt(r("DUMM"), r("DF"), r("DIAG"), A.mult)
+    iota(r("RS8"), [[0, 512]], 1, 0)
+    zero(r("RS8", (0, 512, 8)))
     iota(r("DK", 0), [[-1, 128]], 1152 + 71 * 2048, 0)
     iota(r("DK", 1), [[-1, 128]], 1152 + 7 * 2048, 0)
-    ms(r("RS16"), 1.0)
-    ms(r("RS16", (0, 128, 16)), 0.0)
+    iota(r("RS16"), [[0, 128]], 1, 0)
+    zero(r("RS16", (0, 128, 16)))
     scan(r("MD"), r("RS16"), r("DUMM"), 0.0, A.mult, A.add)
-    ms(r("QE"), 0.0)
-    ms(r("XACC", None, (1024, 1152)), 0.0)
+    zero(r("XACC", None, (1024, 1152)))
+    sel(r("QE", (0, 256)), r("XACC", None, (1024, 1152)))
+    sel(r("QE", (256, 384)), r("LS", (1024, 1152)))
     dma("y", [(r("EE", 4), hbm("ld"))])
     dma("y", [(r("WW", (0, 1024)), hbm("wt"))])
-    ts(r("BASE", (8, 16)), r("EE", 4), 0.5, A.add, 1 / 32, A.mult)
+    lin(LOAD, r("LD"), r("EE", 4), 1.0, 0.0)
+    act(r("I5"), I32, F.Identity, scale=1 / 32)
     iota(r("SEL"), [[1, 16], [16, 8], [0, 16]], 0, -1)
     ts(r("SEL"), r("SEL"), 0.0, A.is_equal, 2048.0, A.mult)
-    ms(r("QS", None, 1), 0.0)
-    ms(r("DM", 0, (0, 4)), 0.0)
-    dma("y", [(r("DM", z // 4, (4 * (z % 4), 4 * (z % 4) + 4)), r("DM", 0, (0, 4))) for z in range(1, 8)])
+    ms(r("DM", 0, 0), 0.0)
+    sel(r("QS", None, 1), r("DM", 0, 0))
+    for z in (1, 2, 4, 8):
+        dma("y", [(r("DM", 0, (z, 2 * z)), r("DM", 0, (0, z)))])
+    dma("y", [(r("DM", 1), r("DM", 0))])
 
     def convert(t):
         for d in range(3):
@@ -420,7 +470,7 @@ def build():
         rho = 7 - t
         LSW = r("LS")
         act_ls = r("LS", (rho, 1024, 8))
-        cp(r("U16"), act_ls)
+        lin(S1S[t][0], r("U16"), act_ls, 1.0, 0.0)
         mm([(x0(0, 64), mx(IB_), r("U16", (0, 128, 2))), (x0(0, 64), r("UP"), r("U16", (1, 128, 2)))])
         ts(r("ON"), x0(0, 64), float(E), A.add, 1024.0, A.min)
         if GMG[t] == "V":
@@ -430,36 +480,41 @@ def build():
             for h in range(2):
                 mm([((x0, x1)[h](k, 512, 8), r("SEL", (k + t) % 8), r("AP", 0, (512 * h + k, 512 * h + 512, 8))) for k in range(8)])
                 act(r("GM", (512 * h, 512 * h + 512)), (X0, X1)[h], F.Identity, scale=oh(0))
-        act(r("EQ"), LSW, F.Relu, bias=1.0, scale=2.0)
-        mm([(x1(0, 128), mx(TRI), r("EQ", (rho, 1024, 8)))])
+        act(r("FC"), act_ls, F.Relu, bias=1.0, scale=2.0)
+        mm([(x1(0, 128), mx(TRI), r("FC"))])
         act(r("FV"), x1(0, 128), F.Relu)
         mm([(x0(0, 64), r("WC", (15 - i, 143 - i)), r("GM", (i, 1024, 16))) for i in range(16)])
         ts(r("OX"), x0(0, 64), float(E), A.add, 1023.0, A.min)
         ts(r("OC"), x0(0, 64), float(E), A.add)
+        if UAM[t] == "G":
+            for k in range(8):
+                sel(r("AP", None, (k, 1024, 8)), r("UW", None, (rho, 1024, 8)))
+        else:
+            lin(UAM[t], r("AP", None, (0, 1024, 8)), r("UW", None, (rho, 1024, 8)), 1.0, 0.0)
+            for k in range(1, 8):
+                cp(r("AP", None, (k, 1024, 8)), r("AP", None, (0, 1024, 8)))
         for h in range(2):
-            o = (32 * h, 32 * h + 32)
+            o, hs = (32 * h, 32 * h + 32), (512 * h, 512 * h + 512)
             neg = S1G[t][h] == "S"
-            if h == 0 or not PAR[t]:
-                ua, ds = [[r("WB", (a, a + 4)), r("WB", (a + 4, a + 8)), r("WB", (a, a + 8))] for a in (0, 8)]
-                ex, ey, at = ds[0], ds[1], 12
+            ua = [r("AP", 0, hs), r("AP", 1, hs), r("AP", None, hs)]
+            if t:
+                ds = [r("AT", h, (0, 512)), r("AT", h, (512, 1024)), r("AT", h)]
+            else:
+                ds = [r("AB", 5 + h, (0, 512)), r("AB", 5 + h, (512, 1024)), r("AB", 5 + h)]
+            if h == 0:
+                ex, ey = r("WB", 1, (0, 512)), r("WB", 1, (512, 1024))
                 d1, mb, cm = r("D1"), r("MB"), r("CM")
                 y0, y1 = x0, x1
             else:
-                ua, ds = [[r("AP", a, (0, 512)), r("AP", a, (512, 1024)), r("AP", a)] for a in (0, 1)]
-                ex, ey, at = r("WB", (0, 4)), r("WB", (4, 8)), 4
-                d1, mb, cm = r("NZ", 0, (0, 2)), r("NZ", 0, (2, 4)), r("NZ", 1, (0, 2))
-                y0, y1 = [lambda a, b, s=1, z=z: r("UL", z, (a, b, s)) for z in range(2)]
+                ex, ey = r("WB", 0, (0, 512)), r("WB", 0, (512, 1024))
+                if PAR[t]:
+                    d1, mb, cm = r("NZ", 0, (0, 2)), r("NZ", 0, (2, 4)), r("NZ", 1, (0, 2))
+                if PAR[t] in (1, 3):
+                    y0, y1 = [lambda a, b, s=1, z=z: r(("UL", "DXY")[PAR[t] // 2], z, (a, b, s)) for z in range(2)]
             Y0, Y1 = y0(0, 512), y1(0, 512)
-            byt = S1G[t][h] == "T"
-            if byt and (h == 0 or not PAR[t]):
-                ua, ds = [[r("G1", a), r("G1", a + 1)] for a in (0, 2)]
-            if byt and (h == 0 or S1G[t][0] != "T"):
-                act(r("UA"), r("UW", None, (rho, 1024, 8)), F.Identity, scale=-1.0)
             for c in range(2):
-                act(ua[c], ind(r("UW", c, (0, 1024)), r("OX", o) if byt else r("OA", t, o)), F.Identity, scale=-1.0 if neg else 1.0)
-            for c in range(0 if byt else 2):
                 if neg:
-                    act(ds[c], ind(r("UW", c, (0, 1024)), r("OX", o)), F.Identity)
+                    act(ds[c], ind(r("UW", c, (0, 1024)), r("OX", o)), F.Identity, scale=-1.0)
                 else:
                     tt(ds[c], ind(r("UW", c, (0, 1024)), r("OX", o)), ua[c], A.subtract)
             if neg:
@@ -473,10 +528,6 @@ def build():
             act(d1, Y0, F.Square)
             mm([(Y0, mx(DXP), d1)])
             mm([(Y1, mx(DYP), d1)])
-            for c in range(2 if byt else 0):
-                y = (y0, y1)[c]
-                act(ds[c], y(0, 512), F.Identity)
-                mm([(y(0, 512), mx(IB_), ua[c])] + [(y(k, 512, 8), mx(IB_), r("UA", c, (64 * h, 64 * h + 64))) for k in range(8)])
             tt(ex, ds[0], Y0, A.mult)
             if S1Z[t][h] == "V":
                 tt(Y1, ds[1], Y1, A.mult)
@@ -501,15 +552,15 @@ def build():
                [(y0(k, 512, 8), mx(PBG), r("FV", (64 * h, 64 * h + 64))) for k in range(8)] +
                [(Y0, mx(SC2 if S1C[t][h] == "S" else SCO), cm)])
             scan(ey, r("RS8"), Y0, 0.0, A.mult, A.max)
-            tt(r("NBI", h), r("WB", (128 * at + 7, 128 * at + 512, 8), raw=True), r("DK", int(S1C[t][h] == "S"), (64 * h, 64 * h + 64)), A.max)
+            tt(r("NBI", h), r("WB", 1 - h, (519, 1024, 8)), r("DK", int(S1C[t][h] == "S"), (64 * h, 64 * h + 64)), A.max)
         up[0] = UP2[t]
         nm = r("NBI", (2, 4))
         ts(nm, r("NBI", (0, 2)), 2047, A.bitwise_and)
         tt(r("S1"), nm, r("DIAG"), A.mult)
-        cp(r("NF"), nm)
+        lin(S1S[t][1], r("NF"), nm, 1.0, 0.0)
         scan(r("SCN"), r("RS16"), r("S1"), 0.0, A.mult, A.add)
         ts(r("OM"), r("SCN", (15, 128, 16)), -1.0, A.add)
-        lin(EVG, r("EV"), ind(r("EQ"), r("OM")), 1.0, 0.0)
+        act(r("EV"), ind(LSW, r("OM")), F.Relu, bias=1.0, scale=2.0)
         mm([(x0(128, 256), mx(TRI), r("EV"))])
         ms(r("GM", (0, 1)), 0.0)
         tt(r("GM", (1, 128)), r("NF", (1, 128)), r("SCN", (0, 127)), A.is_equal)
@@ -536,7 +587,8 @@ def build():
         if t < 2:
             act(r("S1"), r("NF"), F.Identity, bias=-1.0 - E)
             tt(r("OVV", t), r("S1"), r("FV"), A.mult)
-            tt(r("OVC", t), r("VID", t), r("FC"), A.mult)
+            iota(r("VID"), [[8, 128]], rho - E, 0)
+            tt(r("OVC", t), r("VID"), r("FC"), A.mult)
 
     def ec(t, lo, hi):
         return r("EC", (64 * t * (t + 1) + 128 * lo, 64 * t * (t + 1) + 128 * hi))
@@ -576,15 +628,25 @@ def build():
     def ot(b):
         return r("OT", (8 * b, 8 * b + 8))
 
+    def into(who, x, y, op, tmp):
+        if who == "S":
+            act(tmp, x, F.Identity)
+            tt(x, tmp, y, op)
+        else:
+            tt(tmp, x, y, op)
+            cp(x, tmp)
+
+    def byp(t):
+        return [b for b in range(t + 1) if ENDP[t][b] == "P" and (b < t or not EARLY[t])]
+
     def ends(t, lo, hi):
         for b in range(lo, hi):
             bs = (128 * b, 128 * b + 128)
             own = r("XACC", None, (7 - b, 1024, 8))
-            tt(own, own, r("WX", (0, 2), bs), A.add)
+            if b not in byp(t):
+                tt(own, own, r("WX", (0, 2), bs), A.add)
             for c in range(2):
-                tmp = (r("WX", 2, bs), r("SC2"))[c]
-                tt(tmp, ind(r("XACC", c), ot(b)), r("WX", c, bs), A.subtract)
-                cp(ind(r("XACC", c), ot(b)), tmp)
+                into(ENDG[t][b], ind(r("XACC", c), ot(b)), r("WX", c, bs), A.subtract, (r("WX", 2, bs), r("SC2"))[c])
             if t == 2:
                 if b == 0:
                     act(r("LS", (0, 1024)), r("MASK", (0, 1024)), F.Identity, scale=0.0)
@@ -595,11 +657,10 @@ def build():
                     ae = r("MD" if b else "DUMM")
                     act(ae, x, F.Identity)
                 own = r("LS", (7 - b, 1024, 8))
-                tt(r("WX", 0, bs), ind(r("WW"), ot(b)), ae, A.mult)
-                tt(r("WX", 1, bs), r("WW", (7 - b, 1024, 8)), ae, A.mult)
-                tt(own, own, r("WX", 0, bs), A.add)
-                tt(r("WX", 2, bs), ind(r("LS"), ot(b)), r("WX", 1, bs), A.add)
-                cp(ind(r("LS"), ot(b)), r("WX", 2, bs))
+                tt(r("S1"), ind(r("WW"), ot(b)), ae, A.mult)
+                tt(r("SCN"), r("WW", (7 - b, 1024, 8)), ae, A.mult)
+                tt(own, own, r("S1"), A.add)
+                into(ENDG[t][b], ind(r("LS"), ot(b)), r("SCN"), A.add, r("WX", 2, bs))
 
     def rows_update(t):
         for b in range(t + 1):
@@ -608,8 +669,7 @@ def build():
             tt(r("S2"), r("OVV", b), se, A.mult)
             tt(r("SC2"), r("OVC", b), se, A.mult)
             tt(own, own, r("S2"), A.add)
-            tt(r("S2"), ind(r("LS"), ot(b)), r("SC2"), A.add)
-            cp(ind(r("LS"), ot(b)), r("S2"))
+            into(ROWG[t], ind(r("LS"), ot(b)), r("SC2"), A.add, r("S2"))
 
     def blocks(sp):
         q, kh = divmod(sp, 2)
@@ -645,78 +705,129 @@ def build():
                  r("QC", q, (1024 * h + a, 1024 * h + a + w), raw=True)) for h in range(2) for k, v, a, w in blocks(2 * q + h)])
             act(r("EC", (384, 640)), hi, F.Square, scale=2048.0)
             act(r("D2", js), hi, F.Identity)
-            mm([(lo, mx(D8), r("EC", (384, 640))), (lo, mx(QE8), r("EQ", js))])
+            if EMP == "S":
+                act(r("T2", js), r("LS", js), F.Relu, bias=1.0, scale=2.0)
+            else:
+                ts(r("T2", js), r("LS", js), 0.0, A.is_equal)
+            mm([(lo, mx(D8), r("EC", (384, 640))), (lo, mx(QE8), r("T2", js))])
             act(r("TT", js), lo, F.Identity, scale=col(25))
+            if "E" in "".join(x[2 * q:2 * q + 2] for x in CLIP):
+                act(r("T2", js), lo, F.Identity, scale=1 / 16)
             mm([(r("CNT", (2, 4)), r("MX", D16, p=(0, 16)), pt)] +
                [(r("CNT", (2, 4), (8 * j, 8 * j + 8)), tile(q, j), r("PL")) for j in range(16)])
-            act(r("AT", (q, 8, 4)), r("CNT", (2, 4)), F.Identity)
+            act(r("AT", None, (128 * q, 128 * q + 128)), r("CNT", (2, 4)), F.Identity)
             if q % 2:
                 u = q - 1
                 dma("y", [(r("DM", c, j, (128 * u, 128 * u + 256), p=(j, 128, 16)),
-                           r("AT", (4 * c + u, 4 * c + u + 2), p=(j, 128, 16))) for j in range(16) for c in range(2)], nb=300000)
+                           r("AT", c, (128 * u, 128 * u + 256), p=(j, 128, 16))) for j in range(16) for c in range(2)], nb=300000)
+
+    def repeat(t, sp, src):
+        q, kh = divmod(sp, 2)
+        ur = ((4 + len(TALL)) * t + unit(q, kh)) % NR
+        v, w = blocks(sp)[0][1], blocks(sp)[0][3]
+        lin(OWN[t][q], r("UR", ur, None, (0, w)), r(src, None, (v, v + w)), 1.0, 0.0)
+        byg = URG[t][unit(q, kh)]
+        while w < 1024:
+            if byg > 0:
+                for a in range(0, w, 256):
+                    sel(r("UR", ur, None, (w + a, w + a + min(w, 256))), r("UR", ur, None, (0, min(w, 256))))
+            else:
+                dma("y", [(r("UR", ur, None, (w, 2 * w)), r("UR", ur, None, (0, w)))])
+            byg -= 1
+            w *= 2
 
     def forces(t, sp):
         q, kh = divmod(sp, 2)
         b, bg, be = sp % 2, (8 * t + sp) % NG, (8 * t + sp) % NE
         js = (256 * q, 256 * q + 256)
         bl = blocks(sp)
-        ur = (NU * t + unit(q, kh)) % NR
-        if kh == 0 or q in TALL:
-            v, w = bl[0][1], bl[0][3]
-            lin(OWN[t][q], r("UR", ur, None, (0, w)), r("UW", None, (v, v + w)), -1.0, 0.0)
-            if FAST[t][q] == "F":
-                dma("y", [(r("UR", ur, None, (a, a + w)), r("UR", ur, None, (0, w))) for a in range(w, 1024, w)])
-            while w < 1024 and FAST[t][q] != "F":
-                dma("y", [(r("UR", ur, None, (w, 2 * w)), r("UR", ur, None, (0, w)))])
-                w *= 2
-        how = GMODE[t][2 * sp:2 * sp + 2]
+        ur = ((4 + len(TALL)) * t + unit(q, kh)) % NR
+        if (kh == 0 or q in TALL) and q >= AHEAD[t]:
+            repeat(t, sp, "UW")
+        how = GMODE[t][sp]
+        neg = how == "S"
         for c in range(2):
-            if how[c] == "R":
-                tt(r("G", bg, c), ind(r("UW", c), onb(sp)), r("UR", ur, c), A.add)
-            elif how[c] == "F":
+            if how == "R":
+                tt(r("G", bg, c), ind(r("UW", c), onb(sp)), r("UR", ur, c), A.subtract)
+            elif how == "F":
                 for k, v, a, w in bl:
-                    tt(r("G", bg, c, (a, a + w)), ind(r("UW", c), onb(sp, a, w)), r("UR", ur, c, (0, w)), A.add)
+                    tt(r("G", bg, c, (a, a + w)), ind(r("UW", c), onb(sp, a, w)), r("UR", ur, c, (0, w)), A.subtract)
             else:
-                lin(how[c], r("G", bg, c), ind(r("UW", c), onb(sp)), 1.0, 0.0)
-        cs = (int(how[0] in "FR"), 2 - int(how[1] in "FR"))
-        if cs[0] < cs[1]:
-            dma("g", [(r("G", bg, cs), r("UR", ur, cs))], acc=True)
-        for c in range(2):
-            for h in range(2):
-                mm([(r("DXY", h, (a % 512, a % 512 + w)), r("SEL", 8 * c + k), r("D2", (v, v + w))) for k, v, a, w in bl if a // 512 == h])
-            if EADD[t][sp] == "V" and c:
-                tt(r("DXY"), r("G", bg, c), r("DXY"), A.mult)
-                tt(r("EE", be), r("EE", be), r("DXY"), A.add)
-            else:
-                tt(r("EE", (be, 3 + b)[c]), r("G", bg, c), r("DXY"), A.mult)
-        if EADD[t][sp] != "V":
-            dma("g", [(r("EE", be), r("EE", 3 + b))], acc=True)
-        qc, e, m, ap = r("QC", q, (4 * kh, 4 * kh + 4)), r("EE", be), r("EE", 3 + b), r("AP", b)
+                lin(how, r("G", bg, c), ind(r("UW", c), onb(sp)), -1.0, 0.0)
+        if neg:
+            dma("g", [(r("G", bg), r("UR", ur))], acc=True)
+        clip = CLIP[t][sp]
+        if clip in "BC" and not neg:
+            clip = "A"
+        en, e0, e1 = ("EE", be, 3 + b) if clip in "DEV" else (EBUF[t][sp % 2], 0, 1)
 
-        def bound(s):
-            for h in range(2):
-                ks = (4 * kh + 2 * h, 4 * kh + 2 * h + 2)
-                mm([(r("UL", h, (a % 512, a % 512 + w)), r("SEL", 8 * s + k), r("TT", (v, v + w))) for k, v, a, w in bl if a // 512 == h] +
-                   ([(r("UL", h), mx(NI), r("QC", q, ks))] if t else []))
-        bound(0)
-        if CLIP[t][sp] == "D":
-            tt(ap, e, r("UL"), A.subtract)
-            bound(1)
-            ts(ap, ap, 0.0, A.max, 1023.0, A.min)
-            tt(qc, e, r("UL"), A.subtract)
+        def spread(name, bank, h, tab, row):
+            return [(r(name, bank, (a % 512, a % 512 + w)), r("SEL", row + k), r(tab, (v, v + w))) for k, v, a, w in bl if a // 512 == h]
+
+        def runs(wide):
+            return [((0, 1024), [(0, 0), (1, 1)], [None, None])] if wide else \
+                [((512 * h, 512 * h + 512), [(None, h)], [0, 1]) for h in range(2)]
+        for hs, fill, bank in runs(WIDE[t][sp] in "WX"):
+            for c in range(2):
+                for x, h in fill:
+                    mm(spread("DXY", c if x is None else x, h, "D2", 8 * c))
+                z = r("DXY", bank[c])
+                if EADD[t][sp] == "V" and c:
+                    tt(z, r("G", bg, c, hs), z, A.mult)
+                    tt(r(en, e0, hs), r(en, e0, hs), z, A.add)
+                else:
+                    tt(r(en, (e0, e1)[c], hs), r("G", bg, c, hs), z, A.mult)
+        if EADD[t][sp] != "V":
+            dma("g", [(r(en, e0), r(en, e1))], acc=True)
+        qc, ap = r("QC", q, (4 * kh, 4 * kh + 4)), r("AP", b)
+        neg = not neg
+        for hs, fill, bank in runs(WIDE[t][sp] in "WY"):
+            e, m = r(en, e0, hs), r(en, e1, hs)
+            qh = r("QC", q, (1024 * kh + hs[0], 1024 * kh + hs[1]), raw=True)
+
+            def bound(s, c, whole=False):
+                for x, h in fill:
+                    x = c if x is None else x
+                    ks = (4 * kh + 2 * h, 4 * kh + 2 * h + 2)
+                    mm(spread("UL", x, h, "TT", 8 * s) + ([(r("UL", x), mx(IB_ if neg != whole else NI), r("QC", q, ks))] if t else []) +
+                       ([(r("UL", x), I32, r(en, e0, (512 * h, 512 * h + 512)))] if whole else []))
+                return r("UL", bank[c])
+
+            def less(out, z):
+                tt(out, *((z, e) if neg else (e, z)), A.subtract)
+            if clip in "AB":
+                act(r("AP", b, hs), bound(1 - neg, 0, True), F.Relu, scale=-1.0 if neg else 1.0)
+            elif clip == "C":
+                ts(r("AP", b, hs), bound(1, 0, True), 0.0, A.max, 1023.0, A.min)
+            elif clip == "D":
+                less(r("AP", b, hs), bound(int(neg), 0))
+            elif clip == "E":
+                less(m, bound(int(neg), 0))
+                act(r("AP", b, hs), m, F.Relu)
+            if clip in "ACD":
+                less(qh, bound(1 - neg, 1))
+            elif clip == "E":
+                for x, h in fill:
+                    mm(spread("UL", 1 if x is None else x, h, "T2", 0))
+                tt(qh, m, r("UL", bank[1]), A.add)
+            elif clip == "B":
+                tt(qh, bound(0, 1, True), r("AP", b, hs), A.min)
+            else:
+                tt(m, e, bound(0, 0), A.min)
+                z = bound(1, 1)
+                tt(z, m, z, A.max)
+                less(qh, z)
+        if clip in "ACDE":
+            if clip != "C":
+                ts(ap, ap, 0.0, A.max, 1023.0, A.min)
             ts(qc, qc, 0.0, A.min, -1023.0, A.max)
             dma("g", [(qc, ap)], acc=True)
-        else:
-            tt(m, e, r("UL"), A.min)
-            bound(1)
-            tt(r("UL"), m, r("UL"), A.max)
-            tt(qc, e, r("UL"), A.subtract)
         if MARK[t][sp] == "S":
             act(r("NZ", b), qc, F.Sign)
             act(r("NZ", b), r("NZ", b), F.Abs)
         else:
             ts(r("NZ", b), qc, 0.0, A.not_equal)
-        if CLIP[t][sp] != "D":
+        if clip in "BV":
             ts(qc, qc, -1023.0, A.max, 1023.0, A.min)
         tall = q in TALL
         first = [(r("CNT", 0), mx(I16), r("SC", (t + 1) % 2, unit(q, kh)))] if t and (kh == 0 or tall) else []
@@ -743,10 +854,11 @@ def build():
         s = r("XACC", None, js)
         cs = (vs[0] % 256, (vs[1] - 1) % 256 + 1)
         off = [(r("XS", 0, cs), mx(CX), r("D2", vs)), (r("XS", 1, cs), mx(CY), r("D2", vs))]
-        half = (r("XS", 0), mx(C64), r("MASK", (0, 256)))
+        half = [(r("XS", 1), r("I5"), r("LD", js)), (X1, mx(C64), r("MASK", (0, 512)))]
+        half = [(r("XS", None, (7 - b, 256, 8)), I32, r("WX", (0, 2), (128 * b + 32 * q, 128 * b + 32 * q + 32))) for b in byp(t)] + half
         byv = q < EARLY[t] or (FIN[t][q] in "VSA" and q < 3)
         if not h:
-            mm([(X1, I32, s), half] if q == 3 else off, True, False)
+            mm([(X1, I32, s)] + half if q == 3 else off if h is None else half[::-1], True, False)
         if t < 2:
             tt(r("LS", vs), r("LS", vs), sb, A.mult)
         if t:
@@ -755,7 +867,7 @@ def build():
         for b in range(4) if h is None else (2 * h, 2 * h + 1):
             tr = TRB[t][q == 3][b % 2]
             mm([(r(tr), sa, r("SEL", (4 * b, 4 * b + 4)))] +
-               [(r(tr, j), tile(q, 4 * b + j), mx(IB_)) for j in range(4)])
+               [(r(tr, j), tile(q, 4 * b + j), mx(NI)) for j in range(4)])
             qs = r("QS", (16 * (b % 2), 16 * (b % 2) + 16), (0, 3, 2))
             if EVAC[t][4 * q + b] == "S":
                 act(qs, r(tr), F.Relu, bias=-1024.0)
@@ -769,17 +881,24 @@ def build():
                     terms.append((r("XS", None, cs, p=(32 * pr, 32 * pr + 32)),
                                   r("QS", 4 * (j % 8) + pr, (odd, odd + 2)), r("DM", None, None, 128 * q + 8 * j + gg)))
             mm(terms, False, False)
-            if b % 2:
-                out = r("AB", 2 * q + b // 2) if t == 0 else r("AT", (4 * b - 4, 4 * b + 4))
+            if (t, u) in SPLIT:
+                act(r("AT", b // 2, (512 * (b % 2), 512 * (b % 2) + 512)), qs, F.Abs, bias=-1024.0)
+            elif b % 2:
+                out = r("AB", 2 * q + b // 2) if t == 0 else r("AT", b // 2)
                 act(out, r("QS", None, (0, 3, 2)), F.Abs, bias=-1024.0)
         if t == 1:
-            dma("g", [(r("AB", (2 * q, 2 * q + 2)), r("AT")) if h is None else (r("AB", 2 * q + h), r("AT", (8 * h, 8 * h + 8)))], acc=True)
+            dma("g", [(r("AB", (2 * q, 2 * q + 2)), r("AT")) if h is None else (r("AB", 2 * q + h), r("AT", h))], acc=True)
         plain = FIN[t][q] == "Q" and not byv
-        mm(off if q == 3 else [half] + [(X1, I32, s)] * plain, False, byv or (plain and h != 0))
+        mm((half if h is None else off) + [(X1, I32, s)] * (plain and q < 3 and h != 0), False, (byv or plain) and h != 0)
         if h == 0:
             return
         if byv:
-            tt(s, s, X1, A.add)
+            if LAY[t][q] == "V":
+                tt(s, s, X1, A.add)
+            else:
+                x = r("BASE", None, (256 * q, 256 * q + 256)) if t < 2 else r("WX", (0, 2), (0, 256))
+                act(x, X1, F.Identity)
+                dma("g", [(s, x)], acc=True)
             if q >= EARLY[t]:
                 close(s, FIN[t][q])
         elif plain:
@@ -825,10 +944,10 @@ def build():
             return r("UW", kh, (a, b))
 
         def back(out, j, u, ks):
-            return [(out, r("SEL", j), r("SS", u, ks)), (out, atile(q, j), r("MX", IB_, ks)), (out, r("AT", j), r("MX", IB_, ks))]
+            return [(out, r("SEL", j), r("SS", u, ks)), (out, atile(q, j), r("MX", IB_, ks)), (out, r("AT", j // 8, (128 * (j % 8), 128 * (j % 8) + 128)), r("MX", IB_, ks))]
         w = WBUF[q]
         for kh in range(2):
-            out = wg(kh, 0, 1024) if q == 3 else r(w, (8 * kh, 8 * kh + 8))
+            out = wg(kh, 0, 1024) if q == 3 else r(w, kh)
             lin(WMODE[2 * q + kh], out, ind(r("WW"), onb(2 * q + kh)), 1.0, 0.0)
             if q == 3:
                 vs, x = (768 + 128 * kh, 896 + 128 * kh), r("UL", kh, (0, 128))
@@ -846,28 +965,37 @@ def build():
                         tt(r("LS", vs), r("LS", vs), wg(kh, a, a + 128), A.add)
                 if WT3[kh] == "P":
                     act(r("LS", vs), x, F.Identity)
-                dma("s", [(hbm("yw", slice(None), slice(*vs)), r("LS", vs))])
+                dma(YW, [(hbm("yw", slice(None), slice(*vs)), r("LS", vs))])
                 continue
             for h in range(2):
-                mm([x for j in range(h, 16, 2) for x in back(x0(j // 2, 512, 8), j, unit(q, 0), (64 * kh, 64 * kh + 64))])
-                x = r(w, (1024 * kh + h, 1024 * kh + 1024, 2), raw=True)
+                if q in TALL:
+                    mm([y for j in range(8 * kh, 8 * kh + 8) for y in back(x0(j % 8, 512, 8), j, unit(q, kh), (64 * h, 64 * h + 64))])
+                    x = r(w, kh, (512 * h, 512 * h + 512))
+                else:
+                    mm([x for j in range(h, 16, 2) for x in back(x0(j // 2, 512, 8), j, unit(q, 0), (64 * kh, 64 * kh + 64))])
+                    x = r(w, kh, (h, 1024, 2))
                 tt(x, x, X0, A.mult)
         if q == 3:
             return
-        dma("g", [(r(w, (0, 8)), r(w, (8, 16)))], acc=True)
-        if WTREE[q] == "M":
-            mm([(x0(0, 256), I32, r("LS", js))] + [(x0(0, 256), I32, r(w, (2 * k, 2 * k + 2))) for k in range(4)])
-            act(r("LS", js), x0(0, 256), F.Identity)
-        if WTREE[q] == "D":
-            dma("g", [(r(w, (0, 4)), r(w, (4, 8)))], acc=True)
-            dma("g", [(r("LS", js), r(w, (0, 2)))], acc=True)
-            dma("g", [(r("LS", js), r(w, (2, 4)))], acc=True)
-        dma("s", [(hbm("yw", slice(None), slice(*js)), r("LS", js))])
+        if q in TALL:
+            tree = [(r(w, None, (0, 512)), r(w, None, (512, 1024))), (r(w, None, (0, 256)), r(w, None, (256, 512))),
+                    (r("LS", js), r(w, None, (0, 128))), (r("LS", js), r(w, None, (128, 256)))]
+        else:
+            tree = [(r(w, 0), r(w, 1)), (r(w, 0, (0, 512)), r(w, 0, (512, 1024))),
+                    (r("LS", js), r(w, 0, (0, 256))), (r("LS", js), r(w, 0, (256, 512)))]
+        if WTREE[q][0] == "H":
+            tree = [(r(w, 0, (0, 512)), r(w, 0, (512, 1024))), (r(w, 1, (0, 512)), r(w, 1, (512, 1024))),
+                    (r(w, 0, (0, 512)), r(w, 1, (0, 512))), (r(w, 0, (0, 256)), r(w, 0, (256, 512))), (r("LS", js), r(w, 0, (0, 256)))]
+        for x, who in zip(tree, WTREE[q][1:]):
+            if who == "D":
+                dma("g", [x], acc=True)
+            else:
+                tt(x[0], x[0], x[1], A.add)
+        dma(YW, [(hbm("yw", slice(None), slice(*js)), r("LS", js))])
 
     for t in range(3):
         up[0] = UP[t]
         dma("y", [(r("XACC", None, (768 if t else 0, 1024)), r("UW", None, (768 if t else 0, 1024)))])
-        dma("g", [(r("XACC", 1, (0, 1024)), r("BASE", (8, 16)))], acc=True)
         step1(t)
         if t:
             up[0] = UP3[t]
@@ -902,7 +1030,10 @@ def build():
                 weights(q)
         if t < 2:
             update(t, 0)
-            border()
+            for sp in range(2 * AHEAD[t + 1]):
+                if sp % 2 == 0 or sp // 2 in TALL:
+                    repeat(t + 1, sp, "XACC")
+            border(t + 1)
             la = ("LA1", "LA0")[t]
             send(r("SND", (0, 2)), [r(la, (2 * d, 2 * d + 2)) for d in range(3)], 3 * (t + 1))
             rows_update(t)
@@ -980,7 +1111,7 @@ def arrange(ops):
 
 
 def pace(ops, p):
-    wake = PACE["wake"] * p["wait"]
+    wake = PACE["wake"] * p["wake"]
     return (["vspgyx".index(o["eng"]) for o in ops], [o["cost"] * p["pe" if o["eng"] == "p" else o["sort"]] for o in ops],
             [o["by"] / PACE["rate"] * p["dma"] if o["kind"] == "dma" else 0.0 for o in ops],
             [PACE["rem"] * p["wait"] if o["kind"] == "send" else 0.0 for o in ops],
@@ -988,13 +1119,21 @@ def pace(ops, p):
             PACE["dlat"] * p["wait"] / 2, p["all"])
 
 
-def replay(order, m):
+def replay(order, m, at=0, old=None):
     eng, cost, dur, tail, lat, half = m[:6]
     n = len(order)
     free, last = [0.0] * 6, [-1] * 6
-    t0, t1, par, own = [0.0] * n, [0.0] * n, [-1] * n, [False] * n
+    t0, t1, par, own = [list(x) for x in old[:4]] if at else ([0.0] * n, [0.0] * n, [-1] * n, [False] * n)
     pipe, lastd = 0.0, -1
-    for i in order:
+    for x in range(at - 1, -1, -1):
+        i = order[x]
+        if last[eng[i]] < 0:
+            free[eng[i]], last[eng[i]] = t0[i] + cost[i], i
+        if dur[i] and lastd < 0:
+            pipe, lastd = t1[i] - half, i
+        if lastd >= 0 and min(last[:5]) >= 0:
+            break
+    for i in order[at:]:
         e = eng[i]
         s, p, w = free[e], last[e], True
         for j, l in lat[i]:
@@ -1017,19 +1156,102 @@ def replay(order, m):
 
 def smooth(ops, order, paces):
     eng, dep = paces[0][0], [set(o["dep"]) for o in ops]
+    n = len(ops)
+    outs = []
+    for m in paces:
+        outs.append([[] for o in ops])
+        for i in range(n):
+            for j, l in m[4][i]:
+                outs[-1][j].append((i, l))
+
+    def state(order, runs, at=None, old=None):
+        pos, pre, nxt, last = [0] * n, [-1] * n, [-1] * n, {}
+        pd, nd, ld = [-1] * n, [-1] * n, -1
+        for x, i in enumerate(order):
+            pos[i] = x
+            j = last.get(eng[i], -1)
+            if j >= 0:
+                pre[i], nxt[j] = j, i
+            last[eng[i]] = i
+            if paces[0][2][i]:
+                if ld >= 0:
+                    pd[i], nd[ld] = ld, i
+                ld = i
+        chains, rest = [], []
+        for k, (m, out, (t0, t1, par, own)) in enumerate(zip(paces, outs, runs)):
+            i, pairs = t1.index(max(t1)), []
+            while i >= 0:
+                if own[i] and par[i] >= 0:
+                    pairs.append(i)
+                i = par[i]
+            chains.append(pairs)
+            cost, dur, tail, half = m[1], m[2], m[3], m[5]
+            q, qd = old[k] if old else ([0.0] * (n + 1), [0.0] * (n + 1))
+            for i in order[at::-1]:
+                s = 0.0
+                for j, l in out[i]:
+                    if q[j] + l > s:
+                        s = q[j] + l
+                if dur[i]:
+                    qd[i] = dur[i] + max(s + half, qd[nd[i]])
+                    s = qd[i] + half
+                q[i] = cost[i] + max(s + tail[i], q[nxt[i]])
+            rest.append((q, qd))
+        return pos, pre, nxt, pd, nd, chains, rest
+
+    def guess(seg, new):
+        inside, tot = set(seg), 0.0
+        for m, out, run, (q, qd) in zip(paces, outs, runs, rest):
+            cost, dur, tail, lat, half = m[1:6]
+            t0, t1 = run[:2]
+            span = max(t0[i] + q[i] for i in seg)
+            free, last, pipe, ld, t, s2 = {}, {}, None, -1, {}, 0.0
+            for i in seg:
+                if eng[i] not in free:
+                    free[eng[i]] = t0[pre[i]] + cost[pre[i]] if pre[i] >= 0 else 0.0
+                last[eng[i]] = i
+                if dur[i]:
+                    if pipe is None:
+                        pipe = t1[pd[i]] - half if pd[i] >= 0 else 0.0
+                    ld = i
+            for i in new:
+                s = free[eng[i]]
+                for j, l in lat[i]:
+                    x = t.get(j, t1[j]) + l
+                    if x > s:
+                        s = x
+                s += cost[i]
+                free[eng[i]] = s
+                if dur[i]:
+                    pipe = max(pipe, s + half) + dur[i]
+                    s = pipe + half
+                t[i] = s = s + tail[i]
+                s2 = max(s2, s)
+                for j, l in out[i]:
+                    if j not in inside and s + l + q[j] > s2:
+                        s2 = s + l + q[j]
+            for e, i in last.items():
+                s2 = max(s2, free[e] + q[nxt[i]])
+            if ld >= 0:
+                s2 = max(s2, pipe + qd[nd[ld]])
+            tot += (s2 if span > run[4] - 1e-6 else max(s2, run[4])) / m[6]
+        return tot
     runs = [replay(order, m) for m in paces]
     cur = sum(max(x[1]) / m[6] for x, m in zip(runs, paces))
+    pos, pre, nxt, pd, nd, chains, rest = state(order, runs)
+    runs = [x + (max(x[1]),) for x in runs]
     seed = 1
     for it in range(SWAPS):
         seed = (seed * 1103515245 + 12345) % 2 ** 31
-        t0, t1, par, own = runs[it % len(runs)]
-        i, pairs = t1.index(max(t1)), []
-        while i >= 0:
-            if own[i] and par[i] >= 0:
-                pairs.append((par[i], i))
-            i = par[i]
-        a, b = pairs[(seed >> 8) % len(pairs)]
-        pa, pb = order.index(a), order.index(b)
+        pairs = chains[it % len(runs)]
+        b = pairs[(seed >> 8) % len(pairs)]
+        a = pre[b]
+        for k in range((0, 0, 1, 2)[seed >> 5 & 3]):
+            if seed >> 7 & 1 and nxt[b] >= 0:
+                b = nxt[b]
+            elif pre[a] >= 0:
+                a = pre[a]
+        pa, pb = pos[a], pos[b]
         seg = order[pa:pb + 1]
         if seed >> 7 & 1:
             mv, qs = {a}, set()
@@ -1048,11 +1270,17 @@ def smooth(ops, order, paces):
             new = [x for x in seg if x in mv] + [x for x in seg if x not in mv]
         if a in mv and b in mv:
             continue
+        room = SLACK * (1 - it / SWAPS)
+        s = guess(seg, new)
+        if s > cur + room + 1e-6 or (s > cur - 1e-6 and seed >> 12 & LEVEL):
+            continue
         od = order[:pa] + new + order[pb + 1:]
-        rs = [replay(od, m) for m in paces]
+        rs = [replay(od, m, pa, x) for m, x in zip(paces, runs)]
         s = sum(max(x[1]) / m[6] for x, m in zip(rs, paces))
-        if s <= cur + SLACK * (1 - it / SWAPS):
-            cur, runs, order = s, rs, od
+        if s <= cur + room + 1e-6:
+            cur, order = s, od
+            pos, pre, nxt, pd, nd, chains, rest = state(order, rs, pb, rest)
+            runs = [x + (max(x[1]),) for x in rs]
     return order
 
 
@@ -1287,6 +1515,8 @@ def rank_program(g, core, T, topo):
                 ins = q.tensor_tensor_scan(*x)
             elif kind == "act":
                 ins = q.activation(x[0], x[1], x[2], bias=x[3], scale=x[4])
+            elif kind == "sel":
+                ins = q.affine_select(*x)
             elif kind == "iota":
                 kw = {} if SCRATCH[a[0]["name"]][2] == i32 else {"allow_small_or_imprecise_dtypes": True}
                 ins = q.iota(*x, **kw)

from concourse.bass import DstId, RemoteDMATransfer
from concourse.mybir import dt, AluOpType, AxisListType, ActivationFunctionType

A = AluOpType
F = ActivationFunctionType
f32, b16, h16, i32, u16 = "float32", "bfloat16", "float16", "int32", "uint16"
E = 1792
BIG = float(2 ** 20)
RND = float(3 * 2 ** 22)
GMODE = ["S" * 16] * 3
DMODE = "S" * 8
WMODE = "S" * 8
EVAC = ["S" * 16] * 3
TRB = [(("TR", "TR"), ("TR", "X0"))] * 3
WTREE = "DDDP"
EADD = ["D" * 8] * 3
S1G = ["SS"] * 3
CONV = "vvv"
GMODE = ['RRSSSSSSSSSSSSSS', 'RRSSSSSSSSSSSSSS', 'RSSSSSSSSSSSSSSS']
EADD = ['VDDDDDDD', 'DDDDDDDD', 'VDDDDDDD']
S1G = ['VS', 'VS', 'VS']
DMODE = "VVSSSSSS"
FAST = ["FDDD"] * 3
CUT = ["SSSV"] * 3
MARK = ["VVVVVVVV"] * 3
CONV = 'svs'
S1Z = ["PP", "VP", "VP"]
S1C = ["VS", "VS", "VS"]
CONS = "V"
CPU = "VV"
WT3 = "PV"
CLOSE = "SSS"
GMG = "VVV"
WBUF = ("BASE", "WB", "BASE", "UW")
TALL = (3,)
PAR = [1, 1, 1]
FIN = ["PPPP"] * 3
UAC = ["GG"] * 3
CLIP = ["DDDDDDDV"] * 3
NG, NE, NR, NU = 2, 3, 3, 5
OWN = ["SSSS"] * 3
BORD = "VS"
EVG = "S"
PACE = {"ga": 1.56, "sc": 3.8, "wake": 0.1, "dlat": 1.6, "rate": 700e3, "gi": 1.0, "yi": 0.12, "rem": 4.0, "row": 1600}
LOOK = {"v": 0.05, "s": 0.05, "p": 0.05, "g": 0.05, "y": 0.05, "x": 0.05}
EARLY = [2, 2, 1]
RUN = 0.4
UP = [0.0, 0.0, 0.0]
UP2 = [0.0, 0.0, 0.0]
UP3 = [0.0, 0.0, 0.0]
GLOOK = 0.9
PASSES = 1
GMODE = ['FFSSSSSSSSSSSSSS', 'FRSSSSSSSSSSSSSS', 'FFSSSSSSSSSSSSSS']
FAST = ["DDDD"] * 3
EARLY, WT3, CLOSE, CONV = [0, 2, 0], "VV", "AAV", "svv"
S1G, S1Z, S1C = ['VS', 'VV', 'VV'], ['PV', 'VV', 'VD'], ['SS', 'VS', 'SS']
FIN = ['PVSP', 'PSVP', 'PAAP']
CUT = ['SSSV'] * 3
MARK = ['VVVVVVVV', 'VVVVVSVV', 'VVVVVVVV']
CLIP = ['VVVDVVVV', 'DVVVVVVV', 'DVVVVVVV']
EADD = ['DDDVDDDV', 'DDDDDDDD', 'DDDDDDDD']
LOAD = "V"
GMODE = ['FSSSSSSS'] * 3
UAM = "GGG"
OWN = ["GGGG"] * 3
EQM = "SSS"
INIT = "SSV"
ENDP = ["VVV"] * 3
ENDG = ["SSS"] * 3
ROWG = "SS"
AHEAD = [0, 0, 0]
FILL = "V"
EMP = "S"
LAY = ["VVVV"] * 3
YW = "y"
URG = [[1] * 5] * 3
EBUF = [("BASE", "WB")] * 3
BORD = ["VSV", "VS", "VS"]
S1S = ["SS"] * 3
PAR = [1, 1, 1]
INIT, ENDP, LOAD, CONV, EVG, EQM, CLOSE, CPU = 'VSV', ['PPV', 'VPV', 'VPV'], 'G', 'svv', 'S', 'SLL', 'AAA', 'SV'
EADD = ['DDDVDDDV', 'DDDDDDDV', 'DDDDDDDD']
BORD, UP3, UP2, EARLY = ['SSV', 'VS', 'VS'], [-5.0, 0.0, 0.0], [10.0, 0.0, 10.0], [1, 2, 0]
CLIP, ROWG, WT3, UAM = ['VVVDVVVV', 'DVDVVVVV', 'DVVDVVVV'], 'VV', 'VP', 'SVV'
S1G, OWN, S1S, DMODE, CONS = ['VS', 'SV', 'VV'], ['GGGG', 'GGGS', 'GGGG'], ['SS', 'GS', 'SS'], 'VSSVSSSS', 'S'
ENDG, CUT, MARK = ['SVS', 'SSV', 'SVS'], ['VSSS', 'SVSV', 'SSSS'], ['VVSVVVSV', 'SSVVVVSV', 'VVSVVVSS']
S1Z, S1C, FIN = ['DV', 'VV', 'VP'], ['VS', 'VV', 'SS'], ['SVSA', 'VSVP', 'PAAS']
WIDE = ["WWWWWWWW"] * 3
MARK = ["VVVVVVVV", "SVVVVVVV", "VVSVVVVV"]
URG = [[0, 1, 1, 2, 2]] * 3
WTREE = ["TDDDD", "TDDDD", "HDDVVV"]
SPLIT = [(2, 4)]
WT3, CUT, FIN, AHEAD = "VV", ['VSSS', 'SVSV', 'SSSV'], ['SVSA', 'VSVP', 'AAAP'], [0, 1, 1]
GMODE, CONV, UAM = ["FSSSSSSS", "RSSSSSSS", "RSSSSSSS"], "svs", "SSS"
ENDP, URG = ['VPV', 'VVV', 'VPV'], [[0, 3, 2, 3, 3], [1, 2, 2, 3, 3], [1, 2, 2, 3, 3]]
BORD, CLOSE, CPU, ROWG = ['SSV', 'VV', 'VS'], 'AVV', 'VV', 'VS'
CLIP, WTREE = ['VVVVVVVV', 'DVVVVVVV', 'DVVVVVVV'], ['TDDDD', 'HDDDVV', 'HDVVVV']
WIDE, OWN, S1S = ['WWWWWWWW', 'WWWWWWWW', 'WWWWWWHW'], ['GGVG', 'GGGS', 'GGGG'], ['SG', 'GS', 'SS']
DMODE, ENDG, CUT, MARK = 'VSSVSVSS', ['SSV', 'SSV', 'SVS'], ['VVSS', 'SVSV', 'SSVV'], ['VVVVVVVV'] * 3
S1C, FIN = ['VV'] * 3, ['QVSS', 'VSVA', 'AAAP']
LOOKS = [(0.05, 0.05, 0.05, 0.05, 0.05), (0.0, 0.1, 0.1, 0.3, 0.05)]
SWAPS, SLACK, LEVEL = 70000, 0.8, 3
PACES = [{"work": 1.0, "pe": 1.05, "pick": 1.0, "dma": 1.05, "wait": 1.0, "wake": 1.2, "all": 1.0},
         {"work": 1.25, "pe": 1.25, "pick": 1.65, "dma": 1.2, "wait": 1.3, "wake": 2.5, "all": 1.35},
         {"work": 1.1, "pe": 1.1, "pick": 0.9, "dma": 1.6, "wait": 1.6, "wake": 2.0, "all": 1.3},
         {"work": 1.4, "pe": 1.4, "pick": 1.3, "dma": 1.3, "wait": 1.3, "wake": 3.5, "all": 1.45}]
FIXED = 0.015


def _sb(shape, d):
    return ("sbuf", [128] + list(shape), d)


SCRATCH = {
    "QC": _sb([4, 2048], h16), "NZ": _sb([2, 1024], b16), "AP": _sb([2, 1024], h16), "TT": _sb([1024], h16),
    "T2": _sb([1024], b16),
    "QS": _sb([32, 3, 16], h16), "DM": _sb([2, 16, 512], h16), "AB": _sb([8, 1024], h16), "AT": _sb([2, 1024], h16),
    "G": _sb([NG, 2, 1024], h16), "EE": _sb([5, 1024], i32), "UR": _sb([NR, 2, 1024], h16),
    "UW": _sb([2, 1800], f32), "PW": _sb([1800], b16), "PO": _sb([1024], h16), "WW": _sb([1800], f32),
    "LS": _sb([1152], f32), "XACC": _sb([2, 1152], f32), "BASE": _sb([2, 1024], f32), "WB": _sb([2, 1024], f32),
    "SC": _sb([2, 4 + len(TALL), 128], b16), "SS": _sb([4 + len(TALL), 128], b16), "D2": _sb([1024], h16),
    "SEL": _sb([16, 128], b16), "LA0": _sb([6, 256], h16), "LA1": _sb([6, 256], h16), "SND": _sb([3, 256], h16),
    "NBI": _sb([8, 4, 16], i32), "BI": _sb([16], i32), "ONB": _sb([512], u16), "OB": _sb([16], u16),
    "PI": _sb([8], i32), "CL": _sb([32], f32), "IW": _sb([136], f32), "WC": _sb([144], b16),
    "C2": _sb([136], b16), "W2": _sb([136], b16), "PL": _sb([2, 8], b16), "UP": _sb([128], b16),
    "MX": _sb([32, 128], b16), "DIAG": _sb([128], f32), "MASK": _sb([1032], b16), "RS8": _sb([512], b16),
    "DK": _sb([2, 128], f32),
    "RS16": _sb([128], f32), "DUMM": _sb([128], f32), "VID": _sb([128], f32),
    "LD": _sb([1024], h16), "I5": _sb([128], b16),
    "GM": _sb([1024], h16), "D1": _sb([512], h16), "MB": _sb([512], b16), "CM": _sb([512], h16),
    "NF": _sb([128], f32), "S1": _sb([128], f32), "SCN": _sb([128], f32), "S2": _sb([128], f32), "SC2": _sb([128], f32),
    "U16": _sb([128], h16), "EV": _sb([128], b16), "FV": _sb([128], b16), "FC": _sb([128], b16),
    "MD": _sb([128], f32), "DF": _sb([128], f32), "ON": _sb([64], u16), "OC": _sb([64], u16), "OX": _sb([64], u16),
    "OM": _sb([8], u16), "OT": _sb([24], u16), "OVV": _sb([2, 128], h16), "OVC": _sb([2, 128], h16),
    "DE": _sb([384], b16), "SE": _sb([384], b16), "QE": _sb([384], h16),
    "WX": _sb([3, 384], f32), "EN": _sb([384], b16), "ET": _sb([384], h16), "EC": _sb([768], h16),
}
SCRATCH["DXY"] = ("psum", [128, 2, 512], f32)
SCRATCH["UL"] = ("psum", [128, 2, 512], f32)
SCRATCH["XS"] = ("psum", [128, 2, 256], f32)
for _n in ("TR", "X0"):
    SCRATCH[_n] = ("psum", [128, 512], f32)
SCRATCH["CNT"] = ("psum", [128, 4, 128], f32)
SIZE = {f32: 4, i32: 4, b16: 2, h16: 2, u16: 2}
NDS = 130
SEMAPHORES = ["cv", "cs", "cp", "cg"] + ["d%d" % i for i in range(NDS)] + \
    ["ar%d" % i for i in range(12)] + ["lo%d" % i for i in range(4)]
(BLK, IB_, NI, DXP, D8, DYP, ND8, PX_, PY_, MT, ONC, MC, SCO, NBG, PBG, NON, KC, TRI, BD0, BD1, BD2, I16, QE8,
 CX, CY, RN, NRN, SC2, NMT, D16, C64, OW) = range(32)


UNIT = {"TR": (0, 128), "X0": (0, 128),
        "QC": (1, 256), "NZ": (1, 256)}


def r(name, *ix, p=None, raw=False):
    shape = SCRATCH[name][1][1:]
    ix = list(ix) + [None] * (len(shape) - len(ix))
    if name in UNIT and not raw:
        d, u = UNIT[name]
        if ix[d] is not None:
            ix[d] = (u * ix[d], u * ix[d] + u) if isinstance(ix[d], int) else (u * ix[d][0], u * ix[d][1])
    n = 1
    out = []
    spans = [(0, 1)]
    st = 1
    for x, w in reversed(list(zip(ix, shape))):
        if isinstance(x, int):
            a, c, s = x, 1, 1
            out.append(x)
        else:
            a, b, s = (0, w, 1) if x is None else (tuple(x) + (1,))[:3]
            c = (b - a + s - 1) // s
            out.append(slice(a, b, s) if s != 1 else slice(a, b))
        n *= c
        lo, hi = spans[0][0], spans[-1][1]
        if st == 1 or c * len(spans) > 32 or (len(spans) == 1 and s == 1 and hi - lo == st):
            spans = [(lo + a * st, hi + (a + (c - 1) * s) * st)]
        else:
            spans = [(u + (a + q * s) * st, v + (a + q * s) * st) for q in range(c) for u, v in spans]
        st *= w
    ps = slice(None) if p is None else slice(*p)
    if name == "DM":
        spans = [(out[0], out[0] + 1) if isinstance(out[0], int) else (out[0].start, out[0].stop)]
    if SCRATCH[name][0] == "psum":
        spans = [(spans[0][0] // 512 * 512, (spans[-1][1] - 1) // 512 * 512 + 512)]
    return {"k": "b", "name": name, "ix": (ps,) + tuple(reversed(out)), "spans": spans, "n": n}


def ind(win, off):
    return {"k": "i", "win": win, "off": off, "n": off["n"] * 16, "name": win["name"]}


def hbm(name, *ix):
    return {"k": "h", "name": name, "ix": ix}


def mx(i):
    return r("MX", i)


def col(i):
    return r("CL", (i, i + 1))


def _ap(T, x):
    if not isinstance(x, dict):
        return x
    if x["k"] == "i":
        return _ap(T, x["win"]).indirect(_ap(T, x["off"]))
    if x["k"] == "h":
        return T[x["name"]][x["ix"]] if x["ix"] else T[x["name"]][:]
    return T[x["name"]][x["ix"]]


def _parts(x):
    if not isinstance(x, dict) or x["k"] == "h":
        return []
    return [x["win"], x["off"]] if x["k"] == "i" else [x]


def _two(x):
    return SIZE[SCRATCH[x["name"]][2]] == 2


def _ps(x):
    return SCRATCH[x["name"]][0] == "psum"


def build():
    ops = []
    up = [0.0]

    def add(eng, kind, args, outs, ins, cost, **kw):
        w, rd = [], []
        for o in outs:
            q = _parts(o)
            w += q[:1]
            rd += q[1:]
        for o in ins:
            rd += _parts(o)
        d = {"eng": eng, "kind": kind, "args": args, "w": w, "r": rd, "cost": cost, "up": up[0]}
        d["sort"] = "dma" if kind in ("dma", "send") else "pick" if any(
            isinstance(x, dict) and x["k"] == "i" for x in list(outs) + list(ins)) else "work"
        d.update(kw)
        ops.append(d)
        return len(ops) - 1

    def vc(out, in0, c):
        if out["k"] == "i":
            return 0.05 + out["n"] * PACE["sc"] * 0.00083
        if in0 is not None and in0["k"] == "i":
            return 0.05 + out["n"] * PACE["ga"] * 0.00083
        return FIXED + max(64, out["n"] * c) * 0.00083

    def tt(out, a, b, op):
        add("v", "tt", (out, a, b, op), [out], [a, b], vc(out, a, 1 if _ps(a) or _ps(b) else 2))

    def ts(out, a, s1, o0, s2=None, o1=None):
        add("v", "ts", (out, a, s1, s2, o0, o1), [out], [a, s1, s2], vc(out, a, 0.5 if _two(out) and _two(a) else 1))

    def cp(out, a):
        add("v", "cp", (out, a), [out], [a], vc(out, a, 0.5 if _two(out) and _two(a) else 1))

    def ms(out, v):
        add("v", "ms", (out, v), [out], [], vc(out, None, 0.5 if _two(out) else 1))

    def scan(out, d0, d1, init, o0, o1):
        add("v", "scan", (out, d0, d1, init, o0, o1), [out], [d0, d1], vc(out, d0, 1))

    def act(out, a, fn, bias=0.0, scale=1.0):
        add("s", "act", (out, a, fn, bias, scale), [out], [a, bias, scale],
            (0.065 if a["k"] == "i" else FIXED) + max(64, out["n"] * (PACE["ga"] if a["k"] == "i" else 1)) * 0.00083)

    def lin(who, out, a, scale, bias):
        if who == "G":
            sel(out, a)
        elif who in "Ss":
            act(out, a, F.Identity, bias=bias, scale=scale)
        else:
            ts(out, a, scale, A.mult, bias, A.add)

    def mm(terms, start=True, stop=True):
        c, ins, run = 0.0, [], []
        for m, (o, l, x) in enumerate(terms):
            c += max(min(64, l["n"]), x["n"]) * (1 if _two(x) else 4) * 0.000417
            ins += [l, x]
            run.append((o, l, x))
            if c >= RUN or m == len(terms) - 1:
                add("p", "mm", (run, start, stop and m == len(terms) - 1), [o], ins, c + 0.02, cont=not start)
                c, ins, run, start = 0.0, [], [], False

    def iota(out, pat, base, cm):
        add("g", "iota", (out, pat, base, cm), [out], [], 0.13 + out["n"] * 0.00166)

    def sel(out, a):
        add("g", "sel", (out, a, [[0, out["n"]]], A.is_gt, 0.0, 1, 0), [out], [a], 0.17 + out["n"] * 0.00166)

    def dma(q, pairs, acc=False, nb=None):
        by = rows = 0
        for o, i in pairs:
            x = o if o["k"] == "b" else i
            by += x["n"] * SIZE[SCRATCH[x["name"]][2]] * 128
            rows += max(len(y["spans"]) for y in (o, i) if y["k"] == "b") * (128 if x["ix"][0].step is None else 8)
        add(q, "dma", (pairs, acc), [o for o, i in pairs], [i for o, i in pairs],
            PACE["gi" if q == "g" else "yi"] * len(pairs), by=(nb or by) * (2 if acc else 1) + rows * PACE["row"], rows=rows)

    def send(src, land, base):
        s = add("g", "send", (src, land, base), [], [src], 2.0)
        for d in range(3):
            add("x", "recv", (base, d), [land[d]], [], 0.0, after=s)

    def x0(a, b, s=1):
        return r("X0", (a, b, s), raw=True)

    def x1(a, b, s=1):
        return r("TR", (a, b, s), raw=True)

    X0, X1 = r("X0"), r("TR")
    IC = r("EE", 2)

    dma("s", [(r("EE", 2, p=(8 + j, 128, 16)), hbm("py" if j & 2 else "px")) for j in range(8)], nb=400000)
    dma("y", [(r("EE", 2, p=(k, 128, 16)), hbm("nb", slice(None), slice(64 * k, 64 * k + 64))) for k in range(8)], nb=600000)
    ops[1]["beside"] = 0
    dma("y", [(r("EE", 0), hbm("ux")), (r("BI"), hbm("bord"))])
    dma("s", [(r("EE", 1), hbm("uy"))])
    dma("s", [(r("NBI"), hbm("nb"))])
    iota(r("PI", (0, 1)), [[0, 1]], 0, 1)
    iota(r("WX", 2, (0, 144)), [[1, 144]], 0, -1)
    iota(r("DIAG"), [[0, 8], [1, 16]], 0, 0)
    iota(r("S1"), [[16, 8], [0, 16]], 0, -1)
    iota(r("MASK"), [[0, 129], [1, 8]], 0, 0)
    iota(r("NF", (0, 64)), [[1, 64]], 0, 64)
    ts(r("PI", (1, 2)), r("PI", (0, 1)), 15, A.bitwise_and)
    ts(r("PI", (2, 3)), r("PI", (0, 1)), 8, A.bitwise_and)
    ts(r("PI", (3, 4)), r("PI", (0, 1)), 112, A.bitwise_and)
    cp(col(0), r("PI", (1, 2)))
    cp(col(1), r("PI", (2, 3)))
    ts(col(2), col(0), 8.0, A.is_lt)
    ts(r("DIAG"), r("DIAG"), col(0), A.is_equal)

    def oh(i):
        return r("DIAG", (i, i + 1))

    def mkcol(c, terms, first=0.0):
        prev = first
        for row, v in terms:
            act(col(c), oh(row), F.Identity, bias=prev, scale=float(v))
            prev = col(c)
    tt(r("CL", (3, 5)), r("DIAG", (8, 12, 2)), r("DIAG", (9, 12, 2)), A.subtract)
    tt(r("CL", (21, 23)), r("DIAG", (8, 12, 2)), r("DIAG", (9, 12, 2)), A.add)
    ts(col(16), col(0), 14.0, A.is_ge, col(3), A.add)
    act(col(7), col(4), F.Identity, bias=col(16))
    act(col(15), oh(12), F.Identity, bias=col(7))
    ts(col(18), col(0), 8.0, A.is_ge)
    ts(r("MASK"), r("MASK"), col(0), A.is_equal, col(15), A.add)
    ts(col(30), col(0), 12.0, A.is_ge, col(18), A.subtract)
    lin(INIT[0], r("PO"), IC, col(30), col(7))
    cp(r("OB"), r("BI"))
    for c in range(2):
        lin(CPU[c], r("UW", c, (0, 1024)), r("EE", c), 1.0, 0.0)
    ts(r("IW"), r("WX", 2, (0, 136)), 8.0, A.is_equal)
    I32 = r("IW", (8, 136))
    act(mx(IB_), I32, F.Identity)
    act(mx(NI), I32, F.Identity, scale=-1.0)
    for h in range(2):
        hs, x = (512 * h, 512 * h + 512), (X0, X1)[h]
        mm([(x, mx(IB_), r("MASK", hs)), (x, mx(NI), r("PO", hs))])
        act(r("PW", hs), x, F.Identity)

    def border(t):
        for c in range(2):
            lin(BORD[t][c], r("SND", c), ind(r("UW", c, (0, 1024)) if t else r("EE", c), r("OB")), 1.0, 0.0)
    border(0)
    ts(col(17), col(30), -1.0, A.mult)
    ts(col(19), oh(12), col(2), A.add)
    lin(BORD[0][2], r("SND", 2), ind(IC, r("OB")), col(17), col(19))
    send(r("SND"), [r("AB", d, (0, 768)) for d in range(3)], 0)
    for q in range(4):
        if q in TALL:
            for h in range(2):
                cp(r("ONB", (128 * q + 64 * h, 128 * q + 64 * h + 64)), r("NBI", None, q, (8 * h, 8 * h + 8)))
        else:
            cp(r("ONB", (128 * q, 128 * q + 128)), r("NBI", None, q))
    def zero(out):
        iota(out, [[0, out["n"]]], 0, 0) if FILL == "G" else ms(out, 0.0)
    zero(r("UW", None, (1792, 1800)))
    zero(r("WW", (1792, 1800)))
    ts(r("PW", (1792, 1800)), r("MASK", (0, 8)), 0.0, A.mult, col(2), A.add)
    zero(r("LS", (1024, 1152)))
    ts(col(28), r("PI", (3, 4)), -64.0, A.mult)
    ts(r("ON"), r("NF", (0, 64)), col(28), A.add)
    act(col(29), col(2), F.Identity, scale=-float(E))
    lin(INIT[1], r("LS", (0, 1024)), ind(IC, r("ON")), col(2), col(29))
    ts(mx(BLK), r("S1"), col(0), A.add, 0.0, A.is_equal)
    ts(r("WC"), r("WX", 2, (0, 144)), col(0), A.add, 15.0, A.is_equal)
    act(col(5), col(30), F.Identity, scale=-32.0)
    mkcol(5, [(12, -32768), (15, 32640)], first=col(5))
    mkcol(6, [(12, 32768), (15, -23552)])
    mkcol(8, [(15, -BIG), (14, 1)])
    act(r("CL", (9, 12)), r("DIAG", (5, 8)), F.Identity, bias=col(8), scale=-BIG)
    mkcol(12, [(15, -1)], first=1.0)
    mkcol(13, [(15, 200)])
    ts(col(14), col(0), -2048.0, A.mult, 16128.0, A.add)
    act(col(23), col(18), F.Identity, bias=-0.5)
    act(col(25), col(23), F.Identity, scale=-1 / 16)
    ts(col(27), col(0), col(1), A.subtract)
    iota(r("S2"), [[0, 16], [1, 8]], 0, 0)
    ts(r("S2"), r("S2"), col(27), A.is_equal)
    tt(mx(D8), r("S2"), mx(BLK), A.mult)
    act(r("UP"), r("IW", (0, 128)), F.Identity)
    act(mx(D16), r("DIAG"), F.Identity)
    for c in range(2):
        ts(r("PL", c), r("MX", BLK, (0, 128, 16)), col(21 + c), A.mult, 1 / 64, A.mult)
    for m, s, c, v in ((DXP, BLK, col(3), 0.25), (DYP, BLK, col(4), 0.25), (PX_, BLK, col(3), 1 / 128), (PY_, BLK, col(4), 1 / 128),
                       (KC, BLK, col(14), col(2)), (CX, BLK, col(2), -65536.0), (CY, BLK, col(18), -65536.0),
                       (NBG, BLK, col(23), -BIG), (RN, BLK, oh(15), RND), (NRN, BLK, oh(15), -RND), (C64, BLK, oh(15), 1 / 64),
                       (ND8, D8, col(2), -1.0), (QE8, D8, col(2), 512.0)):
        ts(mx(m), mx(s), c, A.mult, v, A.mult)
    for m, s, v in ((MT, BLK, col(5)), (MC, BLK, col(6)), (BD0, BLK, col(11)), (BD1, BLK, col(10)), (BD2, BLK, col(9)),
                    (ONC, BLK, 1024.0), (SCO, BLK, 16384.0), (PBG, BLK, BIG), (NON, BLK, -1.0), (SC2, BLK, 8192.0),
                    (NMT, MT, -1.0), (I16, IB_, 16.0)):
        if (m not in (SC2, NMT) or "S" in "".join(S1C)) and (m != SCO or "V" in "".join(S1C)):
            ts(mx(m), mx(s), v, A.mult) if CONS == "V" else act(mx(m), mx(s), F.Identity, scale=v)
    ts(mx(TRI), r("WX", 2, (0, 128)), 0.0, A.is_gt, -2.0, A.mult)
    tt(mx(TRI), mx(TRI), I32, A.add)
    ts(r("S2"), mx(BLK), col(2), A.mult)
    tt(mx(TRI), mx(TRI), r("S2"), A.mult)
    ts(r("W2"), r("WC", (8, 144)), col(21), A.mult, 1 / 4096, A.mult)
    ts(r("C2"), r("WC", (0, 136)), col(22), A.mult, 1 / 4096, A.mult)
    tt(r("W2"), r("W2"), r("C2"), A.add)
    mm([(x0(0, 128), r("W2", (7 - k, 135 - k)), mx(IB_)) for k in range(8)])
    act(mx(OW), x0(0, 128), F.Identity)
    mm([(x0(0, 128), mx(OW), mx(IB_))])
    act(mx(OW), x0(0, 128), F.Identity)
    tt(r("C2"), r("WC", (0, 136)), r("WC", (8, 144)), A.add)
    iota(r("DF"), [[-1, 128]], 1152, 0)
    tt(r("DUMM"), r("DF"), r("DIAG"), A.mult)
    iota(r("RS8"), [[0, 512]], 1, 0)
    zero(r("RS8", (0, 512, 8)))
    iota(r("DK", 0), [[-1, 128]], 1152 + 71 * 2048, 0)
    iota(r("DK", 1), [[-1, 128]], 1152 + 7 * 2048, 0)
    iota(r("RS16"), [[0, 128]], 1, 0)
    zero(r("RS16", (0, 128, 16)))
    scan(r("MD"), r("RS16"), r("DUMM"), 0.0, A.mult, A.add)
    zero(r("XACC", None, (1024, 1152)))
    sel(r("QE", (0, 256)), r("XACC", None, (1024, 1152)))
    sel(r("QE", (256, 384)), r("LS", (1024, 1152)))
    dma("y", [(r("EE", 4), hbm("ld"))])
    dma("y", [(r("WW", (0, 1024)), hbm("wt"))])
    lin(LOAD, r("LD"), r("EE", 4), 1.0, 0.0)
    act(r("I5"), I32, F.Identity, scale=1 / 32)
    iota(r("SEL"), [[1, 16], [16, 8], [0, 16]], 0, -1)
    ts(r("SEL"), r("SEL"), 0.0, A.is_equal, 2048.0, A.mult)
    ms(r("DM", 0, 0), 0.0)
    sel(r("QS", None, 1), r("DM", 0, 0))
    for z in (1, 2, 4, 8):
        dma("y", [(r("DM", 0, (z, 2 * z)), r("DM", 0, (0, z)))])
    dma("y", [(r("DM", 1), r("DM", 0))])

    def convert(t):
        for d in range(3):
            la = r(("LA1", "LA0")[t - 1], (2 * d, 2 * d + 2)) if t else r("AB", d, (0, 512))
            lin(CONV[d], r("UW", None, (1024 + 256 * d, 1280 + 256 * d)), la, 1.0, 0.0)
            if t == 0:
                cp(r("PW", (1024 + 256 * d, 1280 + 256 * d)), r("AB", d, (512, 768)))
    convert(0)

    def step1(t):
        rho = 7 - t
        LSW = r("LS")
        act_ls = r("LS", (rho, 1024, 8))
        lin(S1S[t][0], r("U16"), act_ls, 1.0, 0.0)
        mm([(x0(0, 64), mx(IB_), r("U16", (0, 128, 2))), (x0(0, 64), r("UP"), r("U16", (1, 128, 2)))])
        ts(r("ON"), x0(0, 64), float(E), A.add, 1024.0, A.min)
        if GMG[t] == "V":
            tt(r("GM"), ind(LSW, r("ON")), r("MASK", (t, t + 1024)), A.mult)
        else:
            act(r("AP", 0), ind(LSW, r("ON")), F.Identity, scale=1 / 2048)
            for h in range(2):
                mm([((x0, x1)[h](k, 512, 8), r("SEL", (k + t) % 8), r("AP", 0, (512 * h + k, 512 * h + 512, 8))) for k in range(8)])
                act(r("GM", (512 * h, 512 * h + 512)), (X0, X1)[h], F.Identity, scale=oh(0))
        act(r("FC"), act_ls, F.Relu, bias=1.0, scale=2.0)
        mm([(x1(0, 128), mx(TRI), r("FC"))])
        act(r("FV"), x1(0, 128), F.Relu)
        mm([(x0(0, 64), r("WC", (15 - i, 143 - i)), r("GM", (i, 1024, 16))) for i in range(16)])
        ts(r("OX"), x0(0, 64), float(E), A.add, 1023.0, A.min)
        ts(r("OC"), x0(0, 64), float(E), A.add)
        if UAM[t] == "G":
            for k in range(8):
                sel(r("AP", None, (k, 1024, 8)), r("UW", None, (rho, 1024, 8)))
        else:
            lin(UAM[t], r("AP", None, (0, 1024, 8)), r("UW", None, (rho, 1024, 8)), 1.0, 0.0)
            for k in range(1, 8):
                cp(r("AP", None, (k, 1024, 8)), r("AP", None, (0, 1024, 8)))
        for h in range(2):
            o, hs = (32 * h, 32 * h + 32), (512 * h, 512 * h + 512)
            neg = S1G[t][h] == "S"
            ua = [r("AP", 0, hs), r("AP", 1, hs), r("AP", None, hs)]
            if t:
                ds = [r("AT", h, (0, 512)), r("AT", h, (512, 1024)), r("AT", h)]
            else:
                ds = [r("AB", 5 + h, (0, 512)), r("AB", 5 + h, (512, 1024)), r("AB", 5 + h)]
            if h == 0:
                ex, ey = r("WB", 1, (0, 512)), r("WB", 1, (512, 1024))
                d1, mb, cm = r("D1"), r("MB"), r("CM")
                y0, y1 = x0, x1
            else:
                ex, ey = r("WB", 0, (0, 512)), r("WB", 0, (512, 1024))
                if PAR[t]:
                    d1, mb, cm = r("NZ", 0, (0, 2)), r("NZ", 0, (2, 4)), r("NZ", 1, (0, 2))
                if PAR[t] in (1, 3):
                    y0, y1 = [lambda a, b, s=1, z=z: r(("UL", "DXY")[PAR[t] // 2], z, (a, b, s)) for z in range(2)]
            Y0, Y1 = y0(0, 512), y1(0, 512)
            for c in range(2):
                if neg:
                    act(ds[c], ind(r("UW", c, (0, 1024)), r("OX", o)), F.Identity, scale=-1.0)
                else:
                    tt(ds[c], ind(r("UW", c, (0, 1024)), r("OX", o)), ua[c], A.subtract)
            if neg:
                dma("g", [(ds[2], ua[2])], acc=True)
            act(d1, ind(r("PW"), r("OC", o)), F.Identity)
            gm = r("GM", (512 * h, 512 * h + 512))
            mm([(Y1, mx(BLK), gm)] + [(y1(k, 512, 8), mx(ND8), r("U16", (64 * h, 64 * h + 64))) for k in range(8)])
            act(mb, Y1, F.Sign, bias=col(23))
            mm([(Y0, mx(IB_), d1)] +
               [(y0(k, 512, 8), mx(IB_), r("PO", (512 * h + rho, 512 * h + 512, 8))) for k in range(8)])
            act(d1, Y0, F.Square)
            mm([(Y0, mx(DXP), d1)])
            mm([(Y1, mx(DYP), d1)])
            tt(ex, ds[0], Y0, A.mult)
            if S1Z[t][h] == "V":
                tt(Y1, ds[1], Y1, A.mult)
                tt(ex, ex, Y1, A.add)
                act(ex, ex, F.Abs)
            elif S1Z[t][h] == "D":
                tt(ey, ds[1], Y1, A.mult)
                dma("g", [(ex, ey)], acc=True)
                act(ex, ex, F.Abs)
            else:
                tt(ey, ds[1], Y1, A.mult)
                mm([(Y0, I32, ex)], True, False)
                mm([(Y0, I32, ey)], False, True)
                act(ex, Y0, F.Abs)
            if S1C[t][h] == "S":
                mm([(Y1, mx(NMT), d1), (Y1, I32, ex)])
                act(cm, Y1, F.Sign, bias=-0.5)
            else:
                mm([(Y1, mx(MT), d1)])
                tt(cm, ex, Y1, A.is_gt)
            mm([(Y0, mx(BLK), gm), (Y0, mx(KC), r("MASK", (0, 512))), (Y0, mx(BD0 + t), d1), (Y0, mx(NBG), mb)] +
               [(y0(k, 512, 8), mx(PBG), r("FV", (64 * h, 64 * h + 64))) for k in range(8)] +
               [(Y0, mx(SC2 if S1C[t][h] == "S" else SCO), cm)])
            scan(ey, r("RS8"), Y0, 0.0, A.mult, A.max)
            tt(r("NBI", h), r("WB", 1 - h, (519, 1024, 8)), r("DK", int(S1C[t][h] == "S"), (64 * h, 64 * h + 64)), A.max)
        up[0] = UP2[t]
        nm = r("NBI", (2, 4))
        ts(nm, r("NBI", (0, 2)), 2047, A.bitwise_and)
        tt(r("S1"), nm, r("DIAG"), A.mult)
        lin(S1S[t][1], r("NF"), nm, 1.0, 0.0)
        scan(r("SCN"), r("RS16"), r("S1"), 0.0, A.mult, A.add)
        ts(r("OM"), r("SCN", (15, 128, 16)), -1.0, A.add)
        act(r("EV"), ind(LSW, r("OM")), F.Relu, bias=1.0, scale=2.0)
        mm([(x0(128, 256), mx(TRI), r("EV"))])
        ms(r("GM", (0, 1)), 0.0)
        tt(r("GM", (1, 128)), r("NF", (1, 128)), r("SCN", (0, 127)), A.is_equal)
        act(r("GM", (128, 256)), r("NF"), F.Relu, bias=-1024.0)
        terms = [(x0(0, 128), mx(NON), r("GM", (0, 128))), (x0(0, 128), mx(NON), r("GM", (128, 256)))]
        at = 256
        for j in range(7):
            a = 16 * (j + 1)
            ts(r("GM", (at, at + 128 - a)), r("NF", (a, 128)), r("SCN", (a - 1, a)), A.is_equal)
            terms.append((x0(a, 128), mx(NON), r("GM", (at, at + 128 - a))))
            at += 128 - a
        act(r("FC"), x0(128, 256), F.Relu)
        tt(r("DF"), r("S1"), r("DUMM"), A.subtract)
        mm(terms + [(x0(0, 128), mx(BLK), r("FC"))])
        act(x0(0, 128), x0(0, 128), F.Relu)
        tt(r("S2"), r("DF"), x0(0, 128), A.mult)
        act(r("SE", (128 * t, 128 * t + 128)), x0(0, 128), F.Identity, bias=oh(15), scale=col(12))
        scan(r("SC2"), r("RS16"), r("S2"), 0.0, A.mult, A.add)
        tt(r("S2", (0, 8)), r("SC2", (15, 128, 16)), r("MD", (15, 128, 16)), A.add)
        ts(ot(t), r("S2", (0, 8)), -1.0, A.add)
        de = r("DE", (128 * t, 128 * t + 128))
        tt(de, ind(r("PW"), ot(t)), r("PO", (rho, 1024, 8)), A.add)
        act(de, de, F.Square)
        if t < 2:
            act(r("S1"), r("NF"), F.Identity, bias=-1.0 - E)
            tt(r("OVV", t), r("S1"), r("FV"), A.mult)
            iota(r("VID"), [[8, 128]], rho - E, 0)
            tt(r("OVC", t), r("VID"), r("FC"), A.mult)

    def ec(t, lo, hi):
        return r("EC", (64 * t * (t + 1) + 128 * lo, 64 * t * (t + 1) + 128 * hi))

    def extras(t, lo, hi, banks):
        w = (128 * lo, 128 * hi)
        ex, ey, ez = r("WX", 0, w), r("WX", 1, w), r("WX", 2, w)
        bx, by = banks
        de, se, qe, en, et = [r(x, w) for x in ("DE", "SE", "QE", "EN", "ET")]
        eq = ec(t, lo, hi)
        for b in range(lo, hi):
            act(r("WX", (0, 2), (128 * b, 128 * b + 128)), r("UW", None, (7 - b, 1024, 8)), F.Identity)
        for c in range(2):
            tt(r("WX", c, w), ind(r("UW", c, (0, 1152)), r("OT", (8 * lo, 8 * hi))), r("WX", c, w), A.subtract)
        mm([(bx, mx(DXP), de)])
        mm([(by, mx(DYP), de)])
        tt(ex, ex, bx, A.mult)
        tt(ey, ey, by, A.mult)
        mm([(bx, mx(IB_), qe), (bx, I32, ex)], True, False)
        mm([(bx, I32, ey)], False, True)
        act(ez, bx, F.Abs)
        act(bx, bx, F.Sign)
        mm([(by, mx(MT), de)])
        tt(ez, ez, by, A.subtract)
        act(en, ez, F.Sign, bias=-0.5)
        mm([(by, mx(MC), se), (by, mx(ONC), en)])
        tt(et, ez, by, A.min)
        ts(eq, et, 0.0, A.max, 1023.0, A.min)
        tt(qe, eq, bx, A.mult)
        if t < 2:
            act(se, by, F.Sigmoid, bias=col(13), scale=col(12))
        mm([(bx, mx(PX_), de)])
        tt(ex, qe, bx, A.mult)
        mm([(by, mx(PY_), de)])
        tt(ey, qe, by, A.mult)

    def ot(b):
        return r("OT", (8 * b, 8 * b + 8))

    def into(who, x, y, op, tmp):
        if who == "S":
            act(tmp, x, F.Identity)
            tt(x, tmp, y, op)
        else:
            tt(tmp, x, y, op)
            cp(x, tmp)

    def byp(t):
        return [b for b in range(t + 1) if ENDP[t][b] == "P" and (b < t or not EARLY[t])]

    def ends(t, lo, hi):
        for b in range(lo, hi):
            bs = (128 * b, 128 * b + 128)
            own = r("XACC", None, (7 - b, 1024, 8))
            if b not in byp(t):
                tt(own, own, r("WX", (0, 2), bs), A.add)
            for c in range(2):
                into(ENDG[t][b], ind(r("XACC", c), ot(b)), r("WX", c, bs), A.subtract, (r("WX", 2, bs), r("SC2"))[c])
            if t == 2:
                if b == 0:
                    act(r("LS", (0, 1024)), r("MASK", (0, 1024)), F.Identity, scale=0.0)
                ae = ec(2, b, b + 1)
                if b < 2:
                    x = r("CNT", 3)
                    mm([(x, mx(IB_), ec(u, b, b + 1)) for u in range(b, 3)])
                    ae = r("MD" if b else "DUMM")
                    act(ae, x, F.Identity)
                own = r("LS", (7 - b, 1024, 8))
                tt(r("S1"), ind(r("WW"), ot(b)), ae, A.mult)
                tt(r("SCN"), r("WW", (7 - b, 1024, 8)), ae, A.mult)
                tt(own, own, r("S1"), A.add)
                into(ENDG[t][b], ind(r("LS"), ot(b)), r("SCN"), A.add, r("WX", 2, bs))

    def rows_update(t):
        for b in range(t + 1):
            se = r("SE", (128 * b, 128 * b + 128))
            own = r("LS", (7 - b, 1024, 8))
            tt(r("S2"), r("OVV", b), se, A.mult)
            tt(r("SC2"), r("OVC", b), se, A.mult)
            tt(own, own, r("S2"), A.add)
            into(ROWG[t], ind(r("LS"), ot(b)), r("SC2"), A.add, r("S2"))

    def blocks(sp):
        q, kh = divmod(sp, 2)
        if q not in TALL:
            return [(4 * kh + m, 256 * q, 256 * m, 256) for m in range(4)]
        return [(k, 256 * q + 128 * kh, 128 * k, 128) for k in range(8)]

    def unit(q, h):
        return q + sum(x < q for x in TALL) + (h if q in TALL else 0)

    def tile(q, j):
        if q not in TALL:
            return r("QC", q, (j, 2048, 16), raw=True)
        return r("QC", q, (1024 * (j // 8) + j % 8, 1024 * (j // 8) + 1024, 8), raw=True)

    def onb(sp, a=0, w=1024):
        return r("ONB", (64 * sp + a // 16, 64 * sp + (a + w) // 16))

    def positions(sp):
        q, kh = divmod(sp, 2)
        dd = r("QC", q, (4 * kh, 4 * kh + 4))
        js = (256 * q, 256 * q + 256)
        lin(DMODE[sp], dd, ind(r("PW"), onb(sp)), 1.0, 0.0)
        if kh == 1:
            lo, hi = r("XS", 0), r("XS", 1)
            pt = r("AB", 4, js, p=(0, 16))
            mm([(r("CNT", (0, 2), (8 * j, 8 * j + 8), p=(0, 16)),
                 r("PO", (256 * q + 128 * (j // 8) + j % 8, 256 * q + 128 * (j // 8) + 128, 8) if q in TALL else (256 * q + j, 256 * q + 256, 16)),
                 r("PL")) for j in range(16)])
            act(pt, r("CNT", (0, 2), p=(0, 16)), F.Identity)
            mm([(hi, mx(OW), r("PO", js))] +
               [(r("XS", 1, (v % 256, v % 256 + w)), r("W2", (7 - k, 135 - k)),
                 r("QC", q, (1024 * h + a, 1024 * h + a + w), raw=True)) for h in range(2) for k, v, a, w in blocks(2 * q + h)])
            act(r("EC", (384, 640)), hi, F.Square, scale=2048.0)
            act(r("D2", js), hi, F.Identity)
            if EMP == "S":
                act(r("T2", js), r("LS", js), F.Relu, bias=1.0, scale=2.0)
            else:
                ts(r("T2", js), r("LS", js), 0.0, A.is_equal)
            mm([(lo, mx(D8), r("EC", (384, 640))), (lo, mx(QE8), r("T2", js))])
            act(r("TT", js), lo, F.Identity, scale=col(25))
            if "E" in "".join(x[2 * q:2 * q + 2] for x in CLIP):
                act(r("T2", js), lo, F.Identity, scale=1 / 16)
            mm([(r("CNT", (2, 4)), r("MX", D16, p=(0, 16)), pt)] +
               [(r("CNT", (2, 4), (8 * j, 8 * j + 8)), tile(q, j), r("PL")) for j in range(16)])
            act(r("AT", None, (128 * q, 128 * q + 128)), r("CNT", (2, 4)), F.Identity)
            if q % 2:
                u = q - 1
                dma("y", [(r("DM", c, j, (128 * u, 128 * u + 256), p=(j, 128, 16)),
                           r("AT", c, (128 * u, 128 * u + 256), p=(j, 128, 16))) for j in range(16) for c in range(2)], nb=300000)

    def repeat(t, sp, src):
        q, kh = divmod(sp, 2)
        ur = ((4 + len(TALL)) * t + unit(q, kh)) % NR
        v, w = blocks(sp)[0][1], blocks(sp)[0][3]
        lin(OWN[t][q], r("UR", ur, None, (0, w)), r(src, None, (v, v + w)), 1.0, 0.0)
        byg = URG[t][unit(q, kh)]
        while w < 1024:
            if byg > 0:
                for a in range(0, w, 256):
                    sel(r("UR", ur, None, (w + a, w + a + min(w, 256))), r("UR", ur, None, (0, min(w, 256))))
            else:
                dma("y", [(r("UR", ur, None, (w, 2 * w)), r("UR", ur, None, (0, w)))])
            byg -= 1
            w *= 2

    def forces(t, sp):
        q, kh = divmod(sp, 2)
        b, bg, be = sp % 2, (8 * t + sp) % NG, (8 * t + sp) % NE
        js = (256 * q, 256 * q + 256)
        bl = blocks(sp)
        ur = ((4 + len(TALL)) * t + unit(q, kh)) % NR
        if (kh == 0 or q in TALL) and q >= AHEAD[t]:
            repeat(t, sp, "UW")
        how = GMODE[t][sp]
        neg = how == "S"
        for c in range(2):
            if how == "R":
                tt(r("G", bg, c), ind(r("UW", c), onb(sp)), r("UR", ur, c), A.subtract)
            elif how == "F":
                for k, v, a, w in bl:
                    tt(r("G", bg, c, (a, a + w)), ind(r("UW", c), onb(sp, a, w)), r("UR", ur, c, (0, w)), A.subtract)
            else:
                lin(how, r("G", bg, c), ind(r("UW", c), onb(sp)), -1.0, 0.0)
        if neg:
            dma("g", [(r("G", bg), r("UR", ur))], acc=True)
        clip = CLIP[t][sp]
        if clip in "BC" and not neg:
            clip = "A"
        en, e0, e1 = ("EE", be, 3 + b) if clip in "DEV" else (EBUF[t][sp % 2], 0, 1)

        def spread(name, bank, h, tab, row):
            return [(r(name, bank, (a % 512, a % 512 + w)), r("SEL", row + k), r(tab, (v, v + w))) for k, v, a, w in bl if a // 512 == h]

        def runs(wide):
            return [((0, 1024), [(0, 0), (1, 1)], [None, None])] if wide else \
                [((512 * h, 512 * h + 512), [(None, h)], [0, 1]) for h in range(2)]
        for hs, fill, bank in runs(WIDE[t][sp] in "WX"):
            for c in range(2):
                for x, h in fill:
                    mm(spread("DXY", c if x is None else x, h, "D2", 8 * c))
                z = r("DXY", bank[c])
                if EADD[t][sp] == "V" and c:
                    tt(z, r("G", bg, c, hs), z, A.mult)
                    tt(r(en, e0, hs), r(en, e0, hs), z, A.add)
                else:
                    tt(r(en, (e0, e1)[c], hs), r("G", bg, c, hs), z, A.mult)
        if EADD[t][sp] != "V":
            dma("g", [(r(en, e0), r(en, e1))], acc=True)
        qc, ap = r("QC", q, (4 * kh, 4 * kh + 4)), r("AP", b)
        neg = not neg
        for hs, fill, bank in runs(WIDE[t][sp] in "WY"):
            e, m = r(en, e0, hs), r(en, e1, hs)
            qh = r("QC", q, (1024 * kh + hs[0], 1024 * kh + hs[1]), raw=True)

            def bound(s, c, whole=False):
                for x, h in fill:
                    x = c if x is None else x
                    ks = (4 * kh + 2 * h, 4 * kh + 2 * h + 2)
                    mm(spread("UL", x, h, "TT", 8 * s) + ([(r("UL", x), mx(IB_ if neg != whole else NI), r("QC", q, ks))] if t else []) +
                       ([(r("UL", x), I32, r(en, e0, (512 * h, 512 * h + 512)))] if whole else []))
                return r("UL", bank[c])

            def less(out, z):
                tt(out, *((z, e) if neg else (e, z)), A.subtract)
            if clip in "AB":
                act(r("AP", b, hs), bound(1 - neg, 0, True), F.Relu, scale=-1.0 if neg else 1.0)
            elif clip == "C":
                ts(r("AP", b, hs), bound(1, 0, True), 0.0, A.max, 1023.0, A.min)
            elif clip == "D":
                less(r("AP", b, hs), bound(int(neg), 0))
            elif clip == "E":
                less(m, bound(int(neg), 0))
                act(r("AP", b, hs), m, F.Relu)
            if clip in "ACD":
                less(qh, bound(1 - neg, 1))
            elif clip == "E":
                for x, h in fill:
                    mm(spread("UL", 1 if x is None else x, h, "T2", 0))
                tt(qh, m, r("UL", bank[1]), A.add)
            elif clip == "B":
                tt(qh, bound(0, 1, True), r("AP", b, hs), A.min)
            else:
                tt(m, e, bound(0, 0), A.min)
                z = bound(1, 1)
                tt(z, m, z, A.max)
                less(qh, z)
        if clip in "ACDE":
            if clip != "C":
                ts(ap, ap, 0.0, A.max, 1023.0, A.min)
            ts(qc, qc, 0.0, A.min, -1023.0, A.max)
            dma("g", [(qc, ap)], acc=True)
        if MARK[t][sp] == "S":
            act(r("NZ", b), qc, F.Sign)
            act(r("NZ", b), r("NZ", b), F.Abs)
        else:
            ts(r("NZ", b), qc, 0.0, A.not_equal)
        if clip in "BV":
            ts(qc, qc, -1023.0, A.max, 1023.0, A.min)
        tall = q in TALL
        first = [(r("CNT", 0), mx(I16), r("SC", (t + 1) % 2, unit(q, kh)))] if t and (kh == 0 or tall) else []
        if tall:
            sa = [(r("CNT", 0), r("WC", (15 - 8 * kh - j, 143 - 8 * kh - j)), r("NZ", b, (j, 1024, 8), raw=True)) for j in range(8)]
        else:
            sa = [(r("CNT", 0, (64 * kh, 64 * kh + 64)), r("WC", (15 - j, 143 - j)), r("NZ", b, (j, 1024, 16), raw=True))
                  for j in range(16)]
        mm(first + sa + [(r("CNT", (1, 1 + w // 128)), r("C2", (7 - k, 135 - k)), r("NZ", b, (a, a + w), raw=True)) for k, v, a, w in bl],
           kh == 0 or tall, kh == 1 or tall)

    def atile(q, j):
        return r("AB", 2 * q + j // 8, (128 * (j % 8), 128 * (j % 8) + 128))

    def sums(t, q, h=None):
        js = (256 * q, 256 * q + 256)
        vs = js if h is None else (256 * q + 128 * h, 256 * q + 128 * h + 128)
        u = unit(q, h)
        sa, sb = r("SC", t % 2, u), r("CNT", (1, 3 if h is None else 2))
        act(sa, r("CNT", 0), F.Sigmoid, bias=-256.0 * (19.5 if t else 3.5), scale=256.0)
        act(sb, sb, F.Sigmoid, bias=-256.0 * 3.5, scale=256.0)
        tt(r("D2", vs), r("D2", vs), sb, A.mult)
        X1 = r("XS")
        s = r("XACC", None, js)
        cs = (vs[0] % 256, (vs[1] - 1) % 256 + 1)
        off = [(r("XS", 0, cs), mx(CX), r("D2", vs)), (r("XS", 1, cs), mx(CY), r("D2", vs))]
        half = [(r("XS", 1), r("I5"), r("LD", js)), (X1, mx(C64), r("MASK", (0, 512)))]
        half = [(r("XS", None, (7 - b, 256, 8)), I32, r("WX", (0, 2), (128 * b + 32 * q, 128 * b + 32 * q + 32))) for b in byp(t)] + half
        byv = q < EARLY[t] or (FIN[t][q] in "VSA" and q < 3)
        if not h:
            mm([(X1, I32, s)] + half if q == 3 else off if h is None else half[::-1], True, False)
        if t < 2:
            tt(r("LS", vs), r("LS", vs), sb, A.mult)
        if t:
            mm([(r("CNT", 3), mx(IB_), sa), (r("CNT", 3), mx(IB_), r("SC", 0, u) if t == 1 else r("SS", u))])
            act(r("SS", u), r("CNT", 3), F.Identity, bias=0.0 if t == 1 else -1.5, scale=1.0 if t == 1 else 0.5)
        for b in range(4) if h is None else (2 * h, 2 * h + 1):
            tr = TRB[t][q == 3][b % 2]
            mm([(r(tr), sa, r("SEL", (4 * b, 4 * b + 4)))] +
               [(r(tr, j), tile(q, 4 * b + j), mx(NI)) for j in range(4)])
            qs = r("QS", (16 * (b % 2), 16 * (b % 2) + 16), (0, 3, 2))
            if EVAC[t][4 * q + b] == "S":
                act(qs, r(tr), F.Relu, bias=-1024.0)
            else:
                ts(qs, r(tr), -1024.0, A.add, 0.0, A.max)
            terms = []
            for j in range(4 * b, 4 * b + 4):
                cs = (j, 256, 16) if h is None else (128 * h + j % 8, 128 * h + 128, 8)
                for gg in range(8):
                    pr, odd = divmod(gg, 2)
                    terms.append((r("XS", None, cs, p=(32 * pr, 32 * pr + 32)),
                                  r("QS", 4 * (j % 8) + pr, (odd, odd + 2)), r("DM", None, None, 128 * q + 8 * j + gg)))
            mm(terms, False, False)
            if (t, u) in SPLIT:
                act(r("AT", b // 2, (512 * (b % 2), 512 * (b % 2) + 512)), qs, F.Abs, bias=-1024.0)
            elif b % 2:
                out = r("AB", 2 * q + b // 2) if t == 0 else r("AT", b // 2)
                act(out, r("QS", None, (0, 3, 2)), F.Abs, bias=-1024.0)
        if t == 1:
            dma("g", [(r("AB", (2 * q, 2 * q + 2)), r("AT")) if h is None else (r("AB", 2 * q + h), r("AT", h))], acc=True)
        plain = FIN[t][q] == "Q" and not byv
        mm((half if h is None else off) + [(X1, I32, s)] * (plain and q < 3 and h != 0), False, (byv or plain) and h != 0)
        if h == 0:
            return
        if byv:
            if LAY[t][q] == "V":
                tt(s, s, X1, A.add)
            else:
                x = r("BASE", None, (256 * q, 256 * q + 256)) if t < 2 else r("WX", (0, 2), (0, 256))
                act(x, X1, F.Identity)
                dma("g", [(s, x)], acc=True)
            if q >= EARLY[t]:
                close(s, FIN[t][q])
        elif plain:
            ts(s, X1, RND, A.add, RND - 1023.0, A.max)
            ts(r("UW", None, js) if t < 2 and q == 3 else s, s, RND + 1023.0, A.min, RND, A.subtract)
        else:
            mm(([(X1, I32, s)] if q < 3 else []) +
               [(X1, mx(RN), r("MASK", (0, 512))), (X1, mx(NRN), r("MASK", (0, 512)))], False, True)
            out = r("UW", None, js) if t < 2 and q == 3 else s
            if CUT[t][q] == "S":
                cut(out, X1, 0.0)
            else:
                ts(out, X1, -1023.0, A.max, 1023.0, A.min)

    def cut(s, x, off):
        act(s, x, F.Relu, bias=1023.0 - off)
        act(s, s, F.Relu, bias=2046.0, scale=-1.0)
        act(s, s, F.Identity, bias=1023.0, scale=-1.0)

    def close(s, how):
        if how == "V":
            ts(s, s, RND, A.add, RND - 1023.0, A.max)
            ts(s, s, RND + 1023.0, A.min, RND, A.subtract)
        elif how == "S":
            act(s, s, F.Identity, bias=RND)
            ts(s, s, RND + 1023.0, A.min, RND - 1023.0, A.max)
            act(s, s, F.Identity, bias=-RND)
        else:
            act(s, s, F.Identity, bias=RND)
            cut(s, s, RND)

    def update(t, q):
        js = (256 * q, 256 * q + 256)
        if t < 2:
            dma("y", [(r("UW", None, (0, 768)), r("XACC", None, (0, 768)))])
        else:
            dma("y", [(hbm(("yx", "yy")[c], slice(None), slice(*js)), r("XACC", c, js)) for c in range(2)])

    def weights(q):
        js = (256 * q, 256 * q + 256)

        def wg(kh, a, b):
            return r("UW", kh, (a, b))

        def back(out, j, u, ks):
            return [(out, r("SEL", j), r("SS", u, ks)), (out, atile(q, j), r("MX", IB_, ks)), (out, r("AT", j // 8, (128 * (j % 8), 128 * (j % 8) + 128)), r("MX", IB_, ks))]
        w = WBUF[q]
        for kh in range(2):
            out = wg(kh, 0, 1024) if q == 3 else r(w, kh)
            lin(WMODE[2 * q + kh], out, ind(r("WW"), onb(2 * q + kh)), 1.0, 0.0)
            if q == 3:
                vs, x = (768 + 128 * kh, 896 + 128 * kh), r("UL", kh, (0, 128))
                for h in range(2):
                    mm([y for j in range(8 * kh, 8 * kh + 8)
                        for y in back(r("DXY", h, (j % 8, 512, 8)), j, unit(q, kh), (64 * h, 64 * h + 64))])
                    tt(wg(kh, 512 * h, 512 * h + 512), wg(kh, 512 * h, 512 * h + 512), r("DXY", h), A.mult)
                    if WT3[kh] == "P":
                        mm(([] if h else [(x, I32, r("LS", vs))]) +
                           [(x, I32, wg(kh, 128 * k, 128 * k + 128)) for k in range(4 * h, 4 * h + 4)], h == 0, h == 1)
                    else:
                        a = 512 * h
                        tt(wg(kh, a, a + 256), wg(kh, a, a + 256), wg(kh, a + 256, a + 512), A.add)
                        tt(wg(kh, a, a + 128), wg(kh, a, a + 128), wg(kh, a + 128, a + 256), A.add)
                        tt(r("LS", vs), r("LS", vs), wg(kh, a, a + 128), A.add)
                if WT3[kh] == "P":
                    act(r("LS", vs), x, F.Identity)
                dma(YW, [(hbm("yw", slice(None), slice(*vs)), r("LS", vs))])
                continue
            for h in range(2):
                if q in TALL:
                    mm([y for j in range(8 * kh, 8 * kh + 8) for y in back(x0(j % 8, 512, 8), j, unit(q, kh), (64 * h, 64 * h + 64))])
                    x = r(w, kh, (512 * h, 512 * h + 512))
                else:
                    mm([x for j in range(h, 16, 2) for x in back(x0(j // 2, 512, 8), j, unit(q, 0), (64 * kh, 64 * kh + 64))])
                    x = r(w, kh, (h, 1024, 2))
                tt(x, x, X0, A.mult)
        if q == 3:
            return
        if q in TALL:
            tree = [(r(w, None, (0, 512)), r(w, None, (512, 1024))), (r(w, None, (0, 256)), r(w, None, (256, 512))),
                    (r("LS", js), r(w, None, (0, 128))), (r("LS", js), r(w, None, (128, 256)))]
        else:
            tree = [(r(w, 0), r(w, 1)), (r(w, 0, (0, 512)), r(w, 0, (512, 1024))),
                    (r("LS", js), r(w, 0, (0, 256))), (r("LS", js), r(w, 0, (256, 512)))]
        if WTREE[q][0] == "H":
            tree = [(r(w, 0, (0, 512)), r(w, 0, (512, 1024))), (r(w, 1, (0, 512)), r(w, 1, (512, 1024))),
                    (r(w, 0, (0, 512)), r(w, 1, (0, 512))), (r(w, 0, (0, 256)), r(w, 0, (256, 512))), (r("LS", js), r(w, 0, (0, 256)))]
        for x, who in zip(tree, WTREE[q][1:]):
            if who == "D":
                dma("g", [x], acc=True)
            else:
                tt(x[0], x[0], x[1], A.add)
        dma(YW, [(hbm("yw", slice(None), slice(*js)), r("LS", js))])

    for t in range(3):
        up[0] = UP[t]
        dma("y", [(r("XACC", None, (768 if t else 0, 1024)), r("UW", None, (768 if t else 0, 1024)))])
        step1(t)
        if t:
            up[0] = UP3[t]
            extras(t, 0, t, (r("XS", 0, (0, 128 * t)), r("CNT", (0, t))))
            ends(t, 0, t)
            up[0] = UP2[t]
        else:
            cp(r("WX", 2, (128, 384)), ind(r("WW", (0, 1024)), r("OB")))
            send(r("WX", 2, (128, 384)), [r("WW", (1024 + 256 * d, 1280 + 256 * d)) for d in range(3)], 9)
        extras(t, t, t + 1, (x0(0, 128), x0(128, 256)))
        up[0] = 0.0
        for q in range(4):
            if t == 0 and q == 0:
                for sp in range(8):
                    positions(sp)
            if q == EARLY[t]:
                up[0] = UP2[t]
                ends(t, t, t + 1)
                up[0] = 0.0
                if q:
                    close(r("XACC", None, (0, 256 * q)), CLOSE[t])
                for p in range(q if t == 2 else 0):
                    update(t, p)
                    weights(p)
            forces(t, 2 * q)
            if q in TALL:
                sums(t, q, 0)
            forces(t, 2 * q + 1)
            sums(t, q, 1 if q in TALL else None)
            if t == 2 and q >= EARLY[t]:
                update(t, q)
                weights(q)
        if t < 2:
            update(t, 0)
            for sp in range(2 * AHEAD[t + 1]):
                if sp % 2 == 0 or sp // 2 in TALL:
                    repeat(t + 1, sp, "XACC")
            border(t + 1)
            la = ("LA1", "LA0")[t]
            send(r("SND", (0, 2)), [r(la, (2 * d, 2 * d + 2)) for d in range(3)], 3 * (t + 1))
            rows_update(t)
            convert(t + 1)
    return ops


def hazards(ops):
    seen = {}
    for i, o in enumerate(ops):
        dep = set()
        acc = set()
        for xs, wr in ((o["w"], True), (o["r"], False)):
            for x in xs:
                for a, b in x["spans"]:
                    acc.add((x["name"], wr, a, b))
        joined = []
        for x, wr, a, b in sorted(acc, key=lambda y: (not y[1], y[0], y[2])):
            if joined and joined[-1][:2] == (x, wr) and a <= joined[-1][3]:
                joined[-1] = (x, wr, joined[-1][2], max(b, joined[-1][3]))
            else:
                joined.append((x, wr, a, b))
        acc = joined
        for x, wr, a, b in acc:
            ps = SCRATCH[x][0] == "psum"
            for (j, lo, hi, w2) in seen.get(x, []):
                if lo < b and a < hi and (wr or w2 or (ps and ops[j]["eng"] != o["eng"])):
                    dep.add(j)
        if o["kind"] == "recv":
            dep = {o["after"]}
        for x, wr, a, b in acc:
            lst = seen.setdefault(x, [])
            if wr:
                lst[:] = [e for e in lst if e[0] in (i, o.get("beside")) or not (a <= e[1] and e[2] <= b)]
            lst.append((i, a, b, wr))
        dep.discard(i)
        dep.discard(o.get("beside"))
        o["dep"] = sorted(dep)


def arrange(ops):
    hazards(ops)
    n = len(ops)
    succ = [[] for _ in ops]
    for i, o in enumerate(ops):
        for j in o["dep"]:
            succ[j].append(i)

    def tail(o):
        if o["kind"] == "dma":
            return PACE["dlat"] + o["by"] / PACE["rate"]
        return PACE["rem"] if o["kind"] == "send" else 0.0
    level = [0.0] * n
    for i in range(n - 1, -1, -1):
        level[i] = ops[i]["cost"] + tail(ops[i]) + PACE["wake"] + max([level[j] for j in succ[i]] + [0.0])
    best = None
    first = level
    paces = [pace(ops, p) for p in PACES]
    for look in LOOKS:
        LOOK.update(zip("vspgy", look))
        level = first
        for it in range(PASSES + 1):
            order = forward(ops, succ, level)
            t0 = place(ops, [o["dep"] for o in ops], succ, [o["t0"] for o in ops], False)[0]
            for od in (order, sorted(range(n), key=lambda i: (t0[i], i))):
                span = sum(max(replay(od, m)[1]) / m[6] for m in paces)
                if best is None or span < best[0]:
                    best = (span, od)
            if it < PASSES:
                level = backward(ops, succ, tail)
    order = smooth(ops, best[1], paces)
    for o, a, b in zip(ops, *replay(order, paces[0])[:2]):
        o["t0"], o["t1"] = a, b
    return order


def pace(ops, p):
    wake = PACE["wake"] * p["wake"]
    return (["vspgyx".index(o["eng"]) for o in ops], [o["cost"] * p["pe" if o["eng"] == "p" else o["sort"]] for o in ops],
            [o["by"] / PACE["rate"] * p["dma"] if o["kind"] == "dma" else 0.0 for o in ops],
            [PACE["rem"] * p["wait"] if o["kind"] == "send" else 0.0 for o in ops],
            [[(j, 0.0 if o.get("cont") and ops[j]["eng"] == "p" else wake) for j in o["dep"]] for o in ops],
            PACE["dlat"] * p["wait"] / 2, p["all"])


def replay(order, m, at=0, old=None):
    eng, cost, dur, tail, lat, half = m[:6]
    n = len(order)
    free, last = [0.0] * 6, [-1] * 6
    t0, t1, par, own = [list(x) for x in old[:4]] if at else ([0.0] * n, [0.0] * n, [-1] * n, [False] * n)
    pipe, lastd = 0.0, -1
    for x in range(at - 1, -1, -1):
        i = order[x]
        if last[eng[i]] < 0:
            free[eng[i]], last[eng[i]] = t0[i] + cost[i], i
        if dur[i] and lastd < 0:
            pipe, lastd = t1[i] - half, i
        if lastd >= 0 and min(last[:5]) >= 0:
            break
    for i in order[at:]:
        e = eng[i]
        s, p, w = free[e], last[e], True
        for j, l in lat[i]:
            x = t1[j] + l
            if x > s:
                s, p, w = x, j, False
        t0[i] = s
        s += cost[i]
        free[e], last[e] = s, i
        if dur[i]:
            if pipe > s + half:
                p, w = lastd, False
            else:
                pipe = s + half
            pipe += dur[i]
            s, lastd = pipe + half, i
        t1[i], par[i], own[i] = s + tail[i], p, w
    return t0, t1, par, own


def smooth(ops, order, paces):
    eng, dep = paces[0][0], [set(o["dep"]) for o in ops]
    n = len(ops)
    outs = []
    for m in paces:
        outs.append([[] for o in ops])
        for i in range(n):
            for j, l in m[4][i]:
                outs[-1][j].append((i, l))

    def state(order, runs, at=None, old=None):
        pos, pre, nxt, last = [0] * n, [-1] * n, [-1] * n, {}
        pd, nd, ld = [-1] * n, [-1] * n, -1
        for x, i in enumerate(order):
            pos[i] = x
            j = last.get(eng[i], -1)
            if j >= 0:
                pre[i], nxt[j] = j, i
            last[eng[i]] = i
            if paces[0][2][i]:
                if ld >= 0:
                    pd[i], nd[ld] = ld, i
                ld = i
        chains, rest = [], []
        for k, (m, out, (t0, t1, par, own)) in enumerate(zip(paces, outs, runs)):
            i, pairs = t1.index(max(t1)), []
            while i >= 0:
                if own[i] and par[i] >= 0:
                    pairs.append(i)
                i = par[i]
            chains.append(pairs)
            cost, dur, tail, half = m[1], m[2], m[3], m[5]
            q, qd = old[k] if old else ([0.0] * (n + 1), [0.0] * (n + 1))
            for i in order[at::-1]:
                s = 0.0
                for j, l in out[i]:
                    if q[j] + l > s:
                        s = q[j] + l
                if dur[i]:
                    qd[i] = dur[i] + max(s + half, qd[nd[i]])
                    s = qd[i] + half
                q[i] = cost[i] + max(s + tail[i], q[nxt[i]])
            rest.append((q, qd))
        return pos, pre, nxt, pd, nd, chains, rest

    def guess(seg, new):
        inside, tot = set(seg), 0.0
        for m, out, run, (q, qd) in zip(paces, outs, runs, rest):
            cost, dur, tail, lat, half = m[1:6]
            t0, t1 = run[:2]
            span = max(t0[i] + q[i] for i in seg)
            free, last, pipe, ld, t, s2 = {}, {}, None, -1, {}, 0.0
            for i in seg:
                if eng[i] not in free:
                    free[eng[i]] = t0[pre[i]] + cost[pre[i]] if pre[i] >= 0 else 0.0
                last[eng[i]] = i
                if dur[i]:
                    if pipe is None:
                        pipe = t1[pd[i]] - half if pd[i] >= 0 else 0.0
                    ld = i
            for i in new:
                s = free[eng[i]]
                for j, l in lat[i]:
                    x = t.get(j, t1[j]) + l
                    if x > s:
                        s = x
                s += cost[i]
                free[eng[i]] = s
                if dur[i]:
                    pipe = max(pipe, s + half) + dur[i]
                    s = pipe + half
                t[i] = s = s + tail[i]
                s2 = max(s2, s)
                for j, l in out[i]:
                    if j not in inside and s + l + q[j] > s2:
                        s2 = s + l + q[j]
            for e, i in last.items():
                s2 = max(s2, free[e] + q[nxt[i]])
            if ld >= 0:
                s2 = max(s2, pipe + qd[nd[ld]])
            tot += (s2 if span > run[4] - 1e-6 else max(s2, run[4])) / m[6]
        return tot
    runs = [replay(order, m) for m in paces]
    cur = sum(max(x[1]) / m[6] for x, m in zip(runs, paces))
    pos, pre, nxt, pd, nd, chains, rest = state(order, runs)
    runs = [x + (max(x[1]),) for x in runs]
    seed = 1
    for it in range(SWAPS):
        seed = (seed * 1103515245 + 12345) % 2 ** 31
        pairs = chains[it % len(runs)]
        b = pairs[(seed >> 8) % len(pairs)]
        a = pre[b]
        for k in range((0, 0, 1, 2)[seed >> 5 & 3]):
            if seed >> 7 & 1 and nxt[b] >= 0:
                b = nxt[b]
            elif pre[a] >= 0:
                a = pre[a]
        pa, pb = pos[a], pos[b]
        seg = order[pa:pb + 1]
        if seed >> 7 & 1:
            mv, qs = {a}, set()
            for x in seg[1:]:
                if dep[x] & mv or eng[x] in qs:
                    mv.add(x)
                    qs.add(eng[x])
            new = [x for x in seg if x not in mv] + [x for x in seg if x in mv]
        else:
            mv, qs, need = {b}, set(), set(dep[b])
            for x in reversed(seg[:-1]):
                if x in need or eng[x] in qs:
                    mv.add(x)
                    qs.add(eng[x])
                    need |= dep[x]
            new = [x for x in seg if x in mv] + [x for x in seg if x not in mv]
        if a in mv and b in mv:
            continue
        room = SLACK * (1 - it / SWAPS)
        s = guess(seg, new)
        if s > cur + room + 1e-6 or (s > cur - 1e-6 and seed >> 12 & LEVEL):
            continue
        od = order[:pa] + new + order[pb + 1:]
        rs = [replay(od, m, pa, x) for m, x in zip(paces, runs)]
        s = sum(max(x[1]) / m[6] for x, m in zip(rs, paces))
        if s <= cur + room + 1e-6:
            cur, order = s, od
            pos, pre, nxt, pd, nd, chains, rest = state(order, rs, pb, rest)
            runs = [x + (max(x[1]),) for x in rs]
    return order


def place(ops, pre, nxt, key, back):
    n = len(ops)
    left = [len(p) for p in pre]
    busy = {e: [] for e in "vspgyD"}
    t0, t1 = [0.0] * n, [0.0] * n
    ready = sorted((key[i], i) for i in range(n) if not left[i])

    def fit(e, at, c):
        lst = busy[e]
        k = len(lst)
        while k and lst[k - 1][1] > at:
            k -= 1
        while k < len(lst) and lst[k][0] < at + c - 1e-9:
            at = max(at, lst[k][1])
            k += 1
        lst.insert(k, (at, at + c))
        return at
    while ready:
        i = ready.pop(0)[1]
        o = ops[i]
        at = 0.0
        for j in pre[i]:
            a, b = (i, j) if back else (j, i)
            at = max(at, t1[j] + (0.0 if ops[b].get("cont") and ops[a]["eng"] == "p" else PACE["wake"]))
        c, half = o["cost"], PACE["dlat"] / 2
        if o["kind"] == "recv":
            t0[i] = t1[i] = at
        elif o["kind"] == "dma":
            d = o["by"] / PACE["rate"]
            if back:
                t1[i] = fit(o["eng"], fit("D", at + half, d) + d + half, c) + c
            else:
                t0[i] = fit(o["eng"], at, c)
                t1[i] = fit("D", t0[i] + c + half, d) + d + half
        else:
            rem = PACE["rem"] if o["kind"] == "send" else 0.0
            t0[i] = fit(o["eng"], at + (rem if back else 0.0), c)
            t1[i] = t0[i] + c + (0.0 if back else rem)
        for j in nxt[i]:
            left[j] -= 1
            if not left[j]:
                ready.append((key[j], j))
                ready.sort()
    return t0, t1


def backward(ops, succ, tail):
    n = len(ops)
    left = [len(s) for s in succ]
    ready = {e: [] for e in "vspgyx"}
    at = [tail(o) for o in ops]
    for i, o in enumerate(ops):
        if not left[i]:
            ready[o["eng"]].append(i)
    free = {e: 0.0 for e in "vspgyx"}
    out = [0.0] * n
    for step in range(n):
        best = None
        for e, lst in ready.items():
            if not lst:
                continue
            s = min(max(free[e], at[i]) for i in lst)
            i = max((i for i in lst if max(free[e], at[i]) <= s + LOOK[e]), key=lambda q: ops[q]["t1"])
            s = max(free[e], at[i])
            if best is None or s < best[0]:
                best = (s, i)
        s, i = best
        o = ops[i]
        ready[o["eng"]].remove(i)
        out[i] = s + o["cost"]
        if o["kind"] != "recv":
            free[o["eng"]] = out[i]
        for j in o["dep"]:
            at[j] = max(at[j], out[i] + PACE["wake"] + tail(ops[j]))
            left[j] -= 1
            if not left[j]:
                ready[ops[j]["eng"]].append(j)
    return out


def forward(ops, succ, level):
    n = len(ops)
    left = [len(o["dep"]) for o in ops]
    ready = {e: [] for e in "vspgyx"}
    at = [0.0] * n
    for i, o in enumerate(ops):
        if not left[i]:
            ready[o["eng"]].append(i)
    free = {e: 0.0 for e in "vspgyx"}
    pipe = [0.0]
    order = []
    hold = [None]
    feeds = {i: [j for j in o["dep"]] for i, o in enumerate(ops) if o["kind"] == "send" and o["args"][2] in (3, 6)}
    while len(order) < n:
        hold[0] = None
        for i, d in feeds.items():
            if 0 < left[i] <= 2 and all(left[j] == 0 for j in d):
                hold[0] = [max(d, key=lambda q: at[q])]
        best = None
        for e, lst in ready.items():
            if not lst:
                continue
            s = min(max(free[e], at[i]) for i in lst)
            i = max((i for i in lst if max(free[e], at[i]) <= s + LOOK[e]), key=lambda q: level[q] + ops[q]["up"])
            if e == "g" and ops[i]["kind"] == "dma" and hold[0] and at[hold[0][0]] <= s + GLOOK:
                continue
            s = max(free[e], at[i])
            if best is None or s < best[0]:
                best = (s, i)
        s, i = best
        o = ops[i]
        ready[o["eng"]].remove(i)
        order.append(i)
        o["t0"] = s
        end = s + o["cost"]
        if o["kind"] != "recv":
            free[o["eng"]] = end
        if o["kind"] == "dma":
            pipe[0] = max(pipe[0], end + PACE["dlat"] / 2) + o["by"] / PACE["rate"]
            end = pipe[0] + PACE["dlat"] / 2
        if o["kind"] == "send":
            end += PACE["rem"]
        o["t1"] = end
        for j in succ[i]:
            lat = 0.0 if ops[j].get("cont") and o["eng"] == "p" else PACE["wake"]
            at[j] = max(at[j], end + lat)
            left[j] -= 1
            if not left[j]:
                ready[ops[j]["eng"]].append(j)
    return order


PLAN = []


def rank_program(g, core, T, topo):
    rank = T.rank_of(core)
    if rank is None:
        return
    if not PLAN:
        ops = build()
        PLAN.append((ops, arrange(ops)))
    ops, order = PLAN[0]
    n = len(T.cores)

    def engines(src, d):
        en = topo.engines(T.cores[src], T.cores[(src + d + 1) % n])
        q = len(en) // 4
        return (en[0::2][:q], en[0::2][q:2 * q], en[1::2][:2 * q])[d]

    queue = {"v": g.vector, "s": g.scalar, "p": g.tensor, "g": g, "y": g.sync}
    known = {e: {} for e in queue}
    count = {e: 0 for e in queue}
    waited, top, token, clock = {}, {}, {}, {}
    nd = [0]
    user, succ = {}, [[] for o in ops]
    for i, o in enumerate(ops):
        for j in o["dep"]:
            succ[j].append(i)

    def wait(e, s, v):
        queue[e].wait_ge(T.sem[s], v)
        waited[s] = max(waited.get(s, 0), v)

    for i in order:
        o = ops[i]
        e, kind, a = o["eng"], o["kind"], o["args"]
        if kind == "recv":
            token[i] = ("ar%d" % (a[0] + a[1]), len(engines((rank - a[1] - 1) % n, a[1])))
            top[token[i][0]] = token[i][1]
            clock[i] = {}
            continue
        kn = known[e]
        need = {}
        for j in o["dep"]:
            if o.get("cont") and ops[j]["eng"] == "p" and ops[j]["w"][0]["name"] == o["w"][0]["name"]:
                continue
            s, v = token[j]
            if kn.get(s, 0) < v and need.get(s, (0, 0))[0] < v:
                need[s] = (v, j)
        for s, (v, j) in sorted(need.items(), key=lambda x: -ops[x[1][1]]["t1"]):
            if kn.get(s, 0) >= v:
                continue
            wait(e, s, v)
            kn[s] = v
            for s2, v2 in clock[j].items():
                if kn.get(s2, 0) < v2:
                    kn[s2] = v2
        q = queue[e]
        if kind == "dma":
            s = None
            if nd[0] >= NDS:
                for s2, j in user.items():
                    if (ops[j]["eng"] == "g") == (e == "g") and kn.get(s2, 0) >= top[s2] and \
                            all(x in token and kn.get(token[x][0], 0) >= token[x][1] for x in succ[j]):
                        s = s2
                        break
            else:
                s = "d%d" % nd[0]
                nd[0] += 1
            user.pop(s, None)
            user[s] = i
            for out, src in a[0]:
                kw = {"accum_op": A.add} if a[1] else {}
                q.dma_start(_ap(T, out), _ap(T, src), **kw).then_inc(T.sem[s], 16)
            token[i] = (s, top.get(s, 0) + 16 * len(a[0]))
        elif kind == "send":
            trs, tot = [], 0
            for d in range(n - 1):
                rid, pid, se = topo.addr(T.cores[(rank + d + 1) % n])
                en = engines(rank, d)
                tot += len(en)
                trs.append(RemoteDMATransfer(dst_ids=[DstId(rid=rid, pnc=pid)], dma_engine_mask=sum(1 << x for x in en),
                                             remote_sem=T.sem["ar%d" % (a[2] + d)], src=_ap(T, a[0]), dst=_ap(T, a[1][d])))
            s = "lo%d" % (a[2] // 3)
            g.remote_dma_fused(trs, local_sem=T.sem[s])
            token[i] = (s, tot)
        else:
            x = [_ap(T, y) for y in a] if kind != "mm" else None
            if kind == "tt":
                ins = q.tensor_tensor(*x)
            elif kind == "ts":
                ins = q.tensor_scalar(*(x if x[5] is not None else x[:5]))
            elif kind == "cp":
                ins = q.tensor_copy(*x)
            elif kind == "ms":
                ins = q.memset(*x)
            elif kind == "scan":
                ins = q.tensor_tensor_scan(*x)
            elif kind == "act":
                ins = q.activation(x[0], x[1], x[2], bias=x[3], scale=x[4])
            elif kind == "sel":
                ins = q.affine_select(*x)
            elif kind == "iota":
                kw = {} if SCRATCH[a[0]["name"]][2] == i32 else {"allow_small_or_imprecise_dtypes": True}
                ins = q.iota(*x, **kw)
            else:
                for m, (out, l, rhs) in enumerate(a[0]):
                    ins = q.matmul(_ap(T, out), _ap(T, l), _ap(T, rhs), a[1] and m == 0, a[2] and m == len(a[0]) - 1)
            count[e] += 1
            ins.then_inc(T.sem["c" + e], 1)
            token[i] = ("c" + e, count[e])
        top[token[i][0]] = token[i][1]
        clock[i] = dict(kn)
    for s, v in top.items():
        if waited.get(s, 0) < v:
            wait("g", s, v)
